import numpy as np
import ml_dtypes


def mxq(x, axis, fmt="e4m3"):
    dtype, down = {"e4m3": (ml_dtypes.float8_e4m3fn, 7), "e5m2": (ml_dtypes.float8_e5m2, 14)}[fmt]
    v = np.moveaxis(np.asarray(x, np.float32).astype(ml_dtypes.bfloat16).astype(np.float64), axis, -1)
    blocks = v.reshape(v.shape[:-1] + (-1, 32))
    amax = np.abs(blocks).max(-1, keepdims=True)
    byte = np.maximum(np.where(amax > 0, np.frexp(amax)[1] - 1 + 127, 0) - down, 1)
    scale = np.exp2(byte - 127.0)
    codes = (blocks / scale).astype(np.float32).astype(dtype).astype(np.float64)
    return np.moveaxis((codes * scale).reshape(v.shape), -1, axis)


WIDE = False


def mx_kscale(k):
    if not WIDE:
        return np.ones(k)
    levels = np.array([10, -10, 5, -5, 0])
    if k % 512:
        return np.exp2(np.random.permutation(np.resize(levels, k // 32))).repeat(32)
    a = np.empty((k // 512, 16))
    for p in range(k // 512):
        a[p, :8] = np.random.permutation(np.resize(levels, 8))
        for g in range(8):
            far = levels[np.abs(levels - a[p, g]) >= 10]
            a[p, g + 8] = far[np.random.randint(len(far))]
    return np.exp2(a.ravel()).repeat(32)


BF16 = ml_dtypes.bfloat16


def bf(x):
    return np.asarray(x, np.float32).astype(BF16)


def f64(x):
    return np.asarray(x).astype(np.float64)


E2M1 = np.array([0.0, 0.5, 1.0, 1.5, 2.0, 3.0, 4.0, 6.0, -0.0, -0.5, -1.0, -1.5, -2.0, -3.0, -4.0, -6.0])


def pack_weight(w, fmt):
    k, n = w.shape
    w = f64(bf(w)).reshape(k // 32, 32, n)
    amax = np.abs(w).max(1)
    if fmt == "e4m3":
        byte = np.frexp(amax)[1] - 1 + 127 - 7
    else:
        mant, ex = np.frexp(amax / 6.0)
        byte = np.where(mant > 0.5, ex, ex - 1) + 127
    byte = np.clip(np.where(amax > 0, byte, 1), 1, 254)
    scaled = (w * np.exp2(127.0 - byte)[:, None, :]).reshape(k, n).astype(np.float32)
    by_word = np.ascontiguousarray(scaled.reshape(k // 512, 128, 4, n).transpose(0, 1, 3, 2))
    if fmt == "e4m3":
        words = by_word.astype(ml_dtypes.float8_e4m3fn).view(np.uint8)
    else:
        c = by_word.astype(ml_dtypes.float4_e2m1fn).view(np.uint8) & 0xF
        words = c[..., 0::2] | (c[..., 1::2] << 4)
    return np.ascontiguousarray(words), np.ascontiguousarray(byte.astype(np.uint8).reshape(k // 512, 16, n))


def unpack_weight(words, scales, fmt):
    g, p, n, _ = words.shape
    if fmt == "e4m3":
        vals = np.ascontiguousarray(words).view(ml_dtypes.float8_e4m3fn).astype(np.float64)
    else:
        nib = np.empty((g, p, n, 4), np.uint8)
        nib[..., 0::2] = words & 0xF
        nib[..., 1::2] = words >> 4
        vals = E2M1[nib]
    vals = vals * np.repeat(np.exp2(scales.astype(np.float64) - 127.0), 8, axis=1)[..., None]
    return vals.transpose(0, 1, 3, 2).reshape(g * 512, n)

E4M3FN = np.array([(-1.0 if i & 128 else 1.0) * ((1.0 + (i & 7) / 8.0) * 2.0 ** (((i >> 3) & 15) - 7) if i & 120 else (i & 7) * 2.0 ** -9) for i in range(256)])


def e4m3fn_bytes(y):
    return np.clip(np.asarray(y, np.float64), -448.0, 448.0).astype(np.float32).astype(ml_dtypes.float8_e4m3fn).view(np.uint8)


def e4m3fn_values(b):
    return E4M3FN[b]


H, W, Z, D, F, E = 32, 32, 4, 512, 512, 256


def stable_softplus(t):
    return np.maximum(t, 0.0) + np.log(1.0 + np.exp(-np.abs(t)))


def draw0():
    s, r = mx_kscale(D), mx_kscale(F)
    thw = bf(np.random.standard_normal((H, W, D)) * s)
    tzh = bf(np.random.standard_normal((Z, H, D)) * s)
    twz = bf(np.random.standard_normal((W, Z, D)) * s)
    w1_words, w1_scales = pack_weight(np.random.standard_normal((D, F)) / np.sqrt(D) / s[:, None], "e4m3")
    b1 = bf(np.random.standard_normal(F) * 0.3)
    g = bf(np.random.standard_normal(F) * r)
    w2_words, w2_scales = pack_weight(np.random.standard_normal((F, E)) / np.sqrt(F) / r[:, None], "e4m3")
    b2 = bf(np.random.standard_normal(E) * 0.3)
    return {
        "thw": thw,
        "tzh": tzh,
        "twz": twz,
        "w1_words": w1_words,
        "w1_scales": w1_scales,
        "b1": b1,
        "g": g,
        "w2_words": w2_words,
        "w2_scales": w2_scales,
        "b2": b2,
    }


def core(thw, tzh, twz, w1_words, w1_scales, b1, g, w2_words, w2_scales, b2):
    w1q = unpack_weight(w1_words, w1_scales, "e4m3")
    a = mxq(f64(thw), 2, "e4m3") @ w1q
    b = mxq(f64(tzh), 2, "e4m3") @ w1q
    c = mxq(f64(twz), 2, "e4m3") @ w1q

    a_vox = a[:, :, None, :]
    b_vox = np.transpose(b, (1, 0, 2))[:, None, :, :]
    c_vox = c[None, :, :, :]
    u = a_vox + b_vox + c_vox + f64(b1)

    v = f64(g) * stable_softplus(u)

    return (mxq(v, 3, "e4m3") @ unpack_weight(w2_words, w2_scales, "e4m3")) + f64(b2)


def setup_inputs():
    drawn = draw0()
    full = np.asarray(drawn['thw']).astype(np.float64)
    scale = (np.abs(full).reshape(32, 32, 4, 128).max(axis=(3,)) / 448.0).astype(np.float32)
    given = {}
    for key, value in drawn.items():
        if key == 'thw':
            given['thw_bytes'] = e4m3fn_bytes(full / np.repeat(scale.astype(np.float64), 128, axis=2))
            given['thw_scale'] = scale
        else:
            given[key] = value
    return given


def reference(thw_bytes, thw_scale, tzh, twz, w1_words, w1_scales, b1, g, w2_words, w2_scales, b2):
    return core(e4m3fn_values(thw_bytes) * np.repeat(thw_scale.astype(np.float64), 128, axis=2), tzh, twz, w1_words, w1_scales, b1, g, w2_words, w2_scales, b2)

@@ -1,0 +1,434 @@
+import math
+from contextlib import ExitStack
+
+import concourse.mybir as mybir
+from concourse.masks import make_identity
+
+H, W, Z, D, F, E = 32, 32, 4, 512, 512, 256
+FLOPS = 2 * (H * W + Z * H + W * Z) * D * F + 2 * H * W * Z * F * E
+
+F32 = mybir.dt.float32
+BF16 = mybir.dt.bfloat16
+I32 = mybir.dt.int32
+U32 = mybir.dt.uint32
+U8 = mybir.dt.uint8
+FP8 = mybir.dt.float8_e4m3fn
+FP8X4 = mybir.dt.float8_e4m3fn_x4
+AF = mybir.ActivationFunctionType
+ALU = mybir.AluOpType
+
+P = 128
+NU = 8
+CLIP = 32.0
+ECLIP = math.exp(CLIP)
+
+
+def tile_tpvformersoftplusoccupancydecoder_d1p_kernel(
+    tc, thw_bytes, thw_scale, tzh, twz, w1_words, w1_scales, b1, g, w2_words, w2_scales, b2, out
+):
+    nc = tc.nc
+    with ExitStack() as ctx:
+        keep = ctx.enter_context(tc.tile_pool(name="keep", bufs=1))
+        head = ctx.enter_context(tc.tile_pool(name="head", bufs=1))
+        grp = ctx.enter_context(tc.tile_pool(name="grp", bufs=2))
+        upool = ctx.enter_context(tc.tile_pool(name="upool", bufs=2))
+        apool = ctx.enter_context(tc.tile_pool(name="apool", bufs=4))
+        epool = ctx.enter_context(tc.tile_pool(name="epool", bufs=8))
+        vpool = ctx.enter_context(tc.tile_pool(name="vpool", bufs=3))
+        opool = ctx.enter_context(tc.tile_pool(name="opool", bufs=3))
+        ptr = ctx.enter_context(tc.psum_pool(name="ptr", bufs=2))
+        pmm = ctx.enter_context(tc.psum_pool(name="pmm", bufs=4))
+        pout = ctx.enter_context(tc.psum_pool(name="pout", bufs=2))
+        ctx.enter_context(tc.manual_schedule())
+
+        ident = keep.tile([P, P], F32)
+        byt = keep.tile([P, NU, D], U8)
+        sc0 = keep.tile([P, 4], F32)
+        sc = keep.tile([P, NU - 1, 4], F32)
+        xa = keep.tile([P, NU, D], BF16, align_bytes=64)
+        xc = keep.tile([P, D], BF16, align_bytes=64)
+        xb = keep.tile([P, D], BF16, align_bytes=64)
+        w1raw = head.tile([P, F], I32, align_bytes=64)
+        s1raw = head.tile([P, F], U8, align_bytes=64)
+        w1p = keep.tile([P, 4, P], I32, align_bytes=64)
+        s1p = keep.tile([P, 4, P], U8, align_bytes=64)
+        w2w = keep.tile([P, E], I32, align_bytes=64)
+        s2w = keep.tile([P, E], U8, align_bytes=64)
+        b1t = keep.tile([P, 4], BF16)
+        gt = keep.tile([P, 4], BF16)
+        b1f = keep.tile([P, 4], F32)
+        gq = keep.tile([P, 4], F32)
+        b2t = keep.tile([P, E], BF16)
+        cbc = keep.tile([P, 2 * P], I32, align_bytes=64)
+        cbs = keep.tile([P, 2 * P], U8, align_bytes=64)
+        crc = keep.tile([P, Z, 16, W], I32, align_bytes=64)
+        crs = keep.tile([P, Z, 16, W], U8, align_bytes=64)
+        brc = keep.tile([P, Z, 16, W], I32, align_bytes=64)
+        brs = keep.tile([P, Z, 16, W], U8, align_bytes=64)
+        bsq = keep.tile([P, Z, 16, 4], U8, align_bytes=64)
+        gf = keep.tile([P, 4], F32)
+        b1c = keep.tile([P, 4], F32)
+        ac = keep.tile([P, NU, P], U32, align_bytes=64)
+        as_ = keep.tile([P, NU, P], U8, align_bytes=64)
+        bp = keep.tile([P, 4, Z, H], F32)
+        dum = keep.tile([P, 1], F32)
+
+        bytes_v = thw_bytes.rearrange("(j a) w k -> (a w) j k", a=4)
+        scale_v = thw_scale.rearrange("(j a) w q -> (a w) j q", a=4)
+        nc.vector.memset(dum[:], 0.0)
+        nc.vector.memset(s1raw[:].bitcast(I32), 0)
+        nc.vector.memset(cbs[:].bitcast(I32), 0)
+        nc.vector.memset(s2w[:].bitcast(I32), 0)
+
+        def load_s1(q, eng):
+            eng.dma_start(
+                out=s1raw[32 * q : 32 * q + 4, :].bitcast(I32),
+                in_=w1_scales[0, 4 * q : 4 * q + 4, :].bitcast(I32),
+            )
+
+        nc.sync.dma_start(out=byt[:, 0, :], in_=bytes_v[:, 0, :])
+        nc.scalar.dma_start(out=sc0[:], in_=scale_v[:, 0, :])
+        nc.sync.dma_start(out=xc[:], in_=twz.rearrange("w z d -> (w z) d"))
+        nc.scalar.dma_start(out=w1raw[:], in_=w1_words[0].rearrange("p n t -> p (n t)").bitcast(I32))
+        nc.sync.dma_start(out=xb[:], in_=tzh.rearrange("z h d -> (z h) d"))
+        load_s1(0, nc.scalar)
+        load_s1(1, nc.scalar)
+        load_s1(2, nc.sync)
+        load_s1(3, nc.sync)
+        nc.scalar.activation(out=dum[:], in_=dum[:], func=AF.Exp)
+        nc.sync.dma_start(out=b1t[:], in_=b1.rearrange("(p t) -> p t", t=4))
+        nc.sync.dma_start(out=byt[:, 1, :], in_=bytes_v[:, 1, :])
+        nc.sync.dma_start(out=sc[:], in_=scale_v[:, 1:, :])
+        nc.sync.dma_start(out=byt[:, 2:4, :], in_=bytes_v[:, 2:4, :])
+        make_identity(nc, ident[:])
+        nc.gpsimd.dma_start(out=gt[:], in_=g.rearrange("(p t) -> p t", t=4))
+        nc.sync.dma_start(out=byt[:, 4:8, :], in_=bytes_v[:, 4:8, :])
+        nc.sync.dma_start(out=w2w[:], in_=w2_words[0].rearrange("p n t -> p (n t)").bitcast(I32))
+        for q in range(4):
+            nc.sync.dma_start(
+                out=s2w[32 * q : 32 * q + 4, :].bitcast(I32),
+                in_=w2_scales[0, 4 * q : 4 * q + 4, :].bitcast(I32),
+            )
+        nc.sync.dma_start(out=b2t[:], in_=b2.partition_broadcast(P))
+        nc.gpsimd.tensor_copy(out=b1f[:], in_=b1t[:])
+        nc.gpsimd.tensor_scalar(out=gq[:], in0=gt[:], scalar1=1.0 / CLIP, scalar2=0.0, op0=ALU.mult, op1=ALU.add)
+        nc.gpsimd.tensor_copy(out=gf[:], in_=gt[:])
+        nc.gpsimd.tensor_scalar(out=b1c[:], in0=b1t[:], scalar1=1.0, scalar2=-CLIP, op0=ALU.mult, op1=ALU.add)
+
+        def widen(j, q, vec):
+            cols = slice(128 * q, 128 * q + 128)
+            src = byt[:, j, cols].bitcast(FP8)
+            s = sc0[:, q : q + 1] if j == 0 else sc[:, j - 1, q : q + 1]
+            if vec:
+                nc.vector.tensor_scalar(out=xa[:, j, cols], in0=src, scalar1=s, scalar2=None, op0=ALU.mult)
+            else:
+                nc.scalar.activation(out=xa[:, j, cols], in_=src, func=AF.Copy, scale=s)
+
+        def turn(dst, src):
+            words = src.bitcast(F32)
+            for u in range(2):
+                nc.tensor.transpose(dst[:, u, :], words[:, u : 2 * P : 2], ident[:])
+
+        banks = {}
+
+        def turn_a(first, count):
+            bank = ptr.tile([P, 2, 2, P], F32, name="trb")
+            for s in range(count):
+                turn(bank[:, s], xa[:, first + s, :])
+            banks["a"] = bank
+
+        def copy_a(count):
+            ga = grp.tile([P, 2, P, 4], BF16, name="ga", align_bytes=64)
+            nc.scalar.copy(
+                out=ga[:, 0:count].rearrange("p s r e -> p (s r e)").bitcast(F32).rearrange("p (s r u) -> p s r u", s=count, u=2),
+                in_=banks["a"][:, 0:count].rearrange("p s u r -> p s r u"),
+            )
+            return ga
+
+        def quant_a(ga, first, count):
+            nc.vector.quantize_mx(
+                out=ac[:, first : first + count, :].rearrange("p s r -> p (s r)").bitcast(FP8X4),
+                scales=as_[:, first : first + count, :].rearrange("p s r -> p (s r)"),
+                in_=ga[:, 0:count].rearrange("p s r e -> p (s r e)"),
+            )
+
+        def project(j, z):
+            bank = pmm.tile([P, 4, P], F32, name="mmb")
+            for t in range(4):
+                nc.tensor.matmul_mx(
+                    out=bank[:, t, :],
+                    lhsT=w1p[:, t, :].bitcast(FP8X4), lhsT_scale=s1p[:, t, :],
+                    rhs=ac[:, j, :].bitcast(FP8X4), rhs_scale=as_[:, j, :],
+                    start=True, stop=False,
+                )
+                nc.tensor.matmul_mx(
+                    out=bank[:, t, :],
+                    lhsT=w1p[:, t, :].bitcast(FP8X4), lhsT_scale=s1p[:, t, :],
+                    rhs=crc[:, z, 0:4].rearrange("p a w -> p (a w)").bitcast(FP8X4),
+                    rhs_scale=crs[:, z, 0:4].rearrange("p a w -> p (a w)"),
+                    start=False, stop=True,
+                )
+            return bank
+
+        us, es = {}, {}
+
+        def add_b(j, z, bank):
+            pair, s = divmod(j, 2)
+            if s == 0 and z == 0:
+                us[pair] = upool.tile([P, 4, 2, 512], F32, name="ut")
+            nc.vector.tensor_tensor(
+                out=us[pair][:, :, s, 128 * z : 128 * z + 128].rearrange("p t (a w) -> p t a w", a=4),
+                in0=bank[:].rearrange("p t (a w) -> p t a w", a=4),
+                in1=bp[:, :, z, 4 * j : 4 * j + 4].unsqueeze(3).to_broadcast([P, 4, 4, W]),
+                op=ALU.add,
+            )
+
+        def expo(j, half):
+            pair, s = divmod(j, 2)
+            if half == 0:
+                es[j] = epool.tile([P, 4, 512], F32, name="et")
+            cols = slice(256 * half, 256 * half + 256)
+            nc.scalar.activation(out=es[j][:, :, cols], in_=us[pair][:, :, s, cols], func=AF.Exp)
+
+        def clip(j):
+            e = es[j][:].rearrange("p t n -> p (t n)")
+            nc.vector.tensor_scalar(out=e, in0=e, scalar1=ECLIP, scalar2=None, op0=ALU.min)
+
+        def loga(j):
+            e = es[j][:].rearrange("p t n -> p (t n)")
+            nc.scalar.activation(out=e, in_=e, func=AF.Ln, bias=1.0)
+
+        def guard(pair):
+            for t in range(4):
+                a = us[pair][:, t].rearrange("p s n -> p (s n)")
+                nc.vector.tensor_scalar(
+                    out=a, in0=a, scalar1=CLIP, scalar2=gq[:, t : t + 1], op0=ALU.max, op1=ALU.mult
+                )
+
+        ybanks, ya = {}, {}
+
+        def y_project(z):
+            for t in range(4):
+                bank = pmm.tile([P, 512], F32, name="mmb")
+                for i, (codes, scales) in enumerate((
+                    (ac[:, 4:8].rearrange("p j r -> p (j r)"), as_[:, 4:8].rearrange("p j r -> p (j r)")),
+                    (crc[:, z].rearrange("p a w -> p (a w)"), crs[:, z].rearrange("p a w -> p (a w)")),
+                    (brc[:, z].rearrange("p a w -> p (a w)"), brs[:, z].rearrange("p a w -> p (a w)")),
+                )):
+                    nc.tensor.matmul_mx(
+                        out=bank[:],
+                        lhsT=w1p[:, t, :].bitcast(FP8X4), lhsT_scale=s1p[:, t, :],
+                        rhs=codes.bitcast(FP8X4), rhs_scale=scales,
+                        start=i == 0, stop=i == 2,
+                    )
+                ybanks[z, t] = bank
+
+        def y_evacuate(z):
+            es[4 + z] = epool.tile([P, 4, 512], F32, name="et")
+            ya[z] = apool.tile([P, 4, 512], F32, name="yt")
+            for t in range(4):
+                bank = ybanks[z, t]
+                nc.scalar.activation(out=es[4 + z][:, t, :], in_=bank[:], func=AF.Exp, bias=b1f[:, t : t + 1])
+                nc.scalar.activation(out=ya[z][:, t, :], in_=bank[:], func=AF.Relu, bias=b1c[:, t : t + 1])
+
+        def y_guard(z):
+            for t in range(4):
+                a = ya[z][:, t, :]
+                nc.vector.tensor_scalar(
+                    out=a, in0=a, scalar1=gq[:, t : t + 1], scalar2=gf[:, t : t + 1], op0=ALU.mult, op1=ALU.add
+                )
+
+        vts, vqs, obs = {}, {}, {}
+
+        def combine(j):
+            a = us[j // 2][:, :, j % 2, :] if j < 4 else ya[j - 4][:]
+            vt = vpool.tile([P, 512, 4], BF16, name="vt", align_bytes=64)
+            nc.vector.tensor_tensor(
+                out=vt[:].rearrange("p (c i) t -> p c t i", i=4),
+                in0=es[j][:].rearrange("p t (c i) -> p c t i", i=4),
+                in1=a.rearrange("p t (c i) -> p c t i", i=4),
+                op=ALU.mult,
+            )
+            vts[j] = vt
+
+        def quant_v(j):
+            vc = vpool.tile([P, 512], U32, name="vc", align_bytes=64)
+            vs = vpool.tile([P, 512], U8, name="vs", align_bytes=64)
+            nc.vector.quantize_mx(
+                out=vc[:].bitcast(FP8X4), scales=vs[:], in_=vts[j][:].rearrange("p n t -> p (n t)")
+            )
+            vqs[j] = (vc, vs)
+
+        def decode(j):
+            vc, vs = vqs[j]
+            for zp in range(2):
+                ob = pout.tile([P, 2, E], F32, name="ob")
+                for zz in range(2):
+                    cols = slice(128 * (2 * zp + zz), 128 * (2 * zp + zz) + 128)
+                    nc.tensor.matmul_mx(
+                        out=ob[:, zz, :],
+                        lhsT=vc[:, cols].bitcast(FP8X4), lhsT_scale=vs[:, cols],
+                        rhs=w2w[:].bitcast(FP8X4), rhs_scale=s2w[:],
+                        start=True, stop=True,
+                    )
+                obs[j, zp] = ob
+
+        out_v = out.rearrange("(j a) w z e -> (a w) j z e", a=4)
+
+        def finish(j):
+            ot = opool.tile([P, 4, E], F32, name="ot")
+            dst = out_v[:, j] if j < 4 else out_v[:, 4:8, j - 4, :]
+            for zp in range(2):
+                nc.vector.tensor_tensor(
+                    out=ot[:, 2 * zp : 2 * zp + 2, :], in0=obs[j, zp][:],
+                    in1=b2t[:].unsqueeze(1).to_broadcast([P, 2, E]), op=ALU.add,
+                )
+                if j == NU - 1:
+                    nc.sync.dma_start(out=dst[:, 2 * zp : 2 * zp + 2], in_=ot[:, 2 * zp : 2 * zp + 2, :])
+            if j < NU - 1:
+                nc.sync.dma_start(out=dst, in_=ot[:])
+
+        for q in range(4):
+            widen(0, q, q < 2)
+        cbank = ptr.tile([P, 2, 2, P], F32, name="trb")
+        turn(cbank[:, 0], xc[:])
+        gc = grp.tile([P, P, 4], BF16, name="gc", align_bytes=64)
+        nc.vector.tensor_copy(
+            out=gc[:].rearrange("p r e -> p (r e)").bitcast(F32).rearrange("p (z w u) -> p z w u", z=Z, u=2),
+            in_=cbank[:, 0].rearrange("p u (w z) -> p z w u", z=Z),
+        )
+        turn_a(0, 1)
+        ga0 = copy_a(1)
+        bbank = ptr.tile([P, 2, 2, P], F32, name="trb")
+        turn(bbank[:, 0], xb[:])
+        gb = grp.tile([P, P, 4], BF16, name="gb", align_bytes=64)
+        nc.scalar.copy(
+            out=gb[:].rearrange("p r e -> p (r e)").bitcast(F32).rearrange("p (r u) -> p r u", u=2),
+            in_=bbank[:, 0].rearrange("p u r -> p r u"),
+        )
+        nc.vector.tensor_copy(out=w1p[:], in_=w1raw[:].rearrange("p (m t) -> p t m", t=4))
+        nc.vector.quantize_mx(
+            out=cbc[:, 0:P].bitcast(FP8X4), scales=cbs[:, 0:P], in_=gc[:].rearrange("p r e -> p (r e)")
+        )
+        nc.vector.tensor_copy(out=s1p[:], in_=s1raw[:].rearrange("p (m t) -> p t m", t=4))
+        nc.vector.quantize_mx(
+            out=cbc[:, P : 2 * P].bitcast(FP8X4), scales=cbs[:, P : 2 * P], in_=gb[:].rearrange("p r e -> p (r e)")
+        )
+        quant_a(ga0, 0, 1)
+
+        def spread_c(r0, r1):
+            nc.vector.tensor_copy(
+                out=crc[:, :, r0:r1, :],
+                in_=cbc[:, 0:P].rearrange("p (z w) -> p z w", z=Z).unsqueeze(2).to_broadcast([P, Z, r1 - r0, W]),
+            )
+            nc.vector.tensor_copy(
+                out=crs[:, :, r0:r1, :].bitcast(I32),
+                in_=cbs[:, 0:P].bitcast(I32).rearrange("p (z w) -> p z w", z=Z).unsqueeze(2).to_broadcast([P, Z, r1 - r0, W // 4]),
+            )
+
+        spread_c(0, 4)
+        for q in range(4):
+            widen(1, q, False)
+        def spread_b_scales():
+            late = cbs[:, P : 2 * P].rearrange("p (z h) -> p z h", z=Z)[:, :, 16:32]
+            for i in range(4):
+                nc.vector.tensor_copy(out=bsq[:, :, :, i], in_=late)
+            nc.vector.tensor_copy(
+                out=brs[:].rearrange("p z a w -> p (z a w)").bitcast(I32).rearrange("p (r w) -> p r w", w=W // 4),
+                in_=bsq[:].rearrange("p z a i -> p (z a i)").bitcast(I32).unsqueeze(2).to_broadcast([P, 16 * Z, W // 4]),
+            )
+
+        def spread_b(z):
+            nc.vector.tensor_copy(
+                out=brc[:, z],
+                in_=cbc[:, P + 32 * z + 16 : P + 32 * z + 32].unsqueeze(2).to_broadcast([P, 16, W]),
+            )
+
+        bb = pmm.tile([P, 4, P], F32, name="mmb")
+        for t in range(4):
+            nc.tensor.matmul_mx(
+                out=bb[:, t, :],
+                lhsT=w1p[:, t, :].bitcast(FP8X4), lhsT_scale=s1p[:, t, :],
+                rhs=cbc[:, P : 2 * P].bitcast(FP8X4), rhs_scale=cbs[:, P : 2 * P],
+                start=True, stop=True,
+            )
+        nc.vector.tensor_tensor(
+            out=bp[:].rearrange("p t z h -> p t (z h)"), in0=bb[:],
+            in1=b1f[:].unsqueeze(2).to_broadcast([P, 4, P]), op=ALU.add,
+        )
+        for j in range(2, NU):
+            for q in range(4):
+                widen(j, q, False)
+
+        gas = {}
+        for j in range(4):
+            for z in range(Z):
+                bank = project(j, z)
+                add_b(j, z, bank)
+            if j == 0:
+                turn_a(1, 1)
+                quant_a(copy_a(1), 1, 1)
+            if j == 1:
+                spread_c(4, 16)
+            if j < 3:
+                turn_a(2 * j + 2, 2)
+                gas[j] = copy_a(2)
+            for half in range(2):
+                expo(j, half)
+            if j > 0:
+                quant_a(gas[j - 1], 2 * j, 2)
+            if j == 1:
+                spread_b_scales()
+                spread_b(0)
+            if j == 2:
+                spread_b(1)
+        y_project(0)
+        y_evacuate(0)
+        clip(0)
+        spread_b(2)
+        spread_b(3)
+        clip(1)
+        guard(0)
+        clip(2)
+        clip(3)
+        guard(1)
+        y_project(1)
+        y_evacuate(1)
+        y_guard(0)
+        clip(4)
+        y_guard(1)
+        clip(5)
+        y_project(2)
+        for j in range(6):
+            loga(j)
+
+        def step(k):
+            combine(k)
+            if k >= 2:
+                finish(k - 2)
+            if k >= 1:
+                quant_v(k - 1)
+                decode(k - 1)
+
+        for k in range(4):
+            step(k)
+        y_evacuate(2)
+        y_project(3)
+        y_evacuate(3)
+        step(4)
+        y_guard(2)
+        clip(6)
+        step(5)
+        y_guard(3)
+        clip(7)
+        loga(6)
+        loga(7)
+        step(6)
+        combine(7)
+        quant_v(6)
+        decode(6)
+        finish(5)
+        quant_v(7)
+        decode(7)
+        finish(6)
+        finish(7)

@@ -19,8 +19,10 @@ ALU = mybir.AluOpType
 
 P = 128
 NU = 8
-CLIP = 32.0
-ECLIP = math.exp(CLIP)
+NV = 512
+KNEE = 16.0
+EPS = 2.0 ** -60
+WI = 4
 
 
 def tile_tpvformersoftplusoccupancydecoder_d1p_kernel(
@@ -29,244 +31,272 @@ def tile_tpvformersoftplusoccupancydecoder_d1p_kernel(
     nc = tc.nc
     with ExitStack() as ctx:
         keep = ctx.enter_context(tc.tile_pool(name="keep", bufs=1))
-        head = ctx.enter_context(tc.tile_pool(name="head", bufs=1))
         grp = ctx.enter_context(tc.tile_pool(name="grp", bufs=2))
-        upool = ctx.enter_context(tc.tile_pool(name="upool", bufs=2))
-        apool = ctx.enter_context(tc.tile_pool(name="apool", bufs=4))
-        epool = ctx.enter_context(tc.tile_pool(name="epool", bufs=8))
         vpool = ctx.enter_context(tc.tile_pool(name="vpool", bufs=3))
         opool = ctx.enter_context(tc.tile_pool(name="opool", bufs=3))
-        ptr = ctx.enter_context(tc.psum_pool(name="ptr", bufs=2))
-        pmm = ctx.enter_context(tc.psum_pool(name="pmm", bufs=4))
-        pout = ctx.enter_context(tc.psum_pool(name="pout", bufs=2))
+        psum = ctx.enter_context(tc.psum_pool(name="psum", bufs=1))
         ctx.enter_context(tc.manual_schedule())
 
-        ident = keep.tile([P, P], F32)
-        byt = keep.tile([P, NU, D], U8)
-        sc0 = keep.tile([P, 4], F32)
-        sc = keep.tile([P, NU - 1, 4], F32)
-        xa = keep.tile([P, NU, D], BF16, align_bytes=64)
-        xc = keep.tile([P, D], BF16, align_bytes=64)
-        xb = keep.tile([P, D], BF16, align_bytes=64)
-        w1raw = head.tile([P, F], I32, align_bytes=64)
-        s1raw = head.tile([P, F], U8, align_bytes=64)
-        w1p = keep.tile([P, 4, P], I32, align_bytes=64)
-        s1p = keep.tile([P, 4, P], U8, align_bytes=64)
-        w2w = keep.tile([P, E], I32, align_bytes=64)
-        s2w = keep.tile([P, E], U8, align_bytes=64)
-        b1t = keep.tile([P, 4], BF16)
-        gt = keep.tile([P, 4], BF16)
-        b1f = keep.tile([P, 4], F32)
-        gq = keep.tile([P, 4], F32)
-        b2t = keep.tile([P, E], BF16)
-        cbc = keep.tile([P, 2 * P], I32, align_bytes=64)
-        cbs = keep.tile([P, 2 * P], U8, align_bytes=64)
-        crc = keep.tile([P, Z, 16, W], I32, align_bytes=64)
-        crs = keep.tile([P, Z, 16, W], U8, align_bytes=64)
-        brc = keep.tile([P, Z, 16, W], I32, align_bytes=64)
-        brs = keep.tile([P, Z, 16, W], U8, align_bytes=64)
-        bsq = keep.tile([P, Z, 16, 4], U8, align_bytes=64)
-        gf = keep.tile([P, 4], F32)
-        b1c = keep.tile([P, 4], F32)
-        ac = keep.tile([P, NU, P], U32, align_bytes=64)
-        as_ = keep.tile([P, NU, P], U8, align_bytes=64)
-        bp = keep.tile([P, 4, Z, H], F32)
-        dum = keep.tile([P, 1], F32)
+        ident = keep.tile([P, P], F32, name="ident")
+        byt0 = keep.tile([P, 2, D], U8, name="byt0")
+        byt1 = keep.tile([P, NU - 2, D], U8, name="byt1")
+        sc = keep.tile([P, NU, 4], F32, name="sc")
+        nsc = keep.tile([P, NU, 4], F32, name="nsc")
+        xa = [keep.tile([P, D], BF16, name="xa%d" % j, align_bytes=64) for j in range(NU)]
+        xc = keep.tile([P, D], BF16, name="xc", align_bytes=64)
+        xb = keep.tile([P, D], BF16, name="xb", align_bytes=64)
+        nxc = keep.tile([P, D], BF16, name="nxc", align_bytes=64)
+        nxb = keep.tile([P, D], BF16, name="nxb", align_bytes=64)
+        w1raw = keep.tile([P, F], I32, name="w1raw", align_bytes=64)
+        s1raw = keep.tile([P, F], U8, name="s1raw", align_bytes=64)
+        w1p = keep.tile([P, 4, P], I32, name="w1p", align_bytes=64)
+        s1p = keep.tile([P, 4, P], U8, name="s1p", align_bytes=64)
+        w2w = keep.tile([P, E], I32, name="w2w", align_bytes=64)
+        s2w = keep.tile([P, E], U8, name="s2w", align_bytes=64)
+        b1t = keep.tile([P, 4], BF16, name="b1t")
+        gt = keep.tile([P, 4], BF16, name="gt")
+        nb1 = keep.tile([P, 4], F32, name="nb1")
+        gk = keep.tile([P, 4], F32, name="gk")
+        ng = keep.tile([P, 4], F32, name="ng")
+        b2t = keep.tile([P, E], BF16, name="b2t")
+        cq = keep.tile([P, P], I32, name="cq", align_bytes=64)
+        cqs = keep.tile([P, P], U8, name="cqs", align_bytes=64)
+        bq = keep.tile([P, P], I32, name="bq", align_bytes=64)
+        bqs = keep.tile([P, P], U8, name="bqs", align_bytes=64)
+        crc = keep.tile([P, NV], I32, name="crc", align_bytes=64)
+        crs = keep.tile([P, NV], U8, name="crs", align_bytes=64)
+        brc = keep.tile([P, NU * NV], I32, name="brc", align_bytes=64)
+        brs = keep.tile([P, NU * NV], U8, name="brs", align_bytes=64)
+        bs4 = keep.tile([P, P, 4], U8, name="bs4", align_bytes=64)
+        ac = keep.tile([P, NU * P], U32, name="ac", align_bytes=64)
+        as_ = keep.tile([P, NU * P], U8, name="as_", align_bytes=64)
+        bp = keep.tile([P, 4, P], F32, name="bp")
+        dum = keep.tile([P, 1], F32, name="dum")
+        soft = [keep.tile([P, 4, NV], F32, name="soft%d" % j) for j in range(NU)]
+        big = {}
 
         bytes_v = thw_bytes.rearrange("(j a) w k -> (a w) j k", a=4)
         scale_v = thw_scale.rearrange("(j a) w q -> (a w) j q", a=4)
         nc.vector.memset(dum[:], 0.0)
         nc.vector.memset(s1raw[:].bitcast(I32), 0)
-        nc.vector.memset(cbs[:].bitcast(I32), 0)
+        nc.vector.memset(cqs[:].bitcast(I32), 0)
+        nc.vector.memset(bqs[:].bitcast(I32), 0)
         nc.vector.memset(s2w[:].bitcast(I32), 0)
 
-        def load_s1(q, eng):
+        def load_rows(tile, scales, q, eng):
             eng.dma_start(
-                out=s1raw[32 * q : 32 * q + 4, :].bitcast(I32),
-                in_=w1_scales[0, 4 * q : 4 * q + 4, :].bitcast(I32),
+                out=tile[32 * q : 32 * q + 4, :].bitcast(I32),
+                in_=scales[0, 4 * q : 4 * q + 4, :].bitcast(I32),
             )
 
-        nc.sync.dma_start(out=byt[:, 0, :], in_=bytes_v[:, 0, :])
-        nc.scalar.dma_start(out=sc0[:], in_=scale_v[:, 0, :])
-        nc.sync.dma_start(out=xc[:], in_=twz.rearrange("w z d -> (w z) d"))
-        nc.scalar.dma_start(out=w1raw[:], in_=w1_words[0].rearrange("p n t -> p (n t)").bitcast(I32))
         nc.sync.dma_start(out=xb[:], in_=tzh.rearrange("z h d -> (z h) d"))
-        load_s1(0, nc.scalar)
-        load_s1(1, nc.scalar)
-        load_s1(2, nc.sync)
-        load_s1(3, nc.sync)
-        nc.scalar.activation(out=dum[:], in_=dum[:], func=AF.Exp)
+        nc.scalar.dma_start(out=xc[:], in_=twz.rearrange("w z d -> (w z) d"))
+        nc.sync.dma_start(out=byt0[:], in_=bytes_v[:, 0:2, :])
+        nc.scalar.dma_start(out=sc[:], in_=scale_v)
+        nc.sync.dma_start(out=w1raw[:], in_=w1_words[0].rearrange("p n t -> p (n t)").bitcast(I32))
+        for q in range(4):
+            load_rows(s1raw, w1_scales, q, nc.sync)
+        nc.scalar.activation(out=dum[:], in_=dum[:], func=AF.Sigmoid)
         nc.sync.dma_start(out=b1t[:], in_=b1.rearrange("(p t) -> p t", t=4))
-        nc.sync.dma_start(out=byt[:, 1, :], in_=bytes_v[:, 1, :])
-        nc.sync.dma_start(out=sc[:], in_=scale_v[:, 1:, :])
-        nc.sync.dma_start(out=byt[:, 2:4, :], in_=bytes_v[:, 2:4, :])
+        nc.sync.dma_start(out=byt1[:], in_=bytes_v[:, 2:NU, :])
+        nc.sync.dma_start(out=gt[:], in_=g.rearrange("(p t) -> p t", t=4))
         make_identity(nc, ident[:])
-        nc.gpsimd.dma_start(out=gt[:], in_=g.rearrange("(p t) -> p t", t=4))
-        nc.sync.dma_start(out=byt[:, 4:8, :], in_=bytes_v[:, 4:8, :])
         nc.sync.dma_start(out=w2w[:], in_=w2_words[0].rearrange("p n t -> p (n t)").bitcast(I32))
         for q in range(4):
-            nc.sync.dma_start(
-                out=s2w[32 * q : 32 * q + 4, :].bitcast(I32),
-                in_=w2_scales[0, 4 * q : 4 * q + 4, :].bitcast(I32),
-            )
+            load_rows(s2w, w2_scales, q, nc.sync)
         nc.sync.dma_start(out=b2t[:], in_=b2.partition_broadcast(P))
-        nc.gpsimd.tensor_copy(out=b1f[:], in_=b1t[:])
-        nc.gpsimd.tensor_scalar(out=gq[:], in0=gt[:], scalar1=1.0 / CLIP, scalar2=0.0, op0=ALU.mult, op1=ALU.add)
-        nc.gpsimd.tensor_copy(out=gf[:], in_=gt[:])
-        nc.gpsimd.tensor_scalar(out=b1c[:], in0=b1t[:], scalar1=1.0, scalar2=-CLIP, op0=ALU.mult, op1=ALU.add)
+
+        def scaled(eng, dst, src, factor):
+            eng.tensor_scalar(out=dst, in0=src, scalar1=factor, scalar2=0.0, op0=ALU.mult, op1=ALU.add)
+
+        def bank_tile(k):
+            return psum.tile([P, NV], F32, name="bank%d" % k)
 
         def widen(j, q, vec):
             cols = slice(128 * q, 128 * q + 128)
-            src = byt[:, j, cols].bitcast(FP8)
-            s = sc0[:, q : q + 1] if j == 0 else sc[:, j - 1, q : q + 1]
+            src = (byt0[:, j, cols] if j < 2 else byt1[:, j - 2, cols]).bitcast(FP8)
+            s = nsc[:, j, q : q + 1]
             if vec:
-                nc.vector.tensor_scalar(out=xa[:, j, cols], in0=src, scalar1=s, scalar2=None, op0=ALU.mult)
+                nc.vector.tensor_scalar(out=xa[j][:, cols], in0=src, scalar1=s, scalar2=None, op0=ALU.mult)
             else:
-                nc.scalar.activation(out=xa[:, j, cols], in_=src, func=AF.Copy, scale=s)
+                nc.scalar.activation(out=xa[j][:, cols], in_=src, func=AF.Copy, scale=s)
 
-        def turn(dst, src):
-            words = src.bitcast(F32)
-            for u in range(2):
-                nc.tensor.transpose(dst[:, u, :], words[:, u : 2 * P : 2], ident[:])
+        def widen_s(j):
+            for q in range(4):
+                widen(j, q, False)
 
-        banks = {}
+        def turn(k, srcs):
+            bank = bank_tile(k)
+            for s, src in enumerate(srcs):
+                words = src[:].bitcast(F32)
+                for u in range(2):
+                    nc.tensor.transpose(bank[:, 256 * s + P * u : 256 * s + P * u + P], words[:, u : 2 * P : 2], ident[:])
+            return bank
 
-        def turn_a(first, count):
-            bank = ptr.tile([P, 2, 2, P], F32, name="trb")
-            for s in range(count):
-                turn(bank[:, s], xa[:, first + s, :])
-            banks["a"] = bank
+        def words_of(tile):
+            return tile.rearrange("p r e -> p (r e)").bitcast(F32)
 
-        def copy_a(count):
-            ga = grp.tile([P, 2, P, 4], BF16, name="ga", align_bytes=64)
-            nc.scalar.copy(
-                out=ga[:, 0:count].rearrange("p s r e -> p (s r e)").bitcast(F32).rearrange("p (s r u) -> p s r u", s=count, u=2),
-                in_=banks["a"][:, 0:count].rearrange("p s u r -> p s r u"),
+        def copy_a(bank, count, vec=False):
+            ga = grp.tile([P, 2 * P, 4], BF16, name="ga", align_bytes=64)
+            (nc.vector.tensor_copy if vec else nc.scalar.copy)(
+                out=words_of(ga[:, 0 : count * P]).rearrange("p (s r u) -> p s r u", s=count, u=2),
+                in_=bank[:, 0 : count * 256].rearrange("p (s u r) -> p s r u", s=count, u=2),
             )
             return ga
 
+        def quant(codes, scales, grouped):
+            nc.vector.quantize_mx(out=codes.bitcast(FP8X4), scales=scales, in_=grouped.rearrange("p r e -> p (r e)"))
+
         def quant_a(ga, first, count):
-            nc.vector.quantize_mx(
-                out=ac[:, first : first + count, :].rearrange("p s r -> p (s r)").bitcast(FP8X4),
-                scales=as_[:, first : first + count, :].rearrange("p s r -> p (s r)"),
-                in_=ga[:, 0:count].rearrange("p s r e -> p (s r e)"),
+            cols = slice(first * P, (first + count) * P)
+            quant(ac[:, cols], as_[:, cols], ga[:, 0 : count * P])
+
+        def spread_c():
+            nc.vector.tensor_copy(
+                out=crc[:].rearrange("p (z a w) -> p z a w", z=Z, a=4),
+                in_=cq[:].rearrange("p (z w) -> p z w", z=Z).unsqueeze(2).to_broadcast([P, Z, 4, W]),
+            )
+            nc.vector.tensor_copy(
+                out=crs[:].bitcast(I32).rearrange("p (z a w) -> p z a w", z=Z, a=4),
+                in_=cqs[:].bitcast(I32).rearrange("p (z w) -> p z w", z=Z).unsqueeze(2).to_broadcast([P, Z, 4, W // 4]),
             )
 
-        def project(j, z):
-            bank = pmm.tile([P, 4, P], F32, name="mmb")
-            for t in range(4):
+        def spread_b_bytes():
+            for i in range(4):
+                nc.vector.tensor_copy(out=bs4[:, :, i], in_=bqs[:])
+
+        def spread_b_scales(first, count):
+            rows = slice(16 * first, 16 * (first + count))
+            cols = slice(NV * first, NV * (first + count))
+            nc.vector.tensor_copy(
+                out=brs[:, cols].bitcast(I32).rearrange("p (r w) -> p r w", w=W // 4),
+                in_=bs4[:, rows].rearrange("p r i -> p (r i)").bitcast(I32).unsqueeze(2).to_broadcast([P, 16 * count, W // 4]),
+            )
+
+        def spread_b(first, count):
+            rows = slice(16 * first, 16 * (first + count))
+            cols = slice(NV * first, NV * (first + count))
+            nc.vector.tensor_copy(
+                out=brc[:, cols].rearrange("p (r w) -> p r w", w=W),
+                in_=bq[:, rows].unsqueeze(2).to_broadcast([P, 16 * count, W]),
+            )
+
+        turnof = {"next": 0}
+
+        def project(j, t, ring):
+            bank = bank_tile(ring[turnof["next"] % len(ring)])
+            turnof.update({"next": turnof["next"] + 1})
+            lhs, lhs_s = w1p[:, t, :].bitcast(FP8X4), s1p[:, t, :]
+            ucols = slice(NV * j, NV * (j + 1))
+            acols = slice(P * j, P * (j + 1))
+            nc.tensor.matmul_mx(out=bank[:], lhsT=lhs, lhsT_scale=lhs_s, rhs=crc[:].bitcast(FP8X4), rhs_scale=crs[:], start=True, stop=False)
+            for z in range(Z):
                 nc.tensor.matmul_mx(
-                    out=bank[:, t, :],
-                    lhsT=w1p[:, t, :].bitcast(FP8X4), lhsT_scale=s1p[:, t, :],
-                    rhs=ac[:, j, :].bitcast(FP8X4), rhs_scale=as_[:, j, :],
-                    start=True, stop=False,
+                    out=bank[:, P * z : P * (z + 1)], lhsT=lhs, lhsT_scale=lhs_s,
+                    rhs=ac[:, acols].bitcast(FP8X4), rhs_scale=as_[:, acols], start=False, stop=False,
                 )
+            nc.tensor.matmul_mx(out=bank[:], lhsT=lhs, lhsT_scale=lhs_s, rhs=brc[:, ucols].bitcast(FP8X4), rhs_scale=brs[:, ucols], start=False, stop=True)
+            return bank
+
+        def project2(j, t, ring):
+            bank = bank_tile(ring[turnof["next"] % len(ring)])
+            turnof.update({"next": turnof["next"] + 1})
+            lhs, lhs_s = w1p[:, t, :].bitcast(FP8X4), s1p[:, t, :]
+            acols = slice(P * j, P * (j + 1))
+            nc.tensor.matmul_mx(out=bank[:], lhsT=lhs, lhsT_scale=lhs_s, rhs=crc[:].bitcast(FP8X4), rhs_scale=crs[:], start=True, stop=False)
+            for z in range(Z):
                 nc.tensor.matmul_mx(
-                    out=bank[:, t, :],
-                    lhsT=w1p[:, t, :].bitcast(FP8X4), lhsT_scale=s1p[:, t, :],
-                    rhs=crc[:, z, 0:4].rearrange("p a w -> p (a w)").bitcast(FP8X4),
-                    rhs_scale=crs[:, z, 0:4].rearrange("p a w -> p (a w)"),
-                    start=False, stop=True,
+                    out=bank[:, P * z : P * (z + 1)], lhsT=lhs, lhsT_scale=lhs_s,
+                    rhs=ac[:, acols].bitcast(FP8X4), rhs_scale=as_[:, acols], start=False, stop=z == Z - 1,
                 )
             return bank
 
-        us, es = {}, {}
-
-        def add_b(j, z, bank):
-            pair, s = divmod(j, 2)
-            if s == 0 and z == 0:
-                us[pair] = upool.tile([P, 4, 2, 512], F32, name="ut")
+        def add_b(j, t, bank):
+            if t == 0:
+                big[j] = keep.tile([P, 4, NV], F32, name="big%d" % j)
             nc.vector.tensor_tensor(
-                out=us[pair][:, :, s, 128 * z : 128 * z + 128].rearrange("p t (a w) -> p t a w", a=4),
-                in0=bank[:].rearrange("p t (a w) -> p t a w", a=4),
-                in1=bp[:, :, z, 4 * j : 4 * j + 4].unsqueeze(3).to_broadcast([P, 4, 4, W]),
+                out=big[j][:, t, :].rearrange("p (r w) -> p r w", w=W),
+                in0=bank[:].rearrange("p (r w) -> p r w", w=W),
+                in1=bp[:, t, 16 * j : 16 * j + 16].unsqueeze(2).to_broadcast([P, 16, W]),
                 op=ALU.add,
             )
 
-        def expo(j, half):
-            pair, s = divmod(j, 2)
-            if half == 0:
-                es[j] = epool.tile([P, 4, 512], F32, name="et")
-            cols = slice(256 * half, 256 * half + 256)
-            nc.scalar.activation(out=es[j][:, :, cols], in_=us[pair][:, :, s, cols], func=AF.Exp)
+        def sigm2(j, t0, t1):
+            nc.scalar.activation(
+                out=soft[j][:, t0:t1, :].rearrange("p t n -> p (t n)"),
+                in_=big[j][:, t0:t1, :].rearrange("p t n -> p (t n)"), func=AF.Sigmoid,
+            )
 
-        def clip(j):
-            e = es[j][:].rearrange("p t n -> p (t n)")
-            nc.vector.tensor_scalar(out=e, in0=e, scalar1=ECLIP, scalar2=None, op0=ALU.min)
+        def knee2(j, t):
+            e = big[j][:, t, :]
+            nc.vector.tensor_scalar(out=e, in0=e, scalar1=-KNEE, scalar2=gk[:, t : t + 1], op0=ALU.min, op1=ALU.mult)
 
-        def loga(j):
-            e = es[j][:].rearrange("p t n -> p (t n)")
-            nc.scalar.activation(out=e, in_=e, func=AF.Ln, bias=1.0)
+        def sigm(j, t, bank):
+            nc.scalar.activation(out=soft[j][:, t, :], in_=bank[:], func=AF.Sigmoid, bias=nb1[:, t : t + 1])
 
-        def guard(pair):
-            for t in range(4):
-                a = us[pair][:, t].rearrange("p s n -> p (s n)")
-                nc.vector.tensor_scalar(
-                    out=a, in0=a, scalar1=CLIP, scalar2=gq[:, t : t + 1], op0=ALU.max, op1=ALU.mult
-                )
+        def knee(j, t, bank):
+            if t == 0:
+                big[j] = keep.tile([P, 4, NV], F32, name="big%d" % j)
+            nc.vector.tensor_scalar(
+                out=big[j][:, t, :], in0=bank[:], scalar1=nb1[:, t : t + 1], scalar2=-KNEE, op0=ALU.add, op1=ALU.min
+            )
 
-        ybanks, ya = {}, {}
+        def loga(j, t0=0, t1=4):
+            e = soft[j][:, t0:t1, :].rearrange("p t n -> p (t n)")
+            nc.scalar.activation(out=e, in_=e, func=AF.Ln, bias=EPS)
 
-        def y_project(z):
-            for t in range(4):
-                bank = pmm.tile([P, 512], F32, name="mmb")
-                for i, (codes, scales) in enumerate((
-                    (ac[:, 4:8].rearrange("p j r -> p (j r)"), as_[:, 4:8].rearrange("p j r -> p (j r)")),
-                    (crc[:, z].rearrange("p a w -> p (a w)"), crs[:, z].rearrange("p a w -> p (a w)")),
-                    (brc[:, z].rearrange("p a w -> p (a w)"), brs[:, z].rearrange("p a w -> p (a w)")),
-                )):
-                    nc.tensor.matmul_mx(
-                        out=bank[:],
-                        lhsT=w1p[:, t, :].bitcast(FP8X4), lhsT_scale=s1p[:, t, :],
-                        rhs=codes.bitcast(FP8X4), rhs_scale=scales,
-                        start=i == 0, stop=i == 2,
-                    )
-                ybanks[z, t] = bank
+        def gain(j, t):
+            e = soft[j][:, t, :]
+            nc.vector.tensor_scalar(out=e, in0=e, scalar1=-KNEE, scalar2=gk[:, t : t + 1], op0=ALU.max, op1=ALU.mult)
 
-        def y_evacuate(z):
-            es[4 + z] = epool.tile([P, 4, 512], F32, name="et")
-            ya[z] = apool.tile([P, 4, 512], F32, name="yt")
-            for t in range(4):
-                bank = ybanks[z, t]
-                nc.scalar.activation(out=es[4 + z][:, t, :], in_=bank[:], func=AF.Exp, bias=b1f[:, t : t + 1])
-                nc.scalar.activation(out=ya[z][:, t, :], in_=bank[:], func=AF.Relu, bias=b1c[:, t : t + 1])
+        def floor_s(j, t0, t1):
+            e = soft[j][:, t0:t1, :].rearrange("p t n -> p (t n)")
+            nc.vector.tensor_scalar(out=e, in0=e, scalar1=math.exp(-KNEE), scalar2=None, op0=ALU.max)
 
-        def y_guard(z):
-            for t in range(4):
-                a = ya[z][:, t, :]
-                nc.vector.tensor_scalar(
-                    out=a, in0=a, scalar1=gq[:, t : t + 1], scalar2=gf[:, t : t + 1], op0=ALU.mult, op1=ALU.add
-                )
+        def floor_l(j, t0, t1):
+            e = soft[j][:, t0:t1, :].rearrange("p t n -> p (t n)")
+            nc.vector.tensor_scalar(out=e, in0=e, scalar1=-KNEE, scalar2=None, op0=ALU.max)
+
+        def gain_big(j, t):
+            e = big[j][:, t, :]
+            nc.vector.tensor_scalar(out=e, in0=e, scalar1=gk[:, t : t + 1], scalar2=None, op0=ALU.mult)
+
+        def lower(j, t, bank):
+            e = soft[j][:, t, :]
+            nc.vector.scalar_tensor_tensor(out=e, in0=bank[:], scalar=nb1[:, t : t + 1], in1=e, op0=ALU.add, op1=ALU.min)
 
         vts, vqs, obs = {}, {}, {}
 
-        def combine(j):
-            a = us[j // 2][:, :, j % 2, :] if j < 4 else ya[j - 4][:]
-            vt = vpool.tile([P, 512, 4], BF16, name="vt", align_bytes=64)
+        def combine(j, c0=0, c1=NV):
+            if c0 == 0:
+                vts[j] = vpool.tile([P, NV, 4], BF16, name="vt", align_bytes=64)
+            if j in big:
+                other = big[j][:, :, c0:c1].rearrange("p t (c i) -> p c t i", i=WI)
+            else:
+                other = ng[:].unsqueeze(1).unsqueeze(3).to_broadcast([P, (c1 - c0) // WI, 4, WI])
             nc.vector.tensor_tensor(
-                out=vt[:].rearrange("p (c i) t -> p c t i", i=4),
-                in0=es[j][:].rearrange("p t (c i) -> p c t i", i=4),
-                in1=a.rearrange("p t (c i) -> p c t i", i=4),
+                out=vts[j][:, c0:c1].rearrange("p (c i) t -> p c t i", i=WI),
+                in0=soft[j][:, :, c0:c1].rearrange("p t (c i) -> p c t i", i=WI),
+                in1=other,
                 op=ALU.mult,
             )
-            vts[j] = vt
 
-        def quant_v(j):
-            vc = vpool.tile([P, 512], U32, name="vc", align_bytes=64)
-            vs = vpool.tile([P, 512], U8, name="vs", align_bytes=64)
-            nc.vector.quantize_mx(
-                out=vc[:].bitcast(FP8X4), scales=vs[:], in_=vts[j][:].rearrange("p n t -> p (n t)")
-            )
-            vqs[j] = (vc, vs)
-
-        def decode(j):
+        def quant_v(j, c0=0, c1=NV):
+            if c0 == 0:
+                vc = vpool.tile([P, NV], U32, name="vc", align_bytes=64)
+                vs = vpool.tile([P, NV], U8, name="vs", align_bytes=64)
+                vqs[j] = (vc, vs)
             vc, vs = vqs[j]
-            for zp in range(2):
-                ob = pout.tile([P, 2, E], F32, name="ob")
+            quant(vc[:, c0:c1], vs[:, c0:c1], vts[j][:, c0:c1])
+
+        def decode(j, ring, halves=(0, 1)):
+            vc, vs = vqs[j]
+            for zp in halves:
+                ob = bank_tile(ring[zp])
                 for zz in range(2):
-                    cols = slice(128 * (2 * zp + zz), 128 * (2 * zp + zz) + 128)
+                    cols = slice(P * (2 * zp + zz), P * (2 * zp + zz + 1))
                     nc.tensor.matmul_mx(
-                        out=ob[:, zz, :],
+                        out=ob[:, E * zz : E * (zz + 1)],
                         lhsT=vc[:, cols].bitcast(FP8X4), lhsT_scale=vs[:, cols],
                         rhs=w2w[:].bitcast(FP8X4), rhs_scale=s2w[:],
                         start=True, stop=True,
@@ -274,161 +304,188 @@ def tile_tpvformersoftplusoccupancydecoder_d1p_kernel(
                 obs[j, zp] = ob
 
         out_v = out.rearrange("(j a) w z e -> (a w) j z e", a=4)
+        ots = {}
 
-        def finish(j):
-            ot = opool.tile([P, 4, E], F32, name="ot")
-            dst = out_v[:, j] if j < 4 else out_v[:, 4:8, j - 4, :]
-            for zp in range(2):
+        def finish(j, split=False, halves=(0, 1)):
+            for zp in halves:
+                if zp == 0:
+                    ots[j] = opool.tile([P, Z, E], F32, name="ot")
+                ot = ots[j]
                 nc.vector.tensor_tensor(
-                    out=ot[:, 2 * zp : 2 * zp + 2, :], in0=obs[j, zp][:],
+                    out=ot[:, 2 * zp : 2 * zp + 2, :], in0=obs[j, zp][:].rearrange("p (z e) -> p z e", z=2),
                     in1=b2t[:].unsqueeze(1).to_broadcast([P, 2, E]), op=ALU.add,
                 )
-                if j == NU - 1:
-                    nc.sync.dma_start(out=dst[:, 2 * zp : 2 * zp + 2], in_=ot[:, 2 * zp : 2 * zp + 2, :])
-            if j < NU - 1:
-                nc.sync.dma_start(out=dst, in_=ot[:])
+                if split:
+                    nc.sync.dma_start(out=out_v[:, j, 2 * zp : 2 * zp + 2], in_=ot[:, 2 * zp : 2 * zp + 2, :])
+                elif zp == 1:
+                    nc.sync.dma_start(out=out_v[:, j], in_=ot[:])
 
+
+        scaled(nc.vector, nxc[:], xc[:], -1.0)
+        scaled(nc.vector, nxb[:], xb[:], -1.0)
+        scaled(nc.vector, nsc[:], sc[:], -1.0)
+        cb_bank = turn(7, [nxc, nxb])
         for q in range(4):
             widen(0, q, q < 2)
-        cbank = ptr.tile([P, 2, 2, P], F32, name="trb")
-        turn(cbank[:, 0], xc[:])
+        widen_s(1)
         gc = grp.tile([P, P, 4], BF16, name="gc", align_bytes=64)
-        nc.vector.tensor_copy(
-            out=gc[:].rearrange("p r e -> p (r e)").bitcast(F32).rearrange("p (z w u) -> p z w u", z=Z, u=2),
-            in_=cbank[:, 0].rearrange("p u (w z) -> p z w u", z=Z),
+        nc.scalar.copy(
+            out=words_of(gc[:]).rearrange("p (z w u) -> p z w u", z=Z, u=2),
+            in_=cb_bank[:, 0:256].rearrange("p (u w z) -> p z w u", u=2, z=Z),
         )
-        turn_a(0, 1)
-        ga0 = copy_a(1)
-        bbank = ptr.tile([P, 2, 2, P], F32, name="trb")
-        turn(bbank[:, 0], xb[:])
         gb = grp.tile([P, P, 4], BF16, name="gb", align_bytes=64)
         nc.scalar.copy(
-            out=gb[:].rearrange("p r e -> p (r e)").bitcast(F32).rearrange("p (r u) -> p r u", u=2),
-            in_=bbank[:, 0].rearrange("p u r -> p r u"),
+            out=words_of(gb[:]).rearrange("p (j z a u) -> p j z a u", z=Z, a=4, u=2),
+            in_=cb_bank[:, 256:512].rearrange("p (u z j a) -> p j z a u", u=2, z=Z, a=4),
         )
+        ga0 = copy_a(turn(6, [xa[0], xa[1]]), 2)
         nc.vector.tensor_copy(out=w1p[:], in_=w1raw[:].rearrange("p (m t) -> p t m", t=4))
-        nc.vector.quantize_mx(
-            out=cbc[:, 0:P].bitcast(FP8X4), scales=cbs[:, 0:P], in_=gc[:].rearrange("p r e -> p (r e)")
-        )
+        quant(cq[:], cqs[:], gc[:])
+        quant(bq[:], bqs[:], gb[:])
         nc.vector.tensor_copy(out=s1p[:], in_=s1raw[:].rearrange("p (m t) -> p t m", t=4))
-        nc.vector.quantize_mx(
-            out=cbc[:, P : 2 * P].bitcast(FP8X4), scales=cbs[:, P : 2 * P], in_=gb[:].rearrange("p r e -> p (r e)")
-        )
-        quant_a(ga0, 0, 1)
-
-        def spread_c(r0, r1):
-            nc.vector.tensor_copy(
-                out=crc[:, :, r0:r1, :],
-                in_=cbc[:, 0:P].rearrange("p (z w) -> p z w", z=Z).unsqueeze(2).to_broadcast([P, Z, r1 - r0, W]),
-            )
-            nc.vector.tensor_copy(
-                out=crs[:, :, r0:r1, :].bitcast(I32),
-                in_=cbs[:, 0:P].bitcast(I32).rearrange("p (z w) -> p z w", z=Z).unsqueeze(2).to_broadcast([P, Z, r1 - r0, W // 4]),
-            )
-
-        spread_c(0, 4)
-        for q in range(4):
-            widen(1, q, False)
-        def spread_b_scales():
-            late = cbs[:, P : 2 * P].rearrange("p (z h) -> p z h", z=Z)[:, :, 16:32]
-            for i in range(4):
-                nc.vector.tensor_copy(out=bsq[:, :, :, i], in_=late)
-            nc.vector.tensor_copy(
-                out=brs[:].rearrange("p z a w -> p (z a w)").bitcast(I32).rearrange("p (r w) -> p r w", w=W // 4),
-                in_=bsq[:].rearrange("p z a i -> p (z a i)").bitcast(I32).unsqueeze(2).to_broadcast([P, 16 * Z, W // 4]),
-            )
-
-        def spread_b(z):
-            nc.vector.tensor_copy(
-                out=brc[:, z],
-                in_=cbc[:, P + 32 * z + 16 : P + 32 * z + 32].unsqueeze(2).to_broadcast([P, 16, W]),
-            )
-
-        bb = pmm.tile([P, 4, P], F32, name="mmb")
+        spread_c()
+        quant_a(ga0, 0, 2)
+        scaled(nc.vector, nb1[:], b1t[:], -1.0)
+        widen_s(2)
+        widen_s(3)
+        bb = bank_tile(7)
         for t in range(4):
             nc.tensor.matmul_mx(
-                out=bb[:, t, :],
-                lhsT=w1p[:, t, :].bitcast(FP8X4), lhsT_scale=s1p[:, t, :],
-                rhs=cbc[:, P : 2 * P].bitcast(FP8X4), rhs_scale=cbs[:, P : 2 * P],
-                start=True, stop=True,
+                out=bb[:, P * t : P * (t + 1)], lhsT=w1p[:, t, :].bitcast(FP8X4), lhsT_scale=s1p[:, t, :],
+                rhs=bq[:].bitcast(FP8X4), rhs_scale=bqs[:], start=True, stop=True,
             )
         nc.vector.tensor_tensor(
-            out=bp[:].rearrange("p t z h -> p t (z h)"), in0=bb[:],
-            in1=b1f[:].unsqueeze(2).to_broadcast([P, 4, P]), op=ALU.add,
+            out=bp[:], in0=bb[:].rearrange("p (t r) -> p t r", t=4),
+            in1=nb1[:].unsqueeze(2).to_broadcast([P, 4, P]), op=ALU.add,
         )
-        for j in range(2, NU):
-            for q in range(4):
-                widen(j, q, False)
+        scaled(nc.gpsimd, gk[:], gt[:], 1.0 / KNEE)
+        scaled(nc.gpsimd, ng[:], gt[:], -1.0)
+        widen_s(4)
+        widen_s(5)
+        ring = [0, 1, 2, 3, 4, 5]
+        outs = [6, 7]
 
-        gas = {}
-        for j in range(4):
-            for z in range(Z):
-                bank = project(j, z)
-                add_b(j, z, bank)
-            if j == 0:
-                turn_a(1, 1)
-                quant_a(copy_a(1), 1, 1)
-            if j == 1:
-                spread_c(4, 16)
-            if j < 3:
-                turn_a(2 * j + 2, 2)
-                gas[j] = copy_a(2)
-            for half in range(2):
-                expo(j, half)
-            if j > 0:
-                quant_a(gas[j - 1], 2 * j, 2)
-            if j == 1:
-                spread_b_scales()
-                spread_b(0)
-            if j == 2:
-                spread_b(1)
-        y_project(0)
-        y_evacuate(0)
-        clip(0)
-        spread_b(2)
-        spread_b(3)
-        clip(1)
-        guard(0)
-        clip(2)
-        clip(3)
-        guard(1)
-        y_project(1)
-        y_evacuate(1)
-        y_guard(0)
-        clip(4)
-        y_guard(1)
-        clip(5)
-        y_project(2)
-        for j in range(6):
-            loga(j)
+        def first(j, t, with_knee):
+            bank = project(j, t, ring)
+            sigm(j, t, bank)
+            if with_knee:
+                knee(j, t, bank)
+            return bank
 
-        def step(k):
-            combine(k)
-            if k >= 2:
-                finish(k - 2)
-            if k >= 1:
-                quant_v(k - 1)
-                decode(k - 1)
-
-        for k in range(4):
-            step(k)
-        y_evacuate(2)
-        y_project(3)
-        y_evacuate(3)
-        step(4)
-        y_guard(2)
-        clip(6)
-        step(5)
-        y_guard(3)
-        clip(7)
-        loga(6)
-        loga(7)
-        step(6)
+        for j in range(2):
+            for t in range(4):
+                add_b(j, t, project2(j, t, ring))
+                if t % 2:
+                    sigm2(j, t - 1, t + 1)
+        bank23 = turn(6, [xa[2], xa[3]])
+        bank45 = turn(7, [xa[4], xa[5]])
+        spread_b_bytes()
+        ga2 = copy_a(bank23, 2, True)
+        spread_b_scales(2, 6)
+        spread_b(2, 2)
+        quant_a(ga2, 2, 2)
+        loga(0, 0, 2)
+        loga(0, 2, 4)
+        loga(1)
+        pre = {(j, t): project(j, t, ring) for j, t in [(2, 0), (2, 1), (2, 2), (2, 3), (3, 0), (3, 1)]}
+        ga4 = copy_a(bank45, 2, True)
+        for t in range(4):
+            knee2(0, t)
+        floor_l(0, 0, 2)
+        quant_a(ga4, 4, 2)
+        floor_l(0, 2, 4)
+        spread_b(4, 1)
+        combine(0)
+        for t in range(4):
+            knee2(1, t)
+        quant_v(0)
+        for jt in pre:
+            sigm(jt[0], jt[1], pre[jt])
+        for t in range(4):
+            knee(2, t, pre[2, t])
+        kept = {}
+        decode(0, outs)
+        for i, jt in enumerate([(3, 2), (3, 3), (4, 0), (4, 1), (4, 2), (4, 3)]):
+            kept[jt] = first(jt[0], jt[1], False)
+            if 1 <= i < 5:
+                widen(6 + (i - 1) // 2, 2 * ((i - 1) % 2), False)
+                widen(6 + (i - 1) // 2, 2 * ((i - 1) % 2) + 1, False)
+        floor_l(1, 0, 4)
+        combine(1)
+        finish(0)
+        quant_v(1)
+        bank67 = turn(6, [xa[6], xa[7]])
+        spread_b(5, 3)
+        ga6 = copy_a(bank67, 2, True)
+        decode(1, [7, 6])
+        finish(1, False, (0,))
+        quant_a(ga6, 6, 2)
+        finish(1, False, (1,))
+        loga(4, 0, 2)
+        loga(4, 2, 4)
+        loga(3, 2, 4)
+        loga(3, 0, 2)
+        loga(2)
+        for t in range(4):
+            lower(4, t, kept[4, t])
+        again = {(j, t): project(j, t, ring) for j, t in [(3, 0), (3, 1)]}
+        pre = {(j, t): project(j, t, ring) for j, t in [(5, 0), (5, 1)]}
+        for t in range(2, 4):
+            lower(3, t, kept[3, t])
+        pre.update({(j, t): project(j, t, ring) for j, t in [(5, 2), (5, 3)]})
+        for t in range(2):
+            lower(3, t, again[3, t])
+        pre.update({(j, t): project(j, t, ring) for j, t in [(6, 0), (6, 1)]})
+        combine(4)
+        for t in range(2):
+            gain(2, t)
+        quant_v(4)
+        decode(4, outs)
+        combine(3)
+        for jt in pre:
+            sigm(jt[0], jt[1], pre[jt])
+        kept = {}
+        for jt in [(6, 2), (6, 3), (7, 0), (7, 1), (7, 2), (7, 3)]:
+            kept[jt] = first(jt[0], jt[1], False)
+        for t in range(2, 4):
+            gain(2, t)
+        quant_v(3)
+        finish(4)
+        decode(3, outs)
+        combine(2)
+        quant_v(2)
+        finish(3)
+        decode(2, outs)
+        loga(7, 0, 2)
+        loga(7, 2, 4)
+        loga(6, 2, 4)
+        loga(6, 0, 2)
+        loga(5)
+        finish(2)
+        for t in range(4):
+            lower(7, t, kept[7, t])
+        again = {(j, t): project(j, t, ring) for j, t in [(6, 0), (6, 1), (5, 0), (5, 1)]}
+        for t in range(2, 4):
+            lower(6, t, kept[6, t])
+        again.update({(j, t): project(j, t, ring) for j, t in [(5, 2), (5, 3)]})
         combine(7)
-        quant_v(6)
-        decode(6)
-        finish(5)
+        for t in range(2):
+            lower(6, t, again[6, t])
         quant_v(7)
-        decode(7)
-        finish(6)
+        decode(7, outs)
+        lower(5, 0, again[5, 0])
+        combine(6)
+        for t in range(1, 4):
+            lower(5, t, again[5, t])
+        quant_v(6)
         finish(7)
+        decode(6, outs)
+        combine(5, 0, NV // 2)
+        finish(6, False, (0,))
+        quant_v(5, 0, NV // 2)
+        decode(5, outs, (0,))
+        combine(5, NV // 2, NV)
+        finish(6, False, (1,))
+        quant_v(5, NV // 2, NV)
+        decode(5, outs, (1,))
+        finish(5, True)

@@ -21,6 +21,7 @@ P = 128
 NU = 8
 NV = 512
 KNEE = 16.0
+CV = 256
 EPS = 2.0 ** -60
 WI = 4
 
@@ -33,6 +34,7 @@ def tile_tpvformersoftplusoccupancydecoder_d1p_kernel(
         keep = ctx.enter_context(tc.tile_pool(name="keep", bufs=1))
         grp = ctx.enter_context(tc.tile_pool(name="grp", bufs=2))
         vpool = ctx.enter_context(tc.tile_pool(name="vpool", bufs=3))
+        one = ctx.enter_context(tc.tile_pool(name="one", bufs=1))
         opool = ctx.enter_context(tc.tile_pool(name="opool", bufs=3))
         psum = ctx.enter_context(tc.psum_pool(name="psum", bufs=1))
         ctx.enter_context(tc.manual_schedule())
@@ -267,14 +269,14 @@ def tile_tpvformersoftplusoccupancydecoder_d1p_kernel(
 
         vts, vqs, obs = {}, {}, {}
 
-        def combine(j, c0=0, c1=NV):
-            if c0 == 0:
-                vts[j] = vpool.tile([P, NV, 4], BF16, name="vt", align_bytes=64)
+        def combine(j, c0=0, c1=NV, eng=nc.vector):
+            if j not in vts:
+                vts[j] = one.tile([P, NV, 4], BF16, name="vt", align_bytes=64)
             if j in big:
                 other = big[j][:, :, c0:c1].rearrange("p t (c i) -> p c t i", i=WI)
             else:
                 other = ng[:].unsqueeze(1).unsqueeze(3).to_broadcast([P, (c1 - c0) // WI, 4, WI])
-            nc.vector.tensor_tensor(
+            eng.tensor_tensor(
                 out=vts[j][:, c0:c1].rearrange("p (c i) t -> p c t i", i=WI),
                 in0=soft[j][:, :, c0:c1].rearrange("p t (c i) -> p c t i", i=WI),
                 in1=other,
@@ -418,67 +420,73 @@ def tile_tpvformersoftplusoccupancydecoder_d1p_kernel(
         spread_b(5, 3)
         ga6 = copy_a(bank67, 2, True)
         decode(1, [7, 6])
-        finish(1, False, (0,))
         quant_a(ga6, 6, 2)
-        finish(1, False, (1,))
         loga(4, 0, 2)
         loga(4, 2, 4)
         loga(3, 2, 4)
         loga(3, 0, 2)
         loga(2)
+        finish(1, False, (0,))
         for t in range(4):
             lower(4, t, kept[4, t])
+        combine(4, CV, NV, nc.gpsimd)
         again = {(j, t): project(j, t, ring) for j, t in [(3, 0), (3, 1)]}
         pre = {(j, t): project(j, t, ring) for j, t in [(5, 0), (5, 1)]}
         for t in range(2, 4):
             lower(3, t, kept[3, t])
         pre.update({(j, t): project(j, t, ring) for j, t in [(5, 2), (5, 3)]})
+        finish(1, False, (1,))
         for t in range(2):
             lower(3, t, again[3, t])
         pre.update({(j, t): project(j, t, ring) for j, t in [(6, 0), (6, 1)]})
-        combine(4)
-        for t in range(2):
-            gain(2, t)
+        combine(4, 0, CV)
+        gain(2, 0)
         quant_v(4)
         decode(4, outs)
+        for t in range(1, 4):
+            gain(2, t)
         combine(3)
         for jt in pre:
             sigm(jt[0], jt[1], pre[jt])
         kept = {}
         for jt in [(6, 2), (6, 3), (7, 0), (7, 1), (7, 2), (7, 3)]:
             kept[jt] = first(jt[0], jt[1], False)
-        for t in range(2, 4):
-            gain(2, t)
+        finish(4, False, (0,))
         quant_v(3)
-        finish(4)
+        finish(4, False, (1,))
         decode(3, outs)
         combine(2)
+        finish(3, False, (0,))
         quant_v(2)
-        finish(3)
+        finish(3, False, (1,))
         decode(2, outs)
         loga(7, 0, 2)
         loga(7, 2, 4)
         loga(6, 2, 4)
         loga(6, 0, 2)
-        loga(5)
-        finish(2)
+        loga(5, 0, 2)
+        loga(5, 2, 4)
+        finish(2, False, (0,))
         for t in range(4):
             lower(7, t, kept[7, t])
+        combine(7, CV, NV, nc.gpsimd)
         again = {(j, t): project(j, t, ring) for j, t in [(6, 0), (6, 1), (5, 0), (5, 1)]}
         for t in range(2, 4):
             lower(6, t, kept[6, t])
         again.update({(j, t): project(j, t, ring) for j, t in [(5, 2), (5, 3)]})
-        combine(7)
+        finish(2, False, (1,))
         for t in range(2):
             lower(6, t, again[6, t])
-        quant_v(7)
-        decode(7, outs)
+        combine(7, 0, CV)
         lower(5, 0, again[5, 0])
-        combine(6)
+        quant_v(7)
+        combine(6, CV, NV, nc.gpsimd)
+        decode(7, outs)
         for t in range(1, 4):
             lower(5, t, again[5, t])
-        quant_v(6)
         finish(7)
+        combine(6, 0, CV)
+        quant_v(6)
         decode(6, outs)
         combine(5, 0, NV // 2)
         finish(6, False, (0,))

@@ -1,4 +1,3 @@
-import math
 from contextlib import ExitStack
 
 import concourse.mybir as mybir
@@ -40,8 +39,8 @@ def tile_tpvformersoftplusoccupancydecoder_d1p_kernel(
         ctx.enter_context(tc.manual_schedule())
 
         ident = keep.tile([P, P], F32, name="ident")
-        byt0 = keep.tile([P, 2, D], U8, name="byt0")
-        byt1 = keep.tile([P, NU - 2, D], U8, name="byt1")
+        byt0 = keep.tile([P, 4, D], U8, name="byt0")
+        byt1 = keep.tile([P, NU - 4, D], U8, name="byt1")
         sc = keep.tile([P, NU, 4], F32, name="sc")
         nsc = keep.tile([P, NU, 4], F32, name="nsc")
         xa = [keep.tile([P, D], BF16, name="xa%d" % j, align_bytes=64) for j in range(NU)]
@@ -73,9 +72,10 @@ def tile_tpvformersoftplusoccupancydecoder_d1p_kernel(
         ac = keep.tile([P, NU * P], U32, name="ac", align_bytes=64)
         as_ = keep.tile([P, NU * P], U8, name="as_", align_bytes=64)
         bp = keep.tile([P, 4, P], F32, name="bp")
+        dg = keep.tile([P, 4, P], F32, name="dg")
         dum = keep.tile([P, 1], F32, name="dum")
         soft = [keep.tile([P, 4, NV], F32, name="soft%d" % j) for j in range(NU)]
-        big = {}
+        big, nsum = {}, {}
 
         bytes_v = thw_bytes.rearrange("(j a) w k -> (a w) j k", a=4)
         scale_v = thw_scale.rearrange("(j a) w q -> (a w) j q", a=4)
@@ -93,14 +93,14 @@ def tile_tpvformersoftplusoccupancydecoder_d1p_kernel(
 
         nc.sync.dma_start(out=xb[:], in_=tzh.rearrange("z h d -> (z h) d"))
         nc.scalar.dma_start(out=xc[:], in_=twz.rearrange("w z d -> (w z) d"))
-        nc.sync.dma_start(out=byt0[:], in_=bytes_v[:, 0:2, :])
+        nc.sync.dma_start(out=byt0[:], in_=bytes_v[:, 0:4, :])
         nc.scalar.dma_start(out=sc[:], in_=scale_v)
         nc.sync.dma_start(out=w1raw[:], in_=w1_words[0].rearrange("p n t -> p (n t)").bitcast(I32))
         for q in range(4):
             load_rows(s1raw, w1_scales, q, nc.sync)
         nc.scalar.activation(out=dum[:], in_=dum[:], func=AF.Sigmoid)
         nc.sync.dma_start(out=b1t[:], in_=b1.rearrange("(p t) -> p t", t=4))
-        nc.sync.dma_start(out=byt1[:], in_=bytes_v[:, 2:NU, :])
+        nc.sync.dma_start(out=byt1[:], in_=bytes_v[:, 4:NU, :])
         nc.sync.dma_start(out=gt[:], in_=g.rearrange("(p t) -> p t", t=4))
         make_identity(nc, ident[:])
         nc.sync.dma_start(out=w2w[:], in_=w2_words[0].rearrange("p n t -> p (n t)").bitcast(I32))
@@ -116,7 +116,7 @@ def tile_tpvformersoftplusoccupancydecoder_d1p_kernel(
 
         def widen(j, q, vec):
             cols = slice(128 * q, 128 * q + 128)
-            src = (byt0[:, j, cols] if j < 2 else byt1[:, j - 2, cols]).bitcast(FP8)
+            src = (byt0[:, j, cols] if j < 4 else byt1[:, j - 4, cols]).bitcast(FP8)
             s = nsc[:, j, q : q + 1]
             if vec:
                 nc.vector.tensor_scalar(out=xa[j][:, cols], in0=src, scalar1=s, scalar2=None, op0=ALU.mult)
@@ -183,11 +183,20 @@ def tile_tpvformersoftplusoccupancydecoder_d1p_kernel(
                 in_=bq[:, rows].unsqueeze(2).to_broadcast([P, 16 * count, W]),
             )
 
-        turnof = {"next": 0}
 
-        def project(j, t, ring):
-            bank = bank_tile(ring[turnof["next"] % len(ring)])
-            turnof.update({"next": turnof["next"] + 1})
+        free = [0, 1, 2, 3, 4, 5]
+        held = {}
+
+        def take(key):
+            k = free.pop(0)
+            held[key] = (bank_tile(k), k)
+            return held[key][0]
+
+        def release(key):
+            free.append(held.pop(key)[1])
+
+        def project(j, t):
+            bank = take((j, t))
             lhs, lhs_s = w1p[:, t, :].bitcast(FP8X4), s1p[:, t, :]
             ucols = slice(NV * j, NV * (j + 1))
             acols = slice(P * j, P * (j + 1))
@@ -200,9 +209,8 @@ def tile_tpvformersoftplusoccupancydecoder_d1p_kernel(
             nc.tensor.matmul_mx(out=bank[:], lhsT=lhs, lhsT_scale=lhs_s, rhs=brc[:, ucols].bitcast(FP8X4), rhs_scale=brs[:, ucols], start=False, stop=True)
             return bank
 
-        def project2(j, t, ring):
-            bank = bank_tile(ring[turnof["next"] % len(ring)])
-            turnof.update({"next": turnof["next"] + 1})
+        def project2(j, t):
+            bank = take((j, t))
             lhs, lhs_s = w1p[:, t, :].bitcast(FP8X4), s1p[:, t, :]
             acols = slice(P * j, P * (j + 1))
             nc.tensor.matmul_mx(out=bank[:], lhsT=lhs, lhsT_scale=lhs_s, rhs=crc[:].bitcast(FP8X4), rhs_scale=crs[:], start=True, stop=False)
@@ -213,35 +221,37 @@ def tile_tpvformersoftplusoccupancydecoder_d1p_kernel(
                 )
             return bank
 
-        def add_b(j, t, bank):
+        def add_b(j, t):
+            bank = held[j, t][0]
             if t == 0:
-                big[j] = keep.tile([P, 4, NV], F32, name="big%d" % j)
+                nsum[j] = keep.tile([P, 4, NV], F32, name="nsum%d" % j)
             nc.vector.tensor_tensor(
-                out=big[j][:, t, :].rearrange("p (r w) -> p r w", w=W),
+                out=nsum[j][:, t, :].rearrange("p (r w) -> p r w", w=W),
                 in0=bank[:].rearrange("p (r w) -> p r w", w=W),
                 in1=bp[:, t, 16 * j : 16 * j + 16].unsqueeze(2).to_broadcast([P, 16, W]),
                 op=ALU.add,
             )
+            release((j, t))
 
         def sigm2(j, t0, t1):
             nc.scalar.activation(
                 out=soft[j][:, t0:t1, :].rearrange("p t n -> p (t n)"),
-                in_=big[j][:, t0:t1, :].rearrange("p t n -> p (t n)"), func=AF.Sigmoid,
+                in_=nsum[j][:, t0:t1, :].rearrange("p t n -> p (t n)"), func=AF.Sigmoid,
             )
 
-        def knee2(j, t):
-            e = big[j][:, t, :]
-            nc.vector.tensor_scalar(out=e, in0=e, scalar1=-KNEE, scalar2=gk[:, t : t + 1], op0=ALU.min, op1=ALU.mult)
+        def sigm(j, t, last=False):
+            nc.scalar.activation(out=soft[j][:, t, :], in_=held[j, t][0][:], func=AF.Sigmoid, bias=nb1[:, t : t + 1])
+            if last:
+                release((j, t))
 
-        def sigm(j, t, bank):
-            nc.scalar.activation(out=soft[j][:, t, :], in_=bank[:], func=AF.Sigmoid, bias=nb1[:, t : t + 1])
-
-        def knee(j, t, bank):
+        def knee(j, t):
+            bank = held[j, t][0]
             if t == 0:
                 big[j] = keep.tile([P, 4, NV], F32, name="big%d" % j)
             nc.vector.tensor_scalar(
                 out=big[j][:, t, :], in0=bank[:], scalar1=nb1[:, t : t + 1], scalar2=-KNEE, op0=ALU.add, op1=ALU.min
             )
+            release((j, t))
 
         def loga(j, t0=0, t1=4):
             e = soft[j][:, t0:t1, :].rearrange("p t n -> p (t n)")
@@ -251,21 +261,11 @@ def tile_tpvformersoftplusoccupancydecoder_d1p_kernel(
             e = soft[j][:, t, :]
             nc.vector.tensor_scalar(out=e, in0=e, scalar1=-KNEE, scalar2=gk[:, t : t + 1], op0=ALU.max, op1=ALU.mult)
 
-        def floor_s(j, t0, t1):
-            e = soft[j][:, t0:t1, :].rearrange("p t n -> p (t n)")
-            nc.vector.tensor_scalar(out=e, in0=e, scalar1=math.exp(-KNEE), scalar2=None, op0=ALU.max)
-
-        def floor_l(j, t0, t1):
-            e = soft[j][:, t0:t1, :].rearrange("p t n -> p (t n)")
-            nc.vector.tensor_scalar(out=e, in0=e, scalar1=-KNEE, scalar2=None, op0=ALU.max)
-
-        def gain_big(j, t):
-            e = big[j][:, t, :]
-            nc.vector.tensor_scalar(out=e, in0=e, scalar1=gk[:, t : t + 1], scalar2=None, op0=ALU.mult)
-
-        def lower(j, t, bank):
+        def lower(j, t):
+            bank = held[j, t][0]
             e = soft[j][:, t, :]
             nc.vector.scalar_tensor_tensor(out=e, in0=bank[:], scalar=nb1[:, t : t + 1], in1=e, op0=ALU.add, op1=ALU.min)
+            release((j, t))
 
         vts, vqs, obs = {}, {}, {}
 
@@ -282,6 +282,37 @@ def tile_tpvformersoftplusoccupancydecoder_d1p_kernel(
                 in1=other,
                 op=ALU.mult,
             )
+
+        def combine_g(j, c0, c1):
+            if j not in vts:
+                vts[j] = one.tile([P, NV, 4], BF16, name="vt", align_bytes=64)
+            if j in big:
+                other = big[j][:, :, c0:c1].rearrange("p t n -> p n t")
+            else:
+                other = ng[:].unsqueeze(1).to_broadcast([P, c1 - c0, 4])
+            nc.gpsimd.tensor_tensor(
+                out=vts[j][:, c0:c1], in0=soft[j][:, :, c0:c1].rearrange("p t n -> p n t"), in1=other, op=ALU.mult
+            )
+
+        def gain_pe(j, q):
+            bank = take((j, "g", q))
+            for t in range(4):
+                nc.tensor.matmul(
+                    out=bank[:, P * t : P * (t + 1)], lhsT=dg[:, t, :], rhs=soft[j][:, t, P * q : P * (q + 1)],
+                    start=True, stop=True,
+                )
+            return bank
+
+        def weave(j, q):
+            bank = held[j, "g", q][0]
+            if j not in vts:
+                vts[j] = vpool.tile([P, NV, 4], BF16, name="vw", align_bytes=64)
+            nc.scalar.copy(out=vts[j][:, P * q : P * (q + 1)], in_=bank[:].rearrange("p (t n) -> p n t", t=4))
+            release((j, "g", q))
+
+        def lower2(j, t0=0, t1=4):
+            e = soft[j][:, t0:t1].rearrange("p t n -> p (t n)")
+            nc.vector.tensor_tensor(out=e, in0=e, in1=nsum[j][:, t0:t1].rearrange("p t n -> p (t n)"), op=ALU.min)
 
         def quant_v(j, c0=0, c1=NV):
             if c0 == 0:
@@ -329,7 +360,8 @@ def tile_tpvformersoftplusoccupancydecoder_d1p_kernel(
         cb_bank = turn(7, [nxc, nxb])
         for q in range(4):
             widen(0, q, q < 2)
-        widen_s(1)
+        for q in range(4):
+            widen(1, q, True)
         gc = grp.tile([P, P, 4], BF16, name="gc", align_bytes=64)
         nc.scalar.copy(
             out=words_of(gc[:]).rearrange("p (z w u) -> p z w u", z=Z, u=2),
@@ -342,13 +374,14 @@ def tile_tpvformersoftplusoccupancydecoder_d1p_kernel(
         )
         ga0 = copy_a(turn(6, [xa[0], xa[1]]), 2)
         nc.vector.tensor_copy(out=w1p[:], in_=w1raw[:].rearrange("p (m t) -> p t m", t=4))
+        for q in range(4):
+            widen(2, q, True)
         quant(cq[:], cqs[:], gc[:])
         quant(bq[:], bqs[:], gb[:])
         nc.vector.tensor_copy(out=s1p[:], in_=s1raw[:].rearrange("p (m t) -> p t m", t=4))
         spread_c()
         quant_a(ga0, 0, 2)
         scaled(nc.vector, nb1[:], b1t[:], -1.0)
-        widen_s(2)
         widen_s(3)
         bb = bank_tile(7)
         for t in range(4):
@@ -362,21 +395,19 @@ def tile_tpvformersoftplusoccupancydecoder_d1p_kernel(
         )
         scaled(nc.gpsimd, gk[:], gt[:], 1.0 / KNEE)
         scaled(nc.gpsimd, ng[:], gt[:], -1.0)
+        for t in range(4):
+            scaled(nc.gpsimd, dg[:, t, :], ident[:], ng[:, t : t + 1])
         widen_s(4)
         widen_s(5)
-        ring = [0, 1, 2, 3, 4, 5]
+        widen_s(6)
+        widen_s(7)
         outs = [6, 7]
 
-        def first(j, t, with_knee):
-            bank = project(j, t, ring)
-            sigm(j, t, bank)
-            if with_knee:
-                knee(j, t, bank)
-            return bank
 
         for j in range(2):
             for t in range(4):
-                add_b(j, t, project2(j, t, ring))
+                project2(j, t)
+                add_b(j, t)
                 if t % 2:
                     sigm2(j, t - 1, t + 1)
         bank23 = turn(6, [xa[2], xa[3]])
@@ -386,41 +417,38 @@ def tile_tpvformersoftplusoccupancydecoder_d1p_kernel(
         spread_b_scales(2, 6)
         spread_b(2, 2)
         quant_a(ga2, 2, 2)
+        bank67 = turn(6, [xa[6], xa[7]])
         loga(0, 0, 2)
         loga(0, 2, 4)
         loga(1)
-        pre = {(j, t): project(j, t, ring) for j, t in [(2, 0), (2, 1), (2, 2), (2, 3), (3, 0), (3, 1)]}
+        early = [(2, 0), (2, 1), (2, 2), (2, 3), (3, 0), (3, 1)]
+        for j, t in early:
+            project(j, t)
         ga4 = copy_a(bank45, 2, True)
-        for t in range(4):
-            knee2(0, t)
-        floor_l(0, 0, 2)
+        spread_b(4, 2)
         quant_a(ga4, 4, 2)
-        floor_l(0, 2, 4)
-        spread_b(4, 1)
-        combine(0)
-        for t in range(4):
-            knee2(1, t)
-        quant_v(0)
-        for jt in pre:
-            sigm(jt[0], jt[1], pre[jt])
-        for t in range(4):
-            knee(2, t, pre[2, t])
-        kept = {}
-        decode(0, outs)
-        for i, jt in enumerate([(3, 2), (3, 3), (4, 0), (4, 1), (4, 2), (4, 3)]):
-            kept[jt] = first(jt[0], jt[1], False)
-            if 1 <= i < 5:
-                widen(6 + (i - 1) // 2, 2 * ((i - 1) % 2), False)
-                widen(6 + (i - 1) // 2, 2 * ((i - 1) % 2) + 1, False)
-        floor_l(1, 0, 4)
-        combine(1)
-        finish(0)
-        quant_v(1)
-        bank67 = turn(6, [xa[6], xa[7]])
-        spread_b(5, 3)
         ga6 = copy_a(bank67, 2, True)
-        decode(1, [7, 6])
+        lower2(0, 0, 2)
         quant_a(ga6, 6, 2)
+        lower2(0, 2, 4)
+        lower2(1)
+        combine_g(0, CV, NV)
+        for j, t in early:
+            sigm(j, t, j == 3)
+            if j == 2:
+                knee(j, t)
+        for j, t in [(3, 2), (3, 3), (4, 0), (4, 1), (4, 2), (4, 3)]:
+            project(j, t)
+            sigm(j, t)
+        combine(0, 0, CV)
+        spread_b(6, 1)
+        quant_v(0)
+        decode(0, outs)
+        combine(1)
+        spread_b(7, 1)
+        quant_v(1)
+        finish(0)
+        decode(1, outs)
         loga(4, 0, 2)
         loga(4, 2, 4)
         loga(3, 2, 4)
@@ -428,32 +456,36 @@ def tile_tpvformersoftplusoccupancydecoder_d1p_kernel(
         loga(2)
         finish(1, False, (0,))
         for t in range(4):
-            lower(4, t, kept[4, t])
-        combine(4, CV, NV, nc.gpsimd)
-        again = {(j, t): project(j, t, ring) for j, t in [(3, 0), (3, 1)]}
-        pre = {(j, t): project(j, t, ring) for j, t in [(5, 0), (5, 1)]}
+            lower(4, t)
+        combine_g(4, CV, NV)
+        for j, t in [(3, 0), (3, 1), (5, 0), (5, 1)]:
+            project(j, t)
         for t in range(2, 4):
-            lower(3, t, kept[3, t])
-        pre.update({(j, t): project(j, t, ring) for j, t in [(5, 2), (5, 3)]})
+            lower(3, t)
+        project(5, 2)
+        project(5, 3)
         finish(1, False, (1,))
         for t in range(2):
-            lower(3, t, again[3, t])
-        pre.update({(j, t): project(j, t, ring) for j, t in [(6, 0), (6, 1)]})
+            lower(3, t)
+        project(6, 0)
+        project(6, 1)
         combine(4, 0, CV)
         gain(2, 0)
         quant_v(4)
         decode(4, outs)
+        combine_g(3, CV, NV)
+        for j, t in [(5, 0), (5, 1), (5, 2), (5, 3), (6, 0), (6, 1)]:
+            sigm(j, t, j == 6)
+            if j == 5:
+                knee(j, t)
+        for j, t in [(6, 2), (6, 3), (7, 0), (7, 1), (7, 2), (7, 3)]:
+            project(j, t)
+            sigm(j, t)
+        finish(4)
+        combine(3, 0, CV)
         for t in range(1, 4):
             gain(2, t)
-        combine(3)
-        for jt in pre:
-            sigm(jt[0], jt[1], pre[jt])
-        kept = {}
-        for jt in [(6, 2), (6, 3), (7, 0), (7, 1), (7, 2), (7, 3)]:
-            kept[jt] = first(jt[0], jt[1], False)
-        finish(4, False, (0,))
         quant_v(3)
-        finish(4, False, (1,))
         decode(3, outs)
         combine(2)
         finish(3, False, (0,))
@@ -462,38 +494,41 @@ def tile_tpvformersoftplusoccupancydecoder_d1p_kernel(
         decode(2, outs)
         loga(7, 0, 2)
         loga(7, 2, 4)
+        loga(5)
         loga(6, 2, 4)
         loga(6, 0, 2)
-        loga(5, 0, 2)
-        loga(5, 2, 4)
-        finish(2, False, (0,))
         for t in range(4):
-            lower(7, t, kept[7, t])
-        combine(7, CV, NV, nc.gpsimd)
-        again = {(j, t): project(j, t, ring) for j, t in [(6, 0), (6, 1), (5, 0), (5, 1)]}
+            lower(7, t)
+        project(6, 0)
+        project(6, 1)
+        gain_pe(7, 0)
+        gain_pe(7, 1)
+        for t in range(4):
+            gain(5, t)
+        combine_g(5, CV, NV)
         for t in range(2, 4):
-            lower(6, t, kept[6, t])
-        again.update({(j, t): project(j, t, ring) for j, t in [(5, 2), (5, 3)]})
-        finish(2, False, (1,))
+            lower(6, t)
+        gain_pe(7, 2)
+        gain_pe(7, 3)
         for t in range(2):
-            lower(6, t, again[6, t])
-        combine(7, 0, CV)
-        lower(5, 0, again[5, 0])
+            lower(6, t)
+        finish(2)
+        gain_pe(6, 0)
+        gain_pe(6, 1)
+        for q in range(4):
+            weave(7, q)
+        combine(5, 0, CV)
         quant_v(7)
-        combine(6, CV, NV, nc.gpsimd)
+        gain_pe(6, 2)
         decode(7, outs)
-        for t in range(1, 4):
-            lower(5, t, again[5, t])
+        gain_pe(6, 3)
+        quant_v(5)
+        decode(5, [free[0], free[1]])
+        for q in range(4):
+            weave(6, q)
         finish(7)
-        combine(6, 0, CV)
+        finish(5, False, (0,))
         quant_v(6)
         decode(6, outs)
-        combine(5, 0, NV // 2)
-        finish(6, False, (0,))
-        quant_v(5, 0, NV // 2)
-        decode(5, outs, (0,))
-        combine(5, NV // 2, NV)
-        finish(6, False, (1,))
-        quant_v(5, NV // 2, NV)
-        decode(5, outs, (1,))
-        finish(5, True)
+        finish(5, False, (1,))
+        finish(6, True)

@@ -71,7 +71,7 @@ def tile_tpvformersoftplusoccupancydecoder_d1p_kernel(
         bs4 = keep.tile([P, P, 4], U8, name="bs4", align_bytes=64)
         ac = keep.tile([P, NU * P], U32, name="ac", align_bytes=64)
         as_ = keep.tile([P, NU * P], U8, name="as_", align_bytes=64)
-        bp = keep.tile([P, 4, P], F32, name="bp")
+        bp = keep.tile([P, 4, 32], F32, name="bp")
         dg = keep.tile([P, 4, P], F32, name="dg")
         dum = keep.tile([P, 1], F32, name="dum")
         soft = [keep.tile([P, 4, NV], F32, name="soft%d" % j) for j in range(NU)]
@@ -91,8 +91,8 @@ def tile_tpvformersoftplusoccupancydecoder_d1p_kernel(
                 in_=scales[0, 4 * q : 4 * q + 4, :].bitcast(I32),
             )
 
-        nc.sync.dma_start(out=xb[:], in_=tzh.rearrange("z h d -> (z h) d"))
-        nc.scalar.dma_start(out=xc[:], in_=twz.rearrange("w z d -> (w z) d"))
+        nc.sync.dma_start(out=xc[:], in_=twz.rearrange("w z d -> (w z) d"))
+        nc.scalar.dma_start(out=xb[:], in_=tzh.rearrange("z h d -> (z h) d"))
         nc.sync.dma_start(out=byt0[:], in_=bytes_v[:, 0:4, :])
         nc.scalar.dma_start(out=sc[:], in_=scale_v)
         nc.sync.dma_start(out=w1raw[:], in_=w1_words[0].rearrange("p n t -> p (n t)").bitcast(I32))
@@ -111,8 +111,16 @@ def tile_tpvformersoftplusoccupancydecoder_d1p_kernel(
         def scaled(eng, dst, src, factor):
             eng.tensor_scalar(out=dst, in0=src, scalar1=factor, scalar2=0.0, op0=ALU.mult, op1=ALU.add)
 
-        def bank_tile(k):
-            return psum.tile([P, NV], F32, name="bank%d" % k)
+        free = list(range(8))
+        held = {}
+
+        def take(key):
+            k = free.pop(0)
+            held[key] = (psum.tile([P, NV], F32, name="bank%d" % k), k)
+            return held[key][0]
+
+        def release(key):
+            free.append(held.pop(key)[1])
 
         def widen(j, q, vec):
             cols = slice(128 * q, 128 * q + 128)
@@ -123,12 +131,16 @@ def tile_tpvformersoftplusoccupancydecoder_d1p_kernel(
             else:
                 nc.scalar.activation(out=xa[j][:, cols], in_=src, func=AF.Copy, scale=s)
 
+        def widen_v(j):
+            for q in range(4):
+                widen(j, q, True)
+
         def widen_s(j):
             for q in range(4):
                 widen(j, q, False)
 
-        def turn(k, srcs):
-            bank = bank_tile(k)
+        def turn(key, srcs):
+            bank = take(key)
             for s, src in enumerate(srcs):
                 words = src[:].bitcast(F32)
                 for u in range(2):
@@ -138,12 +150,14 @@ def tile_tpvformersoftplusoccupancydecoder_d1p_kernel(
         def words_of(tile):
             return tile.rearrange("p r e -> p (r e)").bitcast(F32)
 
-        def copy_a(bank, count, vec=False):
+        def copy_a(first, count, vec=False):
+            bank = held["a", first][0]
             ga = grp.tile([P, 2 * P, 4], BF16, name="ga", align_bytes=64)
             (nc.vector.tensor_copy if vec else nc.scalar.copy)(
                 out=words_of(ga[:, 0 : count * P]).rearrange("p (s r u) -> p s r u", s=count, u=2),
                 in_=bank[:, 0 : count * 256].rearrange("p (s u r) -> p s r u", s=count, u=2),
             )
+            release(("a", first))
             return ga
 
         def quant(codes, scales, grouped):
@@ -165,7 +179,7 @@ def tile_tpvformersoftplusoccupancydecoder_d1p_kernel(
 
         def spread_b_bytes():
             for i in range(4):
-                nc.vector.tensor_copy(out=bs4[:, :, i], in_=bqs[:])
+                nc.gpsimd.tensor_copy(out=bs4[:, 32:P, i], in_=bqs[:, 32:P])
 
         def spread_b_scales(first, count):
             rows = slice(16 * first, 16 * (first + count))
@@ -183,17 +197,6 @@ def tile_tpvformersoftplusoccupancydecoder_d1p_kernel(
                 in_=bq[:, rows].unsqueeze(2).to_broadcast([P, 16 * count, W]),
             )
 
-
-        free = [0, 1, 2, 3, 4, 5]
-        held = {}
-
-        def take(key):
-            k = free.pop(0)
-            held[key] = (bank_tile(k), k)
-            return held[key][0]
-
-        def release(key):
-            free.append(held.pop(key)[1])
 
         def project(j, t):
             bank = take((j, t))
@@ -267,11 +270,12 @@ def tile_tpvformersoftplusoccupancydecoder_d1p_kernel(
             nc.vector.scalar_tensor_tensor(out=e, in0=bank[:], scalar=nb1[:, t : t + 1], in1=e, op0=ALU.add, op1=ALU.min)
             release((j, t))
 
-        vts, vqs, obs = {}, {}, {}
+        vts, vqs = {}, {}
+
+        def product_tile(j, name):
+            vts[j] = one.tile([P, NV, 4], BF16, name=name, align_bytes=64)
 
         def combine(j, c0=0, c1=NV, eng=nc.vector):
-            if j not in vts:
-                vts[j] = one.tile([P, NV, 4], BF16, name="vt", align_bytes=64)
             if j in big:
                 other = big[j][:, :, c0:c1].rearrange("p t (c i) -> p c t i", i=WI)
             else:
@@ -284,8 +288,6 @@ def tile_tpvformersoftplusoccupancydecoder_d1p_kernel(
             )
 
         def combine_g(j, c0, c1):
-            if j not in vts:
-                vts[j] = one.tile([P, NV, 4], BF16, name="vt", align_bytes=64)
             if j in big:
                 other = big[j][:, :, c0:c1].rearrange("p t n -> p n t")
             else:
@@ -322,10 +324,10 @@ def tile_tpvformersoftplusoccupancydecoder_d1p_kernel(
             vc, vs = vqs[j]
             quant(vc[:, c0:c1], vs[:, c0:c1], vts[j][:, c0:c1])
 
-        def decode(j, ring, halves=(0, 1)):
+        def decode(j, halves=(0, 1)):
             vc, vs = vqs[j]
             for zp in halves:
-                ob = bank_tile(ring[zp])
+                ob = take((j, "o", zp))
                 for zz in range(2):
                     cols = slice(P * (2 * zp + zz), P * (2 * zp + zz + 1))
                     nc.tensor.matmul_mx(
@@ -334,7 +336,6 @@ def tile_tpvformersoftplusoccupancydecoder_d1p_kernel(
                         rhs=w2w[:].bitcast(FP8X4), rhs_scale=s2w[:],
                         start=True, stop=True,
                     )
-                obs[j, zp] = ob
 
         out_v = out.rearrange("(j a) w z e -> (a w) j z e", a=4)
         ots = {}
@@ -345,9 +346,10 @@ def tile_tpvformersoftplusoccupancydecoder_d1p_kernel(
                     ots[j] = opool.tile([P, Z, E], F32, name="ot")
                 ot = ots[j]
                 nc.vector.tensor_tensor(
-                    out=ot[:, 2 * zp : 2 * zp + 2, :], in0=obs[j, zp][:].rearrange("p (z e) -> p z e", z=2),
+                    out=ot[:, 2 * zp : 2 * zp + 2, :], in0=held[j, "o", zp][0][:].rearrange("p (z e) -> p z e", z=2),
                     in1=b2t[:].unsqueeze(1).to_broadcast([P, 2, E]), op=ALU.add,
                 )
+                release((j, "o", zp))
                 if split:
                     nc.sync.dma_start(out=out_v[:, j, 2 * zp : 2 * zp + 2], in_=ot[:, 2 * zp : 2 * zp + 2, :])
                 elif zp == 1:
@@ -357,178 +359,192 @@ def tile_tpvformersoftplusoccupancydecoder_d1p_kernel(
         scaled(nc.vector, nxc[:], xc[:], -1.0)
         scaled(nc.vector, nxb[:], xb[:], -1.0)
         scaled(nc.vector, nsc[:], sc[:], -1.0)
-        cb_bank = turn(7, [nxc, nxb])
+        c_bank = turn("c", [nxc])
+        b_bank = turn("b", [nxb])
         for q in range(4):
             widen(0, q, q < 2)
-        for q in range(4):
-            widen(1, q, True)
         gc = grp.tile([P, P, 4], BF16, name="gc", align_bytes=64)
         nc.scalar.copy(
             out=words_of(gc[:]).rearrange("p (z w u) -> p z w u", z=Z, u=2),
-            in_=cb_bank[:, 0:256].rearrange("p (u w z) -> p z w u", u=2, z=Z),
+            in_=c_bank[:, 0:256].rearrange("p (u w z) -> p z w u", u=2, z=Z),
         )
+        release("c")
         gb = grp.tile([P, P, 4], BF16, name="gb", align_bytes=64)
         nc.scalar.copy(
             out=words_of(gb[:]).rearrange("p (j z a u) -> p j z a u", z=Z, a=4, u=2),
-            in_=cb_bank[:, 256:512].rearrange("p (u z j a) -> p j z a u", u=2, z=Z, a=4),
+            in_=b_bank[:, 0:256].rearrange("p (u z j a) -> p j z a u", u=2, z=Z, a=4),
         )
-        ga0 = copy_a(turn(6, [xa[0], xa[1]]), 2)
-        nc.vector.tensor_copy(out=w1p[:], in_=w1raw[:].rearrange("p (m t) -> p t m", t=4))
-        for q in range(4):
-            widen(2, q, True)
+        release("b")
+        widen_v(1)
+        turn(("a", 0), [xa[0]])
+        ga0 = copy_a(0, 1)
+        turn(("a", 1), [xa[1]])
+        ga1 = copy_a(1, 1)
         quant(cq[:], cqs[:], gc[:])
+        nc.vector.tensor_copy(out=w1p[:], in_=w1raw[:].rearrange("p (m t) -> p t m", t=4))
         quant(bq[:], bqs[:], gb[:])
         nc.vector.tensor_copy(out=s1p[:], in_=s1raw[:].rearrange("p (m t) -> p t m", t=4))
         spread_c()
-        quant_a(ga0, 0, 2)
+        quant_a(ga0, 0, 1)
         scaled(nc.vector, nb1[:], b1t[:], -1.0)
+        widen_s(2)
         widen_s(3)
-        bb = bank_tile(7)
+        bb = take("bb")
         for t in range(4):
             nc.tensor.matmul_mx(
-                out=bb[:, P * t : P * (t + 1)], lhsT=w1p[:, t, :].bitcast(FP8X4), lhsT_scale=s1p[:, t, :],
-                rhs=bq[:].bitcast(FP8X4), rhs_scale=bqs[:], start=True, stop=True,
+                out=bb[:, 64 * t : 64 * (t + 1)], lhsT=w1p[:, t, :].bitcast(FP8X4), lhsT_scale=s1p[:, t, :],
+                rhs=bq[:, 0:64].bitcast(FP8X4), rhs_scale=bqs[:, 0:64], start=True, stop=True,
             )
+        quant_a(ga1, 1, 1)
         nc.vector.tensor_tensor(
-            out=bp[:], in0=bb[:].rearrange("p (t r) -> p t r", t=4),
-            in1=nb1[:].unsqueeze(2).to_broadcast([P, 4, P]), op=ALU.add,
+            out=bp[:], in0=bb[:, 0:256].rearrange("p (t r) -> p t r", t=4)[:, :, 0:32],
+            in1=nb1[:].unsqueeze(2).to_broadcast([P, 4, 32]), op=ALU.add,
         )
-        scaled(nc.gpsimd, gk[:], gt[:], 1.0 / KNEE)
-        scaled(nc.gpsimd, ng[:], gt[:], -1.0)
-        for t in range(4):
-            scaled(nc.gpsimd, dg[:, t, :], ident[:], ng[:, t : t + 1])
+        release("bb")
         widen_s(4)
         widen_s(5)
-        widen_s(6)
-        widen_s(7)
-        outs = [6, 7]
-
-
         for j in range(2):
             for t in range(4):
                 project2(j, t)
                 add_b(j, t)
+                if (j, t) == (0, 0):
+                    spread_b_bytes()
                 if t % 2:
                     sigm2(j, t - 1, t + 1)
-        bank23 = turn(6, [xa[2], xa[3]])
-        bank45 = turn(7, [xa[4], xa[5]])
-        spread_b_bytes()
-        ga2 = copy_a(bank23, 2, True)
+        scaled(nc.gpsimd, gk[:], gt[:], 1.0 / KNEE)
+        scaled(nc.gpsimd, ng[:], gt[:], -1.0)
+        nc.gpsimd.tensor_tensor(
+            out=dg[:], in0=ident[:].unsqueeze(1).to_broadcast([P, 4, P]),
+            in1=ng[:].unsqueeze(2).to_broadcast([P, 4, P]), op=ALU.mult,
+        )
+        turn(("a", 2), [xa[2], xa[3]])
+        turn(("a", 4), [xa[4], xa[5]])
+        ga2 = copy_a(2, 2, True)
         spread_b_scales(2, 6)
-        spread_b(2, 2)
         quant_a(ga2, 2, 2)
-        bank67 = turn(6, [xa[6], xa[7]])
+        spread_b(2, 2)
         loga(0, 0, 2)
         loga(0, 2, 4)
         loga(1)
-        early = [(2, 0), (2, 1), (2, 2), (2, 3), (3, 0), (3, 1)]
-        for j, t in early:
-            project(j, t)
-        ga4 = copy_a(bank45, 2, True)
-        spread_b(4, 2)
+        widen_v(6)
+        widen_v(7)
+        project(2, 0)
+        project(2, 1)
+        turn(("a", 6), [xa[6], xa[7]])
+        ga4 = copy_a(4, 2, True)
+        spread_b(4, 1)
         quant_a(ga4, 4, 2)
-        ga6 = copy_a(bank67, 2, True)
         lower2(0, 0, 2)
-        quant_a(ga6, 6, 2)
-        lower2(0, 2, 4)
-        lower2(1)
-        combine_g(0, CV, NV)
-        for j, t in early:
-            sigm(j, t, j == 3)
-            if j == 2:
-                knee(j, t)
-        for j, t in [(3, 2), (3, 3), (4, 0), (4, 1), (4, 2), (4, 3)]:
+        ga6 = copy_a(6, 2, True)
+        for j, t in [(2, 2), (2, 3), (3, 0), (3, 1), (3, 2), (3, 3)]:
             project(j, t)
-            sigm(j, t)
+        lower2(0, 2, 4)
+        quant_a(ga6, 6, 2)
+        spread_b(5, 1)
+        lower2(1)
+        product_tile(0, "vta")
+        combine_g(0, CV, NV)
+        for t in range(4):
+            sigm(2, t)
+            knee(2, t)
+        for t in range(4):
+            project(4, t)
+        for j in (3, 4):
+            for t in range(4):
+                sigm(j, t)
+        spread_b(6, 2)
         combine(0, 0, CV)
-        spread_b(6, 1)
-        quant_v(0)
-        decode(0, outs)
+        product_tile(1, "vtb")
         combine(1)
-        spread_b(7, 1)
+        quant_v(0)
         quant_v(1)
-        finish(0)
-        decode(1, outs)
         loga(4, 0, 2)
         loga(4, 2, 4)
-        loga(3, 2, 4)
         loga(3, 0, 2)
+        loga(3, 2, 4)
         loga(2)
-        finish(1, False, (0,))
         for t in range(4):
             lower(4, t)
-        combine_g(4, CV, NV)
-        for j, t in [(3, 0), (3, 1), (5, 0), (5, 1)]:
-            project(j, t)
-        for t in range(2, 4):
-            lower(3, t)
-        project(5, 2)
-        project(5, 3)
-        finish(1, False, (1,))
+        product_tile(4, "vta")
+        combine_g(4, 96, NV)
+        decode(0)
+        decode(1)
         for t in range(2):
             lower(3, t)
-        project(6, 0)
-        project(6, 1)
-        combine(4, 0, CV)
-        gain(2, 0)
-        quant_v(4)
-        decode(4, outs)
-        combine_g(3, CV, NV)
-        for j, t in [(5, 0), (5, 1), (5, 2), (5, 3), (6, 0), (6, 1)]:
-            sigm(j, t, j == 6)
-            if j == 5:
-                knee(j, t)
-        for j, t in [(6, 2), (6, 3), (7, 0), (7, 1), (7, 2), (7, 3)]:
+        project(5, 0)
+        project(5, 1)
+        finish(0, False, (0,))
+        for t in range(2, 4):
+            lower(3, t)
+        finish(0, False, (1,))
+        for j, t in [(5, 2), (5, 3), (6, 0), (6, 1)]:
             project(j, t)
-            sigm(j, t)
+        finish(1)
+        combine(4, 0, 96)
+        quant_v(4)
+        product_tile(3, "vta")
+        combine_g(3, 128, NV)
+        decode(4)
+        for t in range(4):
+            sigm(5, t)
+            knee(5, t)
+        for j, t in [(6, 2), (6, 3), (7, 0), (7, 1)]:
+            project(j, t)
         finish(4)
-        combine(3, 0, CV)
-        for t in range(1, 4):
+        project(7, 2)
+        project(7, 3)
+        for j in (6, 7):
+            for t in range(4):
+                sigm(j, t)
+        combine(3, 0, 128)
+        for t in range(4):
             gain(2, t)
         quant_v(3)
-        decode(3, outs)
+        product_tile(2, "vtb")
         combine(2)
-        finish(3, False, (0,))
-        quant_v(2)
-        finish(3, False, (1,))
-        decode(2, outs)
         loga(7, 0, 2)
         loga(7, 2, 4)
         loga(5)
-        loga(6, 2, 4)
         loga(6, 0, 2)
+        loga(6, 2, 4)
+        quant_v(2)
         for t in range(4):
             lower(7, t)
-        project(6, 0)
-        project(6, 1)
+        decode(3)
         gain_pe(7, 0)
         gain_pe(7, 1)
+        finish(3)
+        decode(2)
         for t in range(4):
             gain(5, t)
-        combine_g(5, CV, NV)
-        for t in range(2, 4):
+        product_tile(5, "vta")
+        combine_g(5, 128, NV)
+        for t in range(2):
             lower(6, t)
         gain_pe(7, 2)
         gain_pe(7, 3)
-        for t in range(2):
+        finish(2, False, (0,))
+        for t in range(2, 4):
             lower(6, t)
-        finish(2)
+        finish(2, False, (1,))
         gain_pe(6, 0)
         gain_pe(6, 1)
         for q in range(4):
             weave(7, q)
-        combine(5, 0, CV)
+        combine(5, 0, 128)
         quant_v(7)
         gain_pe(6, 2)
-        decode(7, outs)
-        gain_pe(6, 3)
+        decode(7)
         quant_v(5)
-        decode(5, [free[0], free[1]])
+        gain_pe(6, 3)
+        decode(5)
         for q in range(4):
             weave(6, q)
         finish(7)
-        finish(5, False, (0,))
-        quant_v(6)
-        decode(6, outs)
-        finish(5, False, (1,))
+        quant_v(6, 0, NV // 2)
+        decode(6, (0,))
+        finish(5, True, (0,))
+        quant_v(6, NV // 2, NV)
+        decode(6, (1,))
+        finish(5, True, (1,))
         finish(6, True)

@@ -361,33 +361,34 @@ def tile_tpvformersoftplusoccupancydecoder_d1p_kernel(
         scaled(nc.vector, nsc[:], sc[:], -1.0)
         c_bank = turn("c", [nxc])
         b_bank = turn("b", [nxb])
-        for q in range(4):
-            widen(0, q, q < 2)
         gc = grp.tile([P, P, 4], BF16, name="gc", align_bytes=64)
         nc.scalar.copy(
             out=words_of(gc[:]).rearrange("p (z w u) -> p z w u", z=Z, u=2),
             in_=c_bank[:, 0:256].rearrange("p (u w z) -> p z w u", u=2, z=Z),
         )
         release("c")
+        for q in range(4):
+            widen(0, q, q < 2)
         gb = grp.tile([P, P, 4], BF16, name="gb", align_bytes=64)
         nc.scalar.copy(
             out=words_of(gb[:]).rearrange("p (j z a u) -> p j z a u", z=Z, a=4, u=2),
             in_=b_bank[:, 0:256].rearrange("p (u z j a) -> p j z a u", u=2, z=Z, a=4),
         )
         release("b")
-        widen_v(1)
         turn(("a", 0), [xa[0]])
+        widen_s(1)
         ga0 = copy_a(0, 1)
         turn(("a", 1), [xa[1]])
-        ga1 = copy_a(1, 1)
         quant(cq[:], cqs[:], gc[:])
+        spread_c()
         nc.vector.tensor_copy(out=w1p[:], in_=w1raw[:].rearrange("p (m t) -> p t m", t=4))
         quant(bq[:], bqs[:], gb[:])
         nc.vector.tensor_copy(out=s1p[:], in_=s1raw[:].rearrange("p (m t) -> p t m", t=4))
-        spread_c()
         quant_a(ga0, 0, 1)
         scaled(nc.vector, nb1[:], b1t[:], -1.0)
+        widen_v(5)
         widen_s(2)
+        ga1 = copy_a(1, 1)
         widen_s(3)
         bb = take("bb")
         for t in range(4):
@@ -395,39 +396,36 @@ def tile_tpvformersoftplusoccupancydecoder_d1p_kernel(
                 out=bb[:, 64 * t : 64 * (t + 1)], lhsT=w1p[:, t, :].bitcast(FP8X4), lhsT_scale=s1p[:, t, :],
                 rhs=bq[:, 0:64].bitcast(FP8X4), rhs_scale=bqs[:, 0:64], start=True, stop=True,
             )
-        quant_a(ga1, 1, 1)
         nc.vector.tensor_tensor(
             out=bp[:], in0=bb[:, 0:256].rearrange("p (t r) -> p t r", t=4)[:, :, 0:32],
             in1=nb1[:].unsqueeze(2).to_broadcast([P, 4, 32]), op=ALU.add,
         )
         release("bb")
+        quant_a(ga1, 1, 1)
+        widen(6, 0, True)
+        widen(6, 1, True)
         widen_s(4)
-        widen_s(5)
+        widen(6, 2, False)
+        widen(6, 3, False)
         for j in range(2):
             for t in range(4):
                 project2(j, t)
                 add_b(j, t)
                 if (j, t) == (0, 0):
                     spread_b_bytes()
-                if t % 2:
-                    sigm2(j, t - 1, t + 1)
+                sigm2(j, t, t + 1)
         scaled(nc.gpsimd, gk[:], gt[:], 1.0 / KNEE)
         scaled(nc.gpsimd, ng[:], gt[:], -1.0)
-        nc.gpsimd.tensor_tensor(
-            out=dg[:], in0=ident[:].unsqueeze(1).to_broadcast([P, 4, P]),
-            in1=ng[:].unsqueeze(2).to_broadcast([P, 4, P]), op=ALU.mult,
-        )
         turn(("a", 2), [xa[2], xa[3]])
-        turn(("a", 4), [xa[4], xa[5]])
         ga2 = copy_a(2, 2, True)
+        turn(("a", 4), [xa[4], xa[5]])
         spread_b_scales(2, 6)
         quant_a(ga2, 2, 2)
         spread_b(2, 2)
+        widen_v(7)
         loga(0, 0, 2)
         loga(0, 2, 4)
         loga(1)
-        widen_v(6)
-        widen_v(7)
         project(2, 0)
         project(2, 1)
         turn(("a", 6), [xa[6], xa[7]])
@@ -443,7 +441,6 @@ def tile_tpvformersoftplusoccupancydecoder_d1p_kernel(
         spread_b(5, 1)
         lower2(1)
         product_tile(0, "vta")
-        combine_g(0, CV, NV)
         for t in range(4):
             sigm(2, t)
             knee(2, t)
@@ -453,10 +450,12 @@ def tile_tpvformersoftplusoccupancydecoder_d1p_kernel(
             for t in range(4):
                 sigm(j, t)
         spread_b(6, 2)
-        combine(0, 0, CV)
+        combine(0)
         product_tile(1, "vtb")
         combine(1)
         quant_v(0)
+        for t in range(4):
+            scaled(nc.vector, dg[:, t, :], ident[:], ng[:, t : t + 1])
         quant_v(1)
         loga(4, 0, 2)
         loga(4, 2, 4)
@@ -466,7 +465,7 @@ def tile_tpvformersoftplusoccupancydecoder_d1p_kernel(
         for t in range(4):
             lower(4, t)
         product_tile(4, "vta")
-        combine_g(4, 96, NV)
+        combine_g(4, 224, NV)
         decode(0)
         decode(1)
         for t in range(2):
@@ -480,10 +479,10 @@ def tile_tpvformersoftplusoccupancydecoder_d1p_kernel(
         for j, t in [(5, 2), (5, 3), (6, 0), (6, 1)]:
             project(j, t)
         finish(1)
-        combine(4, 0, 96)
+        combine(4, 0, 224)
         quant_v(4)
         product_tile(3, "vta")
-        combine_g(3, 128, NV)
+        combine_g(3, 288, NV)
         decode(4)
         for t in range(4):
             sigm(5, t)
@@ -496,7 +495,7 @@ def tile_tpvformersoftplusoccupancydecoder_d1p_kernel(
         for j in (6, 7):
             for t in range(4):
                 sigm(j, t)
-        combine(3, 0, 128)
+        combine(3, 0, 288)
         for t in range(4):
             gain(2, t)
         quant_v(3)
@@ -518,7 +517,7 @@ def tile_tpvformersoftplusoccupancydecoder_d1p_kernel(
         for t in range(4):
             gain(5, t)
         product_tile(5, "vta")
-        combine_g(5, 128, NV)
+        combine_g(5, 288, NV)
         for t in range(2):
             lower(6, t)
         gain_pe(7, 2)
@@ -531,7 +530,7 @@ def tile_tpvformersoftplusoccupancydecoder_d1p_kernel(
         gain_pe(6, 1)
         for q in range(4):
             weave(7, q)
-        combine(5, 0, 128)
+        combine(5, 0, 288)
         quant_v(7)
         gain_pe(6, 2)
         decode(7)

@@ -71,7 +71,7 @@ def tile_tpvformersoftplusoccupancydecoder_d1p_kernel(
         bs4 = keep.tile([P, P, 4], U8, name="bs4", align_bytes=64)
         ac = keep.tile([P, NU * P], U32, name="ac", align_bytes=64)
         as_ = keep.tile([P, NU * P], U8, name="as_", align_bytes=64)
-        bp = keep.tile([P, 4, 32], F32, name="bp")
+        bp = keep.tile([P, 4, 16], F32, name="bp")
         dg = keep.tile([P, 4, P], F32, name="dg")
         dum = keep.tile([P, 1], F32, name="dum")
         soft = [keep.tile([P, 4, NV], F32, name="soft%d" % j) for j in range(NU)]
@@ -177,9 +177,10 @@ def tile_tpvformersoftplusoccupancydecoder_d1p_kernel(
                 in_=cqs[:].bitcast(I32).rearrange("p (z w) -> p z w", z=Z).unsqueeze(2).to_broadcast([P, Z, 4, W // 4]),
             )
 
-        def spread_b_bytes():
+        def spread_b_bytes(first, count):
+            rows = slice(16 * first, 16 * (first + count))
             for i in range(4):
-                nc.gpsimd.tensor_copy(out=bs4[:, 32:P, i], in_=bqs[:, 32:P])
+                nc.vector.tensor_copy(out=bs4[:, rows, i], in_=bqs[:, rows])
 
         def spread_b_scales(first, count):
             rows = slice(16 * first, 16 * (first + count))
@@ -340,6 +341,16 @@ def tile_tpvformersoftplusoccupancydecoder_d1p_kernel(
         out_v = out.rearrange("(j a) w z e -> (a w) j z e", a=4)
         ots = {}
 
+        def finish_z(j, z, eng):
+            zp, zz = divmod(z, 2)
+            ot = ots[j]
+            nc.vector.tensor_tensor(
+                out=ot[:, z, :], in0=held[j, "o", zp][0][:, E * zz : E * (zz + 1)], in1=b2t[:], op=ALU.add
+            )
+            if zz == 1:
+                release((j, "o", zp))
+            eng.dma_start(out=out_v[:, j, z], in_=ot[:, z, :])
+
         def finish(j, split=False, halves=(0, 1)):
             for zp in halves:
                 if zp == 0:
@@ -380,13 +391,13 @@ def tile_tpvformersoftplusoccupancydecoder_d1p_kernel(
         ga0 = copy_a(0, 1)
         turn(("a", 1), [xa[1]])
         quant(cq[:], cqs[:], gc[:])
-        spread_c()
         nc.vector.tensor_copy(out=w1p[:], in_=w1raw[:].rearrange("p (m t) -> p t m", t=4))
-        quant(bq[:], bqs[:], gb[:])
+        spread_c()
         nc.vector.tensor_copy(out=s1p[:], in_=s1raw[:].rearrange("p (m t) -> p t m", t=4))
+        quant(bq[:], bqs[:], gb[:])
         quant_a(ga0, 0, 1)
         scaled(nc.vector, nb1[:], b1t[:], -1.0)
-        widen_v(5)
+        spread_b_bytes(1, 1)
         widen_s(2)
         ga1 = copy_a(1, 1)
         widen_s(3)
@@ -396,90 +407,100 @@ def tile_tpvformersoftplusoccupancydecoder_d1p_kernel(
                 out=bb[:, 64 * t : 64 * (t + 1)], lhsT=w1p[:, t, :].bitcast(FP8X4), lhsT_scale=s1p[:, t, :],
                 rhs=bq[:, 0:64].bitcast(FP8X4), rhs_scale=bqs[:, 0:64], start=True, stop=True,
             )
+        scaled(nc.vector, gk[:], gt[:], 1.0 / KNEE)
+        quant_a(ga1, 1, 1)
         nc.vector.tensor_tensor(
-            out=bp[:], in0=bb[:, 0:256].rearrange("p (t r) -> p t r", t=4)[:, :, 0:32],
-            in1=nb1[:].unsqueeze(2).to_broadcast([P, 4, 32]), op=ALU.add,
+            out=bp[:], in0=bb[:, 0:256].rearrange("p (t r) -> p t r", t=4)[:, :, 0:16],
+            in1=nb1[:].unsqueeze(2).to_broadcast([P, 4, 16]), op=ALU.add,
         )
         release("bb")
-        quant_a(ga1, 1, 1)
-        widen(6, 0, True)
-        widen(6, 1, True)
+        spread_b_scales(1, 1)
+        spread_b(1, 1)
+        scaled(nc.vector, ng[:], gt[:], -1.0)
+        for t in range(4):
+            scaled(nc.gpsimd, dg[:, t, :], ident[:], ng[:, t : t + 1])
         widen_s(4)
-        widen(6, 2, False)
-        widen(6, 3, False)
-        for j in range(2):
-            for t in range(4):
-                project2(j, t)
-                add_b(j, t)
-                if (j, t) == (0, 0):
-                    spread_b_bytes()
-                sigm2(j, t, t + 1)
-        scaled(nc.gpsimd, gk[:], gt[:], 1.0 / KNEE)
-        scaled(nc.gpsimd, ng[:], gt[:], -1.0)
-        turn(("a", 2), [xa[2], xa[3]])
-        ga2 = copy_a(2, 2, True)
-        turn(("a", 4), [xa[4], xa[5]])
+        widen(5, 0, False)
+        widen(5, 1, False)
+        for t in range(4):
+            project2(0, t)
+            add_b(0, t)
+            sigm2(0, t, t + 1)
+        for t in range(4):
+            project(1, t)
+            sigm(1, t)
+        widen(5, 2, True)
+        widen(5, 3, True)
+        spread_b_bytes(2, 6)
+        widen_v(6)
         spread_b_scales(2, 6)
-        quant_a(ga2, 2, 2)
-        spread_b(2, 2)
         widen_v(7)
-        loga(0, 0, 2)
-        loga(0, 2, 4)
-        loga(1)
+        spread_b(2, 2)
+        turn(("a", 2), [xa[2], xa[3]])
+        turn(("a", 4), [xa[4], xa[5]])
+        turn(("a", 6), [xa[6], xa[7]])
+        ga2 = copy_a(2, 2, True)
+        spread_b(4, 2)
+        quant_a(ga2, 2, 2)
+        ga4 = copy_a(4, 2, True)
+        loga(1, 0, 2)
+        loga(1, 2, 4)
+        loga(0)
         project(2, 0)
         project(2, 1)
-        turn(("a", 6), [xa[6], xa[7]])
-        ga4 = copy_a(4, 2, True)
-        spread_b(4, 1)
         quant_a(ga4, 4, 2)
-        lower2(0, 0, 2)
         ga6 = copy_a(6, 2, True)
-        for j, t in [(2, 2), (2, 3), (3, 0), (3, 1), (3, 2), (3, 3)]:
-            project(j, t)
-        lower2(0, 2, 4)
+        project(2, 2)
+        project(2, 3)
+        for t in range(4):
+            lower(1, t)
+            project(3, t)
         quant_a(ga6, 6, 2)
-        spread_b(5, 1)
-        lower2(1)
+        lower2(0)
         product_tile(0, "vta")
+        combine_g(0, 352, NV)
         for t in range(4):
             sigm(2, t)
             knee(2, t)
         for t in range(4):
             project(4, t)
-        for j in (3, 4):
-            for t in range(4):
-                sigm(j, t)
-        spread_b(6, 2)
-        combine(0)
+        sigm(3, 0, True)
+        sigm(3, 1, True)
+        for j, t in [(3, 2), (3, 3), (4, 0), (4, 1), (4, 2), (4, 3)]:
+            sigm(j, t)
         product_tile(1, "vtb")
         combine(1)
-        quant_v(0)
-        for t in range(4):
-            scaled(nc.vector, dg[:, t, :], ident[:], ng[:, t : t + 1])
+        spread_b(6, 2)
         quant_v(1)
+        decode(1)
+        combine(0, 0, 352)
+        finish(1, False, (0,))
+        quant_v(0)
+        finish(1, False, (1,))
+        decode(0)
         loga(4, 0, 2)
         loga(4, 2, 4)
-        loga(3, 0, 2)
         loga(3, 2, 4)
+        loga(3, 0, 2)
         loga(2)
         for t in range(4):
             lower(4, t)
+            if t == 0:
+                project(3, 0)
         product_tile(4, "vta")
-        combine_g(4, 224, NV)
-        decode(0)
-        decode(1)
+        combine_g(4, 288, NV)
+        project(3, 1)
         for t in range(2):
+            project(5, t)
+        finish(0)
+        project(5, 2)
+        project(5, 3)
+        for t in (2, 3, 0, 1):
             lower(3, t)
-        project(5, 0)
-        project(5, 1)
-        finish(0, False, (0,))
-        for t in range(2, 4):
-            lower(3, t)
-        finish(0, False, (1,))
-        for j, t in [(5, 2), (5, 3), (6, 0), (6, 1)]:
-            project(j, t)
-        finish(1)
-        combine(4, 0, 224)
+        project(6, 0)
+        project(6, 1)
+        combine(4, 0, 288)
+        gain(2, 0)
         quant_v(4)
         product_tile(3, "vta")
         combine_g(3, 288, NV)
@@ -496,7 +517,7 @@ def tile_tpvformersoftplusoccupancydecoder_d1p_kernel(
             for t in range(4):
                 sigm(j, t)
         combine(3, 0, 288)
-        for t in range(4):
+        for t in range(1, 4):
             gain(2, t)
         quant_v(3)
         product_tile(2, "vtb")
@@ -522,28 +543,29 @@ def tile_tpvformersoftplusoccupancydecoder_d1p_kernel(
             lower(6, t)
         gain_pe(7, 2)
         gain_pe(7, 3)
-        finish(2, False, (0,))
+        finish(2, True, (0,))
         for t in range(2, 4):
             lower(6, t)
-        finish(2, False, (1,))
+        finish(2, True, (1,))
         gain_pe(6, 0)
         gain_pe(6, 1)
         for q in range(4):
             weave(7, q)
+        weave(6, 0)
         combine(5, 0, 288)
         quant_v(7)
         gain_pe(6, 2)
         decode(7)
         quant_v(5)
-        gain_pe(6, 3)
         decode(5)
-        for q in range(4):
-            weave(6, q)
-        finish(7)
-        quant_v(6, 0, NV // 2)
-        decode(6, (0,))
-        finish(5, True, (0,))
-        quant_v(6, NV // 2, NV)
-        decode(6, (1,))
-        finish(5, True, (1,))
-        finish(6, True)
+        weave(6, 1)
+        weave(6, 2)
+        combine(6, 3 * P, NV)
+        finish(7, True, (0,))
+        quant_v(6)
+        finish(7, True, (1,))
+        decode(6)
+        finish(5, True)
+        finish(6, True, (0,))
+        finish_z(6, 2, nc.scalar)
+        finish_z(6, 3, nc.sync)

@@ -313,6 +313,15 @@ def tile_tpvformersoftplusoccupancydecoder_d1p_kernel(
             nc.scalar.copy(out=vts[j][:, P * q : P * (q + 1)], in_=bank[:].rearrange("p (t n) -> p n t", t=4))
             release((j, "g", q))
 
+        def gain_s(j, q):
+            cols = slice(P * q, P * (q + 1))
+            if j not in vts:
+                vts[j] = vpool.tile([P, NV, 4], BF16, name="vw", align_bytes=64)
+            flat = grp.tile([P, 4, P], BF16, name="flat")
+            for t in range(4):
+                nc.scalar.activation(out=flat[:, t, :], in_=soft[j][:, t, cols], func=AF.Copy, scale=ng[:, t : t + 1])
+            nc.scalar.copy(out=vts[j][:, cols], in_=flat[:].rearrange("p t n -> p n t"))
+
         def lower2(j, t0=0, t1=4):
             e = soft[j][:, t0:t1].rearrange("p t n -> p (t n)")
             nc.vector.tensor_tensor(out=e, in0=e, in1=nsum[j][:, t0:t1].rearrange("p t n -> p (t n)"), op=ALU.min)
@@ -407,15 +416,14 @@ def tile_tpvformersoftplusoccupancydecoder_d1p_kernel(
                 out=bb[:, 64 * t : 64 * (t + 1)], lhsT=w1p[:, t, :].bitcast(FP8X4), lhsT_scale=s1p[:, t, :],
                 rhs=bq[:, 0:64].bitcast(FP8X4), rhs_scale=bqs[:, 0:64], start=True, stop=True,
             )
-        scaled(nc.vector, gk[:], gt[:], 1.0 / KNEE)
-        quant_a(ga1, 1, 1)
+        spread_b_scales(1, 1)
+        spread_b(1, 1)
         nc.vector.tensor_tensor(
             out=bp[:], in0=bb[:, 0:256].rearrange("p (t r) -> p t r", t=4)[:, :, 0:16],
             in1=nb1[:].unsqueeze(2).to_broadcast([P, 4, 16]), op=ALU.add,
         )
         release("bb")
-        spread_b_scales(1, 1)
-        spread_b(1, 1)
+        quant_a(ga1, 1, 1)
         scaled(nc.vector, ng[:], gt[:], -1.0)
         for t in range(4):
             scaled(nc.gpsimd, dg[:, t, :], ident[:], ng[:, t : t + 1])
@@ -431,6 +439,7 @@ def tile_tpvformersoftplusoccupancydecoder_d1p_kernel(
             sigm(1, t)
         widen(5, 2, True)
         widen(5, 3, True)
+        scaled(nc.vector, gk[:], gt[:], 1.0 / KNEE)
         spread_b_bytes(2, 6)
         widen_v(6)
         spread_b_scales(2, 6)
@@ -443,22 +452,24 @@ def tile_tpvformersoftplusoccupancydecoder_d1p_kernel(
         spread_b(4, 2)
         quant_a(ga2, 2, 2)
         ga4 = copy_a(4, 2, True)
+        loga(0, 0, 2)
+        loga(0, 2, 4)
         loga(1, 0, 2)
         loga(1, 2, 4)
-        loga(0)
         project(2, 0)
         project(2, 1)
         quant_a(ga4, 4, 2)
         ga6 = copy_a(6, 2, True)
         project(2, 2)
         project(2, 3)
+        lower2(0, 0, 2)
+        quant_a(ga6, 6, 2)
+        lower2(0, 2, 4)
+        product_tile(0, "vta")
+        combine_g(0, 160, NV)
         for t in range(4):
             lower(1, t)
             project(3, t)
-        quant_a(ga6, 6, 2)
-        lower2(0)
-        product_tile(0, "vta")
-        combine_g(0, 352, NV)
         for t in range(4):
             sigm(2, t)
             knee(2, t)
@@ -468,38 +479,39 @@ def tile_tpvformersoftplusoccupancydecoder_d1p_kernel(
         sigm(3, 1, True)
         for j, t in [(3, 2), (3, 3), (4, 0), (4, 1), (4, 2), (4, 3)]:
             sigm(j, t)
+        combine(0, 0, 160)
+        spread_b(6, 2)
+        quant_v(0)
+        decode(0)
         product_tile(1, "vtb")
         combine(1)
-        spread_b(6, 2)
+        finish(0, False, (0,))
         quant_v(1)
+        finish(0, False, (1,))
         decode(1)
-        combine(0, 0, 352)
-        finish(1, False, (0,))
-        quant_v(0)
-        finish(1, False, (1,))
-        decode(0)
         loga(4, 0, 2)
         loga(4, 2, 4)
         loga(3, 2, 4)
         loga(3, 0, 2)
         loga(2)
+        finish(1, False, (0,))
         for t in range(4):
             lower(4, t)
             if t == 0:
                 project(3, 0)
         product_tile(4, "vta")
-        combine_g(4, 288, NV)
+        combine_g(4, 336, NV)
         project(3, 1)
         for t in range(2):
             project(5, t)
-        finish(0)
+        finish(1, False, (1,))
         project(5, 2)
         project(5, 3)
         for t in (2, 3, 0, 1):
             lower(3, t)
         project(6, 0)
         project(6, 1)
-        combine(4, 0, 288)
+        combine(4, 0, 336)
         gain(2, 0)
         quant_v(4)
         product_tile(3, "vta")
@@ -533,37 +545,36 @@ def tile_tpvformersoftplusoccupancydecoder_d1p_kernel(
         decode(3)
         gain_pe(7, 0)
         gain_pe(7, 1)
-        finish(3)
-        decode(2)
+        finish(3, True)
+        gain_pe(7, 2)
         for t in range(4):
             gain(5, t)
         product_tile(5, "vta")
         combine_g(5, 288, NV)
         for t in range(2):
             lower(6, t)
-        gain_pe(7, 2)
+        decode(2)
         gain_pe(7, 3)
-        finish(2, True, (0,))
         for t in range(2, 4):
             lower(6, t)
-        finish(2, True, (1,))
-        gain_pe(6, 0)
-        gain_pe(6, 1)
+        finish(2, True)
         for q in range(4):
             weave(7, q)
-        weave(6, 0)
-        combine(5, 0, 288)
+        gain_pe(6, 0)
+        gain_pe(6, 1)
         quant_v(7)
-        gain_pe(6, 2)
         decode(7)
-        quant_v(5)
-        decode(5)
+        gain_pe(6, 2)
+        gain_s(6, 3)
+        weave(6, 0)
         weave(6, 1)
         weave(6, 2)
-        combine(6, 3 * P, NV)
+        combine(5, 0, 288)
         finish(7, True, (0,))
-        quant_v(6)
+        quant_v(5)
+        decode(5)
         finish(7, True, (1,))
+        quant_v(6)
         decode(6)
         finish(5, True)
         finish(6, True, (0,))

@@ -147,6 +147,12 @@ def tile_tpvformersoftplusoccupancydecoder_d1p_kernel(
                     nc.tensor.transpose(bank[:, 256 * s + P * u : 256 * s + P * u + P], words[:, u : 2 * P : 2], ident[:])
             return bank
 
+        def warm_up(count):
+            bank = take("warm")
+            for i in range(count):
+                nc.tensor.matmul(out=bank[:, P * i : P * (i + 1)], lhsT=ident[:], rhs=ident[:], start=True, stop=True)
+            release("warm")
+
         def words_of(tile):
             return tile.rearrange("p r e -> p (r e)").bitcast(F32)
 
@@ -379,6 +385,7 @@ def tile_tpvformersoftplusoccupancydecoder_d1p_kernel(
         scaled(nc.vector, nxc[:], xc[:], -1.0)
         scaled(nc.vector, nxb[:], xb[:], -1.0)
         scaled(nc.vector, nsc[:], sc[:], -1.0)
+        warm_up(2)
         c_bank = turn("c", [nxc])
         b_bank = turn("b", [nxb])
         gc = grp.tile([P, P, 4], BF16, name="gc", align_bytes=64)
@@ -395,10 +402,13 @@ def tile_tpvformersoftplusoccupancydecoder_d1p_kernel(
             in_=b_bank[:, 0:256].rearrange("p (u z j a) -> p j z a u", u=2, z=Z, a=4),
         )
         release("b")
+        warm_up(2)
         turn(("a", 0), [xa[0]])
         widen_s(1)
         ga0 = copy_a(0, 1)
+        warm_up(1)
         turn(("a", 1), [xa[1]])
+        warm_up(1)
         quant(cq[:], cqs[:], gc[:])
         nc.vector.tensor_copy(out=w1p[:], in_=w1raw[:].rearrange("p (m t) -> p t m", t=4))
         spread_c()

@@ -267,8 +267,8 @@ def tile_tpvformersoftplusoccupancydecoder_d1p_kernel(
             e = soft[j][:, t0:t1, :].rearrange("p t n -> p (t n)")
             nc.scalar.activation(out=e, in_=e, func=AF.Ln, bias=EPS)
 
-        def gain(j, t):
-            e = soft[j][:, t, :]
+        def gain(j, t, c0=0, c1=NV):
+            e = soft[j][:, t, c0:c1]
             nc.vector.tensor_scalar(out=e, in0=e, scalar1=-KNEE, scalar2=gk[:, t : t + 1], op0=ALU.max, op1=ALU.mult)
 
         def lower(j, t):
@@ -412,10 +412,9 @@ def tile_tpvformersoftplusoccupancydecoder_d1p_kernel(
         quant(cq[:], cqs[:], gc[:])
         nc.vector.tensor_copy(out=w1p[:], in_=w1raw[:].rearrange("p (m t) -> p t m", t=4))
         spread_c()
-        nc.vector.tensor_copy(out=s1p[:], in_=s1raw[:].rearrange("p (m t) -> p t m", t=4))
         quant(bq[:], bqs[:], gb[:])
+        nc.vector.tensor_copy(out=s1p[:], in_=s1raw[:].rearrange("p (m t) -> p t m", t=4))
         quant_a(ga0, 0, 1)
-        scaled(nc.vector, nb1[:], b1t[:], -1.0)
         spread_b_bytes(1, 1)
         widen_s(2)
         ga1 = copy_a(1, 1)
@@ -427,6 +426,7 @@ def tile_tpvformersoftplusoccupancydecoder_d1p_kernel(
                 rhs=bq[:, 0:64].bitcast(FP8X4), rhs_scale=bqs[:, 0:64], start=True, stop=True,
             )
         spread_b_scales(1, 1)
+        scaled(nc.vector, nb1[:], b1t[:], -1.0)
         spread_b(1, 1)
         nc.vector.tensor_tensor(
             out=bp[:], in0=bb[:, 0:256].rearrange("p (t r) -> p t r", t=4)[:, :, 0:16],
@@ -522,7 +522,7 @@ def tile_tpvformersoftplusoccupancydecoder_d1p_kernel(
         project(6, 0)
         project(6, 1)
         combine(4, 0, 336)
-        gain(2, 0)
+        gain(2, 0, 0, 288)
         quant_v(4)
         product_tile(3, "vta")
         combine_g(3, 288, NV)
@@ -532,40 +532,46 @@ def tile_tpvformersoftplusoccupancydecoder_d1p_kernel(
             knee(5, t)
         for j, t in [(6, 2), (6, 3), (7, 0), (7, 1)]:
             project(j, t)
-        finish(4)
+        sigm(6, 0, True)
+        sigm(6, 1, True)
         project(7, 2)
         project(7, 3)
-        for j in (6, 7):
-            for t in range(4):
-                sigm(j, t)
+        for j, t in [(6, 2), (6, 3), (7, 0), (7, 1), (7, 2), (7, 3)]:
+            sigm(j, t)
+        finish(4)
         combine(3, 0, 288)
         for t in range(1, 4):
-            gain(2, t)
+            gain(2, t, 0, 288)
         quant_v(3)
+        decode(3)
         product_tile(2, "vtb")
-        combine(2)
+        combine(2, 0, 288)
+        for t in range(4):
+            gain(2, t, 288, NV)
+        combine_g(2, 288, NV)
+        finish(3, True)
+        project(6, 0)
+        project(6, 1)
         loga(7, 0, 2)
         loga(7, 2, 4)
-        loga(5)
-        loga(6, 0, 2)
+        loga(5, 0, 2)
+        loga(5, 2, 4)
         loga(6, 2, 4)
-        quant_v(2)
+        loga(6, 0, 2)
         for t in range(4):
             lower(7, t)
-        decode(3)
-        gain_pe(7, 0)
-        gain_pe(7, 1)
-        finish(3, True)
-        gain_pe(7, 2)
+        for q in range(3):
+            gain_pe(7, q)
+        quant_v(2)
         for t in range(4):
             gain(5, t)
         product_tile(5, "vta")
         combine_g(5, 288, NV)
-        for t in range(2):
+        for t in range(2, 4):
             lower(6, t)
         decode(2)
         gain_pe(7, 3)
-        for t in range(2, 4):
+        for t in range(2):
             lower(6, t)
         finish(2, True)
         for q in range(4):

@@ -19,10 +19,11 @@ ALU = mybir.AluOpType
 P = 128
 NU = 8
 NV = 512
+HV = 256
 KNEE = 16.0
-CV = 256
 EPS = 2.0 ** -60
 WI = 4
+NB0 = 4
 
 
 def tile_tpvformersoftplusoccupancydecoder_d1p_kernel(
@@ -32,15 +33,15 @@ def tile_tpvformersoftplusoccupancydecoder_d1p_kernel(
     with ExitStack() as ctx:
         keep = ctx.enter_context(tc.tile_pool(name="keep", bufs=1))
         grp = ctx.enter_context(tc.tile_pool(name="grp", bufs=2))
-        vpool = ctx.enter_context(tc.tile_pool(name="vpool", bufs=3))
+        vpool = ctx.enter_context(tc.tile_pool(name="vpool", bufs=4))
         one = ctx.enter_context(tc.tile_pool(name="one", bufs=1))
-        opool = ctx.enter_context(tc.tile_pool(name="opool", bufs=3))
+        opool = ctx.enter_context(tc.tile_pool(name="opool", bufs=4))
         psum = ctx.enter_context(tc.psum_pool(name="psum", bufs=1))
         ctx.enter_context(tc.manual_schedule())
 
         ident = keep.tile([P, P], F32, name="ident")
-        byt0 = keep.tile([P, 4, D], U8, name="byt0")
-        byt1 = keep.tile([P, NU - 4, D], U8, name="byt1")
+        byt0 = keep.tile([P, NB0, D], U8, name="byt0")
+        byt1 = keep.tile([P, NU - NB0, D], U8, name="byt1")
         sc = keep.tile([P, NU, 4], F32, name="sc")
         nsc = keep.tile([P, NU, 4], F32, name="nsc")
         xa = [keep.tile([P, D], BF16, name="xa%d" % j, align_bytes=64) for j in range(NU)]
@@ -71,7 +72,7 @@ def tile_tpvformersoftplusoccupancydecoder_d1p_kernel(
         bs4 = keep.tile([P, P, 4], U8, name="bs4", align_bytes=64)
         ac = keep.tile([P, NU * P], U32, name="ac", align_bytes=64)
         as_ = keep.tile([P, NU * P], U8, name="as_", align_bytes=64)
-        bp = keep.tile([P, 4, 16], F32, name="bp")
+        bp = keep.tile([P, 4, 4, 16], F32, name="bp")
         dg = keep.tile([P, 4, P], F32, name="dg")
         dum = keep.tile([P, 1], F32, name="dum")
         soft = [keep.tile([P, 4, NV], F32, name="soft%d" % j) for j in range(NU)]
@@ -79,34 +80,13 @@ def tile_tpvformersoftplusoccupancydecoder_d1p_kernel(
 
         bytes_v = thw_bytes.rearrange("(j a) w k -> (a w) j k", a=4)
         scale_v = thw_scale.rearrange("(j a) w q -> (a w) j q", a=4)
-        nc.vector.memset(dum[:], 0.0)
-        nc.vector.memset(s1raw[:].bitcast(I32), 0)
-        nc.vector.memset(cqs[:].bitcast(I32), 0)
-        nc.vector.memset(bqs[:].bitcast(I32), 0)
-        nc.vector.memset(s2w[:].bitcast(I32), 0)
+        out_v = out.rearrange("(j a) w z e -> (a w) j z e", a=4)
 
         def load_rows(tile, scales, q, eng):
             eng.dma_start(
                 out=tile[32 * q : 32 * q + 4, :].bitcast(I32),
                 in_=scales[0, 4 * q : 4 * q + 4, :].bitcast(I32),
             )
-
-        nc.sync.dma_start(out=xc[:], in_=twz.rearrange("w z d -> (w z) d"))
-        nc.scalar.dma_start(out=xb[:], in_=tzh.rearrange("z h d -> (z h) d"))
-        nc.sync.dma_start(out=byt0[:], in_=bytes_v[:, 0:4, :])
-        nc.scalar.dma_start(out=sc[:], in_=scale_v)
-        nc.sync.dma_start(out=w1raw[:], in_=w1_words[0].rearrange("p n t -> p (n t)").bitcast(I32))
-        for q in range(4):
-            load_rows(s1raw, w1_scales, q, nc.sync)
-        nc.scalar.activation(out=dum[:], in_=dum[:], func=AF.Sigmoid)
-        nc.sync.dma_start(out=b1t[:], in_=b1.rearrange("(p t) -> p t", t=4))
-        nc.sync.dma_start(out=byt1[:], in_=bytes_v[:, 4:NU, :])
-        nc.sync.dma_start(out=gt[:], in_=g.rearrange("(p t) -> p t", t=4))
-        make_identity(nc, ident[:])
-        nc.sync.dma_start(out=w2w[:], in_=w2_words[0].rearrange("p n t -> p (n t)").bitcast(I32))
-        for q in range(4):
-            load_rows(s2w, w2_scales, q, nc.sync)
-        nc.sync.dma_start(out=b2t[:], in_=b2.partition_broadcast(P))
 
         def scaled(eng, dst, src, factor):
             eng.tensor_scalar(out=dst, in0=src, scalar1=factor, scalar2=0.0, op0=ALU.mult, op1=ALU.add)
@@ -124,7 +104,7 @@ def tile_tpvformersoftplusoccupancydecoder_d1p_kernel(
 
         def widen(j, q, vec):
             cols = slice(128 * q, 128 * q + 128)
-            src = (byt0[:, j, cols] if j < 4 else byt1[:, j - 4, cols]).bitcast(FP8)
+            src = (byt0[:, j, cols] if j < NB0 else byt1[:, j - NB0, cols]).bitcast(FP8)
             s = nsc[:, j, q : q + 1]
             if vec:
                 nc.vector.tensor_scalar(out=xa[j][:, cols], in0=src, scalar1=s, scalar2=None, op0=ALU.mult)
@@ -156,6 +136,8 @@ def tile_tpvformersoftplusoccupancydecoder_d1p_kernel(
         def words_of(tile):
             return tile.rearrange("p r e -> p (r e)").bitcast(F32)
 
+        grouped = {}
+
         def copy_a(first, count, vec=False):
             bank = held["a", first][0]
             ga = grp.tile([P, 2 * P, 4], BF16, name="ga", align_bytes=64)
@@ -164,14 +146,14 @@ def tile_tpvformersoftplusoccupancydecoder_d1p_kernel(
                 in_=bank[:, 0 : count * 256].rearrange("p (s u r) -> p s r u", s=count, u=2),
             )
             release(("a", first))
-            return ga
+            grouped[first] = ga
 
-        def quant(codes, scales, grouped):
-            nc.vector.quantize_mx(out=codes.bitcast(FP8X4), scales=scales, in_=grouped.rearrange("p r e -> p (r e)"))
+        def quant(codes, scales, src):
+            nc.vector.quantize_mx(out=codes.bitcast(FP8X4), scales=scales, in_=src.rearrange("p r e -> p (r e)"))
 
-        def quant_a(ga, first, count):
+        def quant_a(first, count):
             cols = slice(first * P, (first + count) * P)
-            quant(ac[:, cols], as_[:, cols], ga[:, 0 : count * P])
+            quant(ac[:, cols], as_[:, cols], grouped[first][:, 0 : count * P])
 
         def spread_c():
             nc.vector.tensor_copy(
@@ -204,8 +186,7 @@ def tile_tpvformersoftplusoccupancydecoder_d1p_kernel(
                 in_=bq[:, rows].unsqueeze(2).to_broadcast([P, 16 * count, W]),
             )
 
-
-        def project(j, t):
+        def project(j, t, with_b=True):
             bank = take((j, t))
             lhs, lhs_s = w1p[:, t, :].bitcast(FP8X4), s1p[:, t, :]
             ucols = slice(NV * j, NV * (j + 1))
@@ -214,40 +195,36 @@ def tile_tpvformersoftplusoccupancydecoder_d1p_kernel(
             for z in range(Z):
                 nc.tensor.matmul_mx(
                     out=bank[:, P * z : P * (z + 1)], lhsT=lhs, lhsT_scale=lhs_s,
-                    rhs=ac[:, acols].bitcast(FP8X4), rhs_scale=as_[:, acols], start=False, stop=False,
+                    rhs=ac[:, acols].bitcast(FP8X4), rhs_scale=as_[:, acols], start=False, stop=z == Z - 1 and not with_b,
                 )
-            nc.tensor.matmul_mx(out=bank[:], lhsT=lhs, lhsT_scale=lhs_s, rhs=brc[:, ucols].bitcast(FP8X4), rhs_scale=brs[:, ucols], start=False, stop=True)
-            return bank
-
-        def project2(j, t):
-            bank = take((j, t))
-            lhs, lhs_s = w1p[:, t, :].bitcast(FP8X4), s1p[:, t, :]
-            acols = slice(P * j, P * (j + 1))
-            nc.tensor.matmul_mx(out=bank[:], lhsT=lhs, lhsT_scale=lhs_s, rhs=crc[:].bitcast(FP8X4), rhs_scale=crs[:], start=True, stop=False)
-            for z in range(Z):
-                nc.tensor.matmul_mx(
-                    out=bank[:, P * z : P * (z + 1)], lhsT=lhs, lhsT_scale=lhs_s,
-                    rhs=ac[:, acols].bitcast(FP8X4), rhs_scale=as_[:, acols], start=False, stop=z == Z - 1,
-                )
-            return bank
+            if with_b:
+                nc.tensor.matmul_mx(out=bank[:], lhsT=lhs, lhsT_scale=lhs_s, rhs=brc[:, ucols].bitcast(FP8X4), rhs_scale=brs[:, ucols], start=False, stop=True)
 
         def add_b(j, t):
             bank = held[j, t][0]
-            if t == 0:
+            if j not in nsum:
                 nsum[j] = keep.tile([P, 4, NV], F32, name="nsum%d" % j)
             nc.vector.tensor_tensor(
                 out=nsum[j][:, t, :].rearrange("p (r w) -> p r w", w=W),
                 in0=bank[:].rearrange("p (r w) -> p r w", w=W),
-                in1=bp[:, t, 16 * j : 16 * j + 16].unsqueeze(2).to_broadcast([P, 16, W]),
+                in1=bp[:, t, j, :].unsqueeze(2).to_broadcast([P, 16, W]),
                 op=ALU.add,
             )
             release((j, t))
 
-        def sigm2(j, t0, t1):
-            nc.scalar.activation(
-                out=soft[j][:, t0:t1, :].rearrange("p t n -> p (t n)"),
-                in_=nsum[j][:, t0:t1, :].rearrange("p t n -> p (t n)"), func=AF.Sigmoid,
+        def clip(j, t0, t1):
+            nc.vector.tensor_scalar(
+                out=soft[j][:, t0:t1, :], in0=nsum[j][:, t0:t1, :], scalar1=-KNEE, scalar2=None, op0=ALU.max
             )
+
+        def factor(j, t):
+            big[j] = nsum[j]
+            e = nsum[j][:, t, :]
+            nc.vector.tensor_scalar(out=e, in0=e, scalar1=-KNEE, scalar2=gk[:, t : t + 1], op0=ALU.min, op1=ALU.mult)
+
+        def sigm2(j, t0, t1):
+            e = soft[j][:, t0:t1, :]
+            nc.scalar.activation(out=e, in_=e, func=AF.Sigmoid)
 
         def sigm(j, t, last=False):
             nc.scalar.activation(out=soft[j][:, t, :], in_=held[j, t][0][:], func=AF.Sigmoid, bias=nb1[:, t : t + 1])
@@ -256,51 +233,66 @@ def tile_tpvformersoftplusoccupancydecoder_d1p_kernel(
 
         def knee(j, t):
             bank = held[j, t][0]
-            if t == 0:
+            if j not in big:
                 big[j] = keep.tile([P, 4, NV], F32, name="big%d" % j)
             nc.vector.tensor_scalar(
                 out=big[j][:, t, :], in0=bank[:], scalar1=nb1[:, t : t + 1], scalar2=-KNEE, op0=ALU.add, op1=ALU.min
             )
             release((j, t))
 
-        def loga(j, t0=0, t1=4):
-            e = soft[j][:, t0:t1, :].rearrange("p t n -> p (t n)")
+        def knee2(j):
+            big[j] = keep.tile([P, 4, NV], F32, name="big%d" % j)
+            nc.vector.tensor_scalar(out=big[j][:], in0=nsum[j][:], scalar1=-KNEE, scalar2=None, op0=ALU.min)
+
+        def loga(j, t0=0, t1=4, c0=0, c1=NV):
+            e = soft[j][:, t0:t1, c0:c1]
             nc.scalar.activation(out=e, in_=e, func=AF.Ln, bias=EPS)
 
         def gain(j, t, c0=0, c1=NV):
             e = soft[j][:, t, c0:c1]
             nc.vector.tensor_scalar(out=e, in0=e, scalar1=-KNEE, scalar2=gk[:, t : t + 1], op0=ALU.max, op1=ALU.mult)
 
-        def lower(j, t):
+        def lower(j, t, c0=0, c1=NV):
             bank = held[j, t][0]
-            e = soft[j][:, t, :]
-            nc.vector.scalar_tensor_tensor(out=e, in0=bank[:], scalar=nb1[:, t : t + 1], in1=e, op0=ALU.add, op1=ALU.min)
-            release((j, t))
+            e = soft[j][:, t, c0:c1]
+            nc.vector.scalar_tensor_tensor(out=e, in0=bank[:, c0:c1], scalar=nb1[:, t : t + 1], in1=e, op0=ALU.add, op1=ALU.min)
+            if c1 == NV:
+                release((j, t))
+
+        def lower2(j, c0=0, c1=NV):
+            e = soft[j][:, :, c0:c1]
+            nc.vector.tensor_tensor(out=e, in0=e, in1=nsum[j][:, :, c0:c1], op=ALU.min)
 
         vts, vqs = {}, {}
 
-        def product_tile(j, name):
-            vts[j] = one.tile([P, NV, 4], BF16, name=name, align_bytes=64)
+        def walk(ap):
+            return ap.rearrange("p t (c i) -> p c t i", i=WI)
 
-        def combine(j, c0=0, c1=NV, eng=nc.vector):
+        def product_v(j, hf, c0=0, c1=HV, psum_g=True):
+            if (j, hf) not in vts:
+                vts[j, hf] = vpool.tile([P, HV, 4], BF16, name="vv", align_bytes=64)
+            cols = slice(HV * hf + c0, HV * hf + c1)
             if j in big:
-                other = big[j][:, :, c0:c1].rearrange("p t (c i) -> p c t i", i=WI)
+                other = walk(big[j][:, :, cols])
             else:
-                other = ng[:].unsqueeze(1).unsqueeze(3).to_broadcast([P, (c1 - c0) // WI, 4, WI])
-            eng.tensor_tensor(
-                out=vts[j][:, c0:c1].rearrange("p (c i) t -> p c t i", i=WI),
-                in0=soft[j][:, :, c0:c1].rearrange("p t (c i) -> p c t i", i=WI),
-                in1=other,
-                op=ALU.mult,
+                gsrc = held["g"][0][:, 0:4] if psum_g else ng[:]
+                other = gsrc.unsqueeze(1).unsqueeze(3).to_broadcast([P, (c1 - c0) // WI, 4, WI])
+            nc.vector.tensor_tensor(
+                out=vts[j, hf][:, c0:c1].rearrange("p (c i) t -> p c t i", i=WI),
+                in0=walk(soft[j][:, :, cols]), in1=other, op=ALU.mult,
             )
 
-        def combine_g(j, c0, c1):
+        def product_g(j, hf, c0=0, c1=HV):
+            if (j, hf) not in vts:
+                vts[j, hf] = one.tile([P, HV, 4], BF16, name="vg", align_bytes=64)
+            cols = slice(HV * hf + c0, HV * hf + c1)
             if j in big:
-                other = big[j][:, :, c0:c1].rearrange("p t n -> p n t")
+                other = walk(big[j][:, :, cols])
             else:
-                other = ng[:].unsqueeze(1).to_broadcast([P, c1 - c0, 4])
+                other = ng[:].unsqueeze(1).unsqueeze(3).to_broadcast([P, (c1 - c0) // WI, 4, WI])
             nc.gpsimd.tensor_tensor(
-                out=vts[j][:, c0:c1], in0=soft[j][:, :, c0:c1].rearrange("p t n -> p n t"), in1=other, op=ALU.mult
+                out=vts[j, hf][:, c0:c1].rearrange("p (c i) t -> p c t i", i=WI),
+                in0=walk(soft[j][:, :, cols]), in1=other, op=ALU.mult,
             )
 
         def gain_pe(j, q):
@@ -310,83 +302,87 @@ def tile_tpvformersoftplusoccupancydecoder_d1p_kernel(
                     out=bank[:, P * t : P * (t + 1)], lhsT=dg[:, t, :], rhs=soft[j][:, t, P * q : P * (q + 1)],
                     start=True, stop=True,
                 )
-            return bank
 
         def weave(j, q):
             bank = held[j, "g", q][0]
-            if j not in vts:
-                vts[j] = vpool.tile([P, NV, 4], BF16, name="vw", align_bytes=64)
-            nc.scalar.copy(out=vts[j][:, P * q : P * (q + 1)], in_=bank[:].rearrange("p (t n) -> p n t", t=4))
+            hf, c0 = q // 2, P * (q % 2)
+            if (j, hf) not in vts:
+                vts[j, hf] = vpool.tile([P, HV, 4], BF16, name="vv", align_bytes=64)
+            nc.scalar.copy(out=vts[j, hf][:, c0 : c0 + P], in_=bank[:].rearrange("p (t n) -> p n t", t=4))
             release((j, "g", q))
 
-        def gain_s(j, q):
-            cols = slice(P * q, P * (q + 1))
-            if j not in vts:
-                vts[j] = vpool.tile([P, NV, 4], BF16, name="vw", align_bytes=64)
-            flat = grp.tile([P, 4, P], BF16, name="flat")
-            for t in range(4):
-                nc.scalar.activation(out=flat[:, t, :], in_=soft[j][:, t, cols], func=AF.Copy, scale=ng[:, t : t + 1])
-            nc.scalar.copy(out=vts[j][:, cols], in_=flat[:].rearrange("p t n -> p n t"))
+        def quant_v(j, hf):
+            vc = vpool.tile([P, HV], U32, name="vc", align_bytes=64)
+            vs = vpool.tile([P, HV], U8, name="vs", align_bytes=64)
+            vqs[j, hf] = (vc, vs)
+            quant(vc[:], vs[:], vts[j, hf][:])
 
-        def lower2(j, t0=0, t1=4):
-            e = soft[j][:, t0:t1].rearrange("p t n -> p (t n)")
-            nc.vector.tensor_tensor(out=e, in0=e, in1=nsum[j][:, t0:t1].rearrange("p t n -> p (t n)"), op=ALU.min)
-
-        def quant_v(j, c0=0, c1=NV):
-            if c0 == 0:
-                vc = vpool.tile([P, NV], U32, name="vc", align_bytes=64)
-                vs = vpool.tile([P, NV], U8, name="vs", align_bytes=64)
-                vqs[j] = (vc, vs)
-            vc, vs = vqs[j]
-            quant(vc[:, c0:c1], vs[:, c0:c1], vts[j][:, c0:c1])
-
-        def decode(j, halves=(0, 1)):
-            vc, vs = vqs[j]
-            for zp in halves:
-                ob = take((j, "o", zp))
-                for zz in range(2):
-                    cols = slice(P * (2 * zp + zz), P * (2 * zp + zz + 1))
-                    nc.tensor.matmul_mx(
-                        out=ob[:, E * zz : E * (zz + 1)],
-                        lhsT=vc[:, cols].bitcast(FP8X4), lhsT_scale=vs[:, cols],
-                        rhs=w2w[:].bitcast(FP8X4), rhs_scale=s2w[:],
-                        start=True, stop=True,
-                    )
-
-        out_v = out.rearrange("(j a) w z e -> (a w) j z e", a=4)
-        ots = {}
-
-        def finish_z(j, z, eng):
-            zp, zz = divmod(z, 2)
-            ot = ots[j]
-            nc.vector.tensor_tensor(
-                out=ot[:, z, :], in0=held[j, "o", zp][0][:, E * zz : E * (zz + 1)], in1=b2t[:], op=ALU.add
-            )
-            if zz == 1:
-                release((j, "o", zp))
-            eng.dma_start(out=out_v[:, j, z], in_=ot[:, z, :])
-
-        def finish(j, split=False, halves=(0, 1)):
-            for zp in halves:
-                if zp == 0:
-                    ots[j] = opool.tile([P, Z, E], F32, name="ot")
-                ot = ots[j]
-                nc.vector.tensor_tensor(
-                    out=ot[:, 2 * zp : 2 * zp + 2, :], in0=held[j, "o", zp][0][:].rearrange("p (z e) -> p z e", z=2),
-                    in1=b2t[:].unsqueeze(1).to_broadcast([P, 2, E]), op=ALU.add,
+        def decode(j, hf):
+            vc, vs = vqs[j, hf]
+            ob = take((j, "o", hf))
+            for zz in range(2):
+                cols = slice(P * zz, P * (zz + 1))
+                nc.tensor.matmul_mx(
+                    out=ob[:, E * zz : E * (zz + 1)],
+                    lhsT=vc[:, cols].bitcast(FP8X4), lhsT_scale=vs[:, cols],
+                    rhs=w2w[:].bitcast(FP8X4), rhs_scale=s2w[:],
+                    start=True, stop=True,
                 )
-                release((j, "o", zp))
-                if split:
-                    nc.sync.dma_start(out=out_v[:, j, 2 * zp : 2 * zp + 2], in_=ot[:, 2 * zp : 2 * zp + 2, :])
-                elif zp == 1:
-                    nc.sync.dma_start(out=out_v[:, j], in_=ot[:])
+
+        def finish(j, hf):
+            ot = opool.tile([P, 2, E], F32, name="ot")
+            nc.vector.tensor_tensor(
+                out=ot[:], in0=held[j, "o", hf][0][:].rearrange("p (z e) -> p z e", z=2),
+                in1=b2t[:].unsqueeze(1).to_broadcast([P, 2, E]), op=ALU.add,
+            )
+            release((j, "o", hf))
+            nc.sync.dma_start(out=out_v[:, j, 2 * hf : 2 * hf + 2], in_=ot[:])
+
+        def finish_z(j, hf):
+            ot = opool.tile([P, 2, E], F32, name="ot")
+            for zz, eng in enumerate((nc.scalar, nc.sync)):
+                nc.vector.tensor_tensor(
+                    out=ot[:, zz, :], in0=held[j, "o", hf][0][:, E * zz : E * (zz + 1)], in1=b2t[:], op=ALU.add
+                )
+                eng.dma_start(out=out_v[:, j, 2 * hf + zz], in_=ot[:, zz, :])
+            release((j, "o", hf))
+
+        def place_g():
+            bank = take("g")
+            nc.tensor.matmul(out=bank[:, 0:4], lhsT=ident[:], rhs=ng[:], start=True, stop=True)
 
 
+        nc.vector.memset(dum[:], 0.0)
+        nc.vector.memset(s1raw[:].bitcast(I32), 0)
+        nc.vector.memset(cqs[:].bitcast(I32), 0)
+        nc.vector.memset(bqs[:].bitcast(I32), 0)
+        nc.vector.memset(s2w[:].bitcast(I32), 0)
+        nc.sync.dma_start(out=xc[:], in_=twz.rearrange("w z d -> (w z) d"))
+        nc.scalar.dma_start(out=sc[:], in_=scale_v)
+        nc.sync.dma_start(out=byt0[:], in_=bytes_v[:, 0:NB0, :])
+        nc.scalar.dma_start(out=xb[:], in_=tzh.rearrange("z h d -> (z h) d"))
+        nc.sync.dma_start(out=w1raw[:], in_=w1_words[0].rearrange("p n t -> p (n t)").bitcast(I32))
+        for q in range(4):
+            load_rows(s1raw, w1_scales, q, nc.sync)
+        nc.scalar.activation(out=dum[:], in_=dum[:], func=AF.Sigmoid)
+        nc.sync.dma_start(out=b1t[:], in_=b1.rearrange("(p t) -> p t", t=4))
+        nc.sync.dma_start(out=byt1[:], in_=bytes_v[:, NB0:NU, :])
+        nc.sync.dma_start(out=gt[:], in_=g.rearrange("(p t) -> p t", t=4))
+        make_identity(nc, ident[:])
+        nc.sync.dma_start(out=w2w[:], in_=w2_words[0].rearrange("p n t -> p (n t)").bitcast(I32))
+        for q in range(4):
+            load_rows(s2w, w2_scales, q, nc.sync)
+        nc.sync.dma_start(out=b2t[:], in_=b2.partition_broadcast(P))
+
+        warm_up(3)
         scaled(nc.vector, nxc[:], xc[:], -1.0)
-        scaled(nc.vector, nxb[:], xb[:], -1.0)
         scaled(nc.vector, nsc[:], sc[:], -1.0)
-        warm_up(2)
         c_bank = turn("c", [nxc])
+        for q in range(4):
+            widen(0, q, q < 2)
+        scaled(nc.vector, nxb[:], xb[:], -1.0)
+        warm_up(1)
+        turn(("a", 0), [xa[0]])
         b_bank = turn("b", [nxb])
         gc = grp.tile([P, P, 4], BF16, name="gc", align_bytes=64)
         nc.scalar.copy(
@@ -394,205 +390,242 @@ def tile_tpvformersoftplusoccupancydecoder_d1p_kernel(
             in_=c_bank[:, 0:256].rearrange("p (u w z) -> p z w u", u=2, z=Z),
         )
         release("c")
-        for q in range(4):
-            widen(0, q, q < 2)
+        widen_v(1)
+        turn(("a", 1), [xa[1]])
+        warm_up(1)
+        nc.vector.tensor_copy(out=w1p[:], in_=w1raw[:].rearrange("p (m t) -> p t m", t=4))
+        copy_a(0, 1)
         gb = grp.tile([P, P, 4], BF16, name="gb", align_bytes=64)
         nc.scalar.copy(
             out=words_of(gb[:]).rearrange("p (j z a u) -> p j z a u", z=Z, a=4, u=2),
             in_=b_bank[:, 0:256].rearrange("p (u z j a) -> p j z a u", u=2, z=Z, a=4),
         )
         release("b")
-        warm_up(2)
-        turn(("a", 0), [xa[0]])
-        widen_s(1)
-        ga0 = copy_a(0, 1)
-        warm_up(1)
-        turn(("a", 1), [xa[1]])
-        warm_up(1)
+        copy_a(1, 1)
         quant(cq[:], cqs[:], gc[:])
-        nc.vector.tensor_copy(out=w1p[:], in_=w1raw[:].rearrange("p (m t) -> p t m", t=4))
-        spread_c()
-        quant(bq[:], bqs[:], gb[:])
         nc.vector.tensor_copy(out=s1p[:], in_=s1raw[:].rearrange("p (m t) -> p t m", t=4))
-        quant_a(ga0, 0, 1)
-        spread_b_bytes(1, 1)
-        widen_s(2)
-        ga1 = copy_a(1, 1)
-        widen_s(3)
+        spread_c()
+        quant_a(0, 1)
+        quant(bq[:], bqs[:], gb[:])
+        project(0, 0, False)
         bb = take("bb")
         for t in range(4):
             nc.tensor.matmul_mx(
-                out=bb[:, 64 * t : 64 * (t + 1)], lhsT=w1p[:, t, :].bitcast(FP8X4), lhsT_scale=s1p[:, t, :],
-                rhs=bq[:, 0:64].bitcast(FP8X4), rhs_scale=bqs[:, 0:64], start=True, stop=True,
+                out=bb[:, P * t : P * (t + 1)], lhsT=w1p[:, t, :].bitcast(FP8X4), lhsT_scale=s1p[:, t, :],
+                rhs=bq[:].bitcast(FP8X4), rhs_scale=bqs[:], start=True, stop=True,
             )
-        spread_b_scales(1, 1)
+        for t in range(1, 4):
+            project(0, t, False)
         scaled(nc.vector, nb1[:], b1t[:], -1.0)
-        spread_b(1, 1)
+        quant_a(1, 1)
+        spread_b_bytes(1, 1)
+        for j in range(2, 6):
+            widen_s(j)
         nc.vector.tensor_tensor(
-            out=bp[:], in0=bb[:, 0:256].rearrange("p (t r) -> p t r", t=4)[:, :, 0:16],
-            in1=nb1[:].unsqueeze(2).to_broadcast([P, 4, 16]), op=ALU.add,
+            out=bp[:], in0=bb[:].rearrange("p (t j r) -> p t j r", t=4, r=16)[:, :, 0:4, :],
+            in1=nb1[:].unsqueeze(2).unsqueeze(3).to_broadcast([P, 4, 4, 16]), op=ALU.add,
         )
         release("bb")
-        quant_a(ga1, 1, 1)
-        scaled(nc.vector, ng[:], gt[:], -1.0)
-        for t in range(4):
-            scaled(nc.gpsimd, dg[:, t, :], ident[:], ng[:, t : t + 1])
-        widen_s(4)
-        widen(5, 0, False)
-        widen(5, 1, False)
-        for t in range(4):
-            project2(0, t)
-            add_b(0, t)
-            sigm2(0, t, t + 1)
+
+        add_b(0, 0)
+        spread_b_scales(1, 1)
+        spread_b(1, 1)
+        clip(0, 0, 1)
+        add_b(0, 1)
         for t in range(4):
             project(1, t)
-            sigm(1, t)
-        widen(5, 2, True)
-        widen(5, 3, True)
-        scaled(nc.vector, gk[:], gt[:], 1.0 / KNEE)
-        spread_b_bytes(2, 6)
+        sigm2(0, 0, 1)
+        add_b(0, 2)
+        clip(0, 1, 2)
+        sigm(1, 0)
+        sigm2(0, 1, 2)
+        add_b(0, 3)
+        clip(0, 2, 3)
+        sigm(1, 1)
+        sigm2(0, 2, 3)
         widen_v(6)
-        spread_b_scales(2, 6)
-        widen_v(7)
-        spread_b(2, 2)
+        clip(0, 3, 4)
+        sigm(1, 2)
+        sigm2(0, 3, 4)
+        sigm(1, 3)
         turn(("a", 2), [xa[2], xa[3]])
         turn(("a", 4), [xa[4], xa[5]])
+        widen_v(7)
         turn(("a", 6), [xa[6], xa[7]])
-        ga2 = copy_a(2, 2, True)
+        scaled(nc.vector, gk[:], gt[:], 1.0 / KNEE)
+        scaled(nc.vector, ng[:], gt[:], -1.0)
+        spread_b_bytes(4, 4)
+        copy_a(2, 2, True)
+        spread_b_scales(4, 4)
+        quant_a(2, 2)
+        for t in range(2):
+            project(3, t, False)
+        for t in range(4):
+            factor(0, t)
+        copy_a(4, 2, True)
+        project(3, 2, False)
         spread_b(4, 2)
-        quant_a(ga2, 2, 2)
-        ga4 = copy_a(4, 2, True)
-        loga(0, 0, 2)
-        loga(0, 2, 4)
+        quant_a(4, 2)
+        loga(0, 0, 4, 0, HV)
         loga(1, 0, 2)
         loga(1, 2, 4)
-        project(2, 0)
-        project(2, 1)
-        quant_a(ga4, 4, 2)
-        ga6 = copy_a(6, 2, True)
-        project(2, 2)
-        project(2, 3)
-        lower2(0, 0, 2)
-        quant_a(ga6, 6, 2)
-        lower2(0, 2, 4)
-        product_tile(0, "vta")
-        combine_g(0, 160, NV)
-        for t in range(4):
-            lower(1, t)
-            project(3, t)
-        for t in range(4):
-            sigm(2, t)
-            knee(2, t)
-        for t in range(4):
-            project(4, t)
-        sigm(3, 0, True)
-        sigm(3, 1, True)
-        for j, t in [(3, 2), (3, 3), (4, 0), (4, 1), (4, 2), (4, 3)]:
-            sigm(j, t)
-        combine(0, 0, 160)
-        spread_b(6, 2)
-        quant_v(0)
-        decode(0)
-        product_tile(1, "vtb")
-        combine(1)
-        finish(0, False, (0,))
-        quant_v(1)
-        finish(0, False, (1,))
-        decode(1)
-        loga(4, 0, 2)
-        loga(4, 2, 4)
-        loga(3, 2, 4)
-        loga(3, 0, 2)
-        loga(2)
-        finish(1, False, (0,))
-        for t in range(4):
-            lower(4, t)
-            if t == 0:
-                project(3, 0)
-        product_tile(4, "vta")
-        combine_g(4, 336, NV)
-        project(3, 1)
-        for t in range(2):
-            project(5, t)
-        finish(1, False, (1,))
+        loga(0, 0, 4, HV, NV)
+        product_g(0, 0)
+        add_b(3, 0)
+        project(3, 3, False)
+        add_b(3, 1)
+        project(4, 0)
+        add_b(3, 2)
+        project(4, 1)
+        add_b(3, 3)
+        project(2, 0, False)
+        copy_a(6, 2, True)
+        project(2, 1, False)
+        lower(1, 0)
+        project(4, 2)
+        clip(3, 0, 4)
+        quant_v(0, 0)
+        product_g(0, 1)
+        lower(1, 1)
+        place_g()
+        lower(1, 2)
+        project(4, 3)
+        lower(1, 3)
+        decode(0, 0)
+        add_b(2, 0)
+        project(5, 0)
+        add_b(2, 1)
+        project(2, 2, False)
+        finish(0, 0)
+        project(2, 3, False)
+
+        sigm2(3, 0, 4)
+        sigm(4, 0, True)
+        sigm(4, 1, True)
+        sigm(4, 2, True)
+        project(5, 1)
         project(5, 2)
         project(5, 3)
-        for t in (2, 3, 0, 1):
-            lower(3, t)
-        project(6, 0)
-        project(6, 1)
-        combine(4, 0, 336)
-        gain(2, 0, 0, 288)
-        quant_v(4)
-        product_tile(3, "vta")
-        combine_g(3, 288, NV)
-        decode(4)
-        for t in range(4):
-            sigm(5, t)
-            knee(5, t)
-        for j, t in [(6, 2), (6, 3), (7, 0), (7, 1)]:
-            project(j, t)
-        sigm(6, 0, True)
-        sigm(6, 1, True)
-        project(7, 2)
-        project(7, 3)
-        for j, t in [(6, 2), (6, 3), (7, 0), (7, 1), (7, 2), (7, 3)]:
+        for j, t in [(4, 3), (5, 0), (5, 1), (5, 2), (5, 3)]:
             sigm(j, t)
-        finish(4)
-        combine(3, 0, 288)
-        for t in range(1, 4):
-            gain(2, t, 0, 288)
-        quant_v(3)
-        decode(3)
-        product_tile(2, "vtb")
-        combine(2, 0, 288)
+        quant_a(6, 2)
         for t in range(4):
-            gain(2, t, 288, NV)
-        combine_g(2, 288, NV)
-        finish(3, True)
-        project(6, 0)
-        project(6, 1)
-        loga(7, 0, 2)
-        loga(7, 2, 4)
+            factor(3, t)
+        quant_v(0, 1)
+        product_g(1, 0)
+        product_v(1, 1)
+        add_b(2, 2)
+        decode(0, 1)
+        add_b(2, 3)
+        finish(0, 1)
+        spread_b(6, 2)
+        clip(2, 0, 4)
+        quant_v(1, 1)
+        decode(1, 1)
+        quant_v(1, 0)
+        decode(1, 0)
+        for t in range(4):
+            scaled(nc.vector, dg[:, t, :], ident[:], ng[:, t : t + 1])
+        finish(1, 1)
+        project(4, 0)
+        finish(1, 0)
+        project(4, 1)
+        loga(3, 0, 4, 0, HV)
         loga(5, 0, 2)
         loga(5, 2, 4)
-        loga(6, 2, 4)
+        loga(4, 0, 2)
+        loga(4, 2, 4)
+        loga(3, 0, 4, HV, NV)
+        product_g(3, 0)
+        for t in range(4):
+            lower(5, t)
+        project(4, 2)
+        for t in range(3):
+            project(6, t)
+        factor(2, 0)
+        factor(2, 1)
+        quant_v(3, 0)
+        product_g(5, 0)
+        lower(4, 0)
+        decode(3, 0)
+        lower(4, 1)
+        project(6, 3)
+        lower(4, 3)
+        project(7, 0)
+        lower(4, 2)
+        product_v(5, 1)
+        factor(2, 2)
+        factor(2, 3)
+        quant_v(5, 1)
+        decode(5, 1)
+        quant_v(5, 0)
+        product_g(3, 1)
+        finish(3, 0)
+        decode(5, 0)
+        product_v(4, 1)
+
+        sigm2(2, 0, 4)
+        sigm(6, 0, True)
+        sigm(6, 1, True)
+        sigm(6, 2, True)
+        project(7, 1)
+        project(7, 2)
+        project(7, 3)
+        for j, t in [(6, 3), (7, 0), (7, 1), (7, 2), (7, 3)]:
+            sigm(j, t)
+        finish(5, 1)
+        finish(5, 0)
+        quant_v(4, 1)
+        decode(4, 1)
+        quant_v(3, 1)
+        decode(3, 1)
+        product_g(4, 0, 128, HV)
+        product_v(4, 0, 0, 128)
+        finish(4, 1)
+        finish(3, 1)
+        project(6, 0)
+        quant_v(4, 0)
+        decode(4, 0)
+        loga(2, 0, 4, 0, HV)
+        loga(7, 0, 2)
+        loga(7, 2, 4)
         loga(6, 0, 2)
+        loga(6, 2, 4)
+        loga(2, 0, 4, HV, NV)
+        product_g(2, 0)
+        finish(4, 0)
+        project(6, 1)
         for t in range(4):
             lower(7, t)
-        for q in range(3):
-            gain_pe(7, q)
-        quant_v(2)
-        for t in range(4):
-            gain(5, t)
-        product_tile(5, "vta")
-        combine_g(5, 288, NV)
-        for t in range(2, 4):
+        project(6, 2)
+        gain_pe(7, 0)
+        gain_pe(7, 1)
+        quant_v(2, 0)
+        product_g(7, 1)
+        decode(2, 0)
+        for t in (0, 1, 3, 2):
             lower(6, t)
-        decode(2)
-        gain_pe(7, 3)
-        for t in range(2):
-            lower(6, t)
-        finish(2, True)
-        for q in range(4):
-            weave(7, q)
         gain_pe(6, 0)
         gain_pe(6, 1)
-        quant_v(7)
-        decode(7)
-        gain_pe(6, 2)
-        gain_s(6, 3)
+        weave(7, 0)
+        weave(7, 1)
+        finish(2, 0)
+        quant_v(7, 0)
+        decode(7, 0)
+        quant_v(7, 1)
+        product_g(2, 1)
+        decode(7, 1)
+        product_v(6, 1)
         weave(6, 0)
         weave(6, 1)
-        weave(6, 2)
-        combine(5, 0, 288)
-        finish(7, True, (0,))
-        quant_v(5)
-        decode(5)
-        finish(7, True, (1,))
-        quant_v(6)
-        decode(6)
-        finish(5, True)
-        finish(6, True, (0,))
-        finish_z(6, 2, nc.scalar)
-        finish_z(6, 3, nc.sync)
+        finish(7, 0)
+        finish(7, 1)
+        quant_v(6, 1)
+        decode(6, 1)
+        quant_v(6, 0)
+        decode(6, 0)
+        quant_v(2, 1)
+        decode(2, 1)
+        finish(6, 1)
+        finish(6, 0)
+        finish_z(2, 1)

@@ -23,7 +23,7 @@ HV = 256
 KNEE = 16.0
 EPS = 2.0 ** -60
 WI = 4
-NB0 = 4
+NB0 = 2
 
 
 def tile_tpvformersoftplusoccupancydecoder_d1p_kernel(
@@ -35,7 +35,7 @@ def tile_tpvformersoftplusoccupancydecoder_d1p_kernel(
         grp = ctx.enter_context(tc.tile_pool(name="grp", bufs=2))
         vpool = ctx.enter_context(tc.tile_pool(name="vpool", bufs=4))
         one = ctx.enter_context(tc.tile_pool(name="one", bufs=1))
-        opool = ctx.enter_context(tc.tile_pool(name="opool", bufs=4))
+        opool = ctx.enter_context(tc.tile_pool(name="opool", bufs=8))
         psum = ctx.enter_context(tc.psum_pool(name="psum", bufs=1))
         ctx.enter_context(tc.manual_schedule())
 
@@ -74,6 +74,7 @@ def tile_tpvformersoftplusoccupancydecoder_d1p_kernel(
         as_ = keep.tile([P, NU * P], U8, name="as_", align_bytes=64)
         bp = keep.tile([P, 4, 4, 16], F32, name="bp")
         dg = keep.tile([P, 4, P], F32, name="dg")
+        zero = keep.tile([P, P], F32, name="zero")
         dum = keep.tile([P, 1], F32, name="dum")
         soft = [keep.tile([P, 4, NV], F32, name="soft%d" % j) for j in range(NU)]
         big, nsum = {}, {}
@@ -130,7 +131,7 @@ def tile_tpvformersoftplusoccupancydecoder_d1p_kernel(
         def warm_up(count):
             bank = take("warm")
             for i in range(count):
-                nc.tensor.matmul(out=bank[:, P * i : P * (i + 1)], lhsT=ident[:], rhs=ident[:], start=True, stop=True)
+                nc.tensor.matmul(out=bank[:, P * i : P * (i + 1)], lhsT=zero[:], rhs=zero[:], start=True, stop=True)
             release("warm")
 
         def words_of(tile):
@@ -200,6 +201,12 @@ def tile_tpvformersoftplusoccupancydecoder_d1p_kernel(
             if with_b:
                 nc.tensor.matmul_mx(out=bank[:], lhsT=lhs, lhsT_scale=lhs_s, rhs=brc[:, ucols].bitcast(FP8X4), rhs_scale=brs[:, ucols], start=False, stop=True)
 
+        def bias_b(j0, j1):
+            nc.vector.tensor_tensor(
+                out=bp[:, :, j0:j1, :], in0=held["bb"][0][:].rearrange("p (t j r) -> p t j r", t=4, r=16)[:, :, j0:j1, :],
+                in1=nb1[:].unsqueeze(2).unsqueeze(3).to_broadcast([P, 4, j1 - j0, 16]), op=ALU.add,
+            )
+
         def add_b(j, t):
             bank = held[j, t][0]
             if j not in nsum:
@@ -225,6 +232,13 @@ def tile_tpvformersoftplusoccupancydecoder_d1p_kernel(
         def sigm2(j, t0, t1):
             e = soft[j][:, t0:t1, :]
             nc.scalar.activation(out=e, in_=e, func=AF.Sigmoid)
+
+        def sigm3(j, t):
+            nc.scalar.activation(out=soft[j][:, t, :], in_=nsum[j][:, t, :], func=AF.Sigmoid)
+
+        def floor(j, hf):
+            e = soft[j][:, :, HV * hf : HV * (hf + 1)]
+            nc.vector.tensor_scalar(out=e, in0=e, scalar1=-KNEE, scalar2=None, op0=ALU.max)
 
         def sigm(j, t, last=False):
             nc.scalar.activation(out=soft[j][:, t, :], in_=held[j, t][0][:], func=AF.Sigmoid, bias=nb1[:, t : t + 1])
@@ -311,6 +325,17 @@ def tile_tpvformersoftplusoccupancydecoder_d1p_kernel(
             nc.scalar.copy(out=vts[j, hf][:, c0 : c0 + P], in_=bank[:].rearrange("p (t n) -> p n t", t=4))
             release((j, "g", q))
 
+        def gain_s(j, q):
+            hf, c0 = q // 2, P * (q % 2)
+            if (j, hf) not in vts:
+                vts[j, hf] = vpool.tile([P, HV, 4], BF16, name="vv", align_bytes=64)
+            flat = grp.tile([P, 4, P], BF16, name="flat")
+            for t in range(4):
+                nc.scalar.activation(
+                    out=flat[:, t, :], in_=soft[j][:, t, P * q : P * (q + 1)], func=AF.Copy, scale=ng[:, t : t + 1]
+                )
+            nc.scalar.copy(out=vts[j, hf][:, c0 : c0 + P], in_=flat[:].rearrange("p t n -> p n t"))
+
         def quant_v(j, hf):
             vc = vpool.tile([P, HV], U32, name="vc", align_bytes=64)
             vs = vpool.tile([P, HV], U8, name="vs", align_bytes=64)
@@ -352,15 +377,16 @@ def tile_tpvformersoftplusoccupancydecoder_d1p_kernel(
             nc.tensor.matmul(out=bank[:, 0:4], lhsT=ident[:], rhs=ng[:], start=True, stop=True)
 
 
+        nc.vector.memset(zero[:], 0.0)
         nc.vector.memset(dum[:], 0.0)
         nc.vector.memset(s1raw[:].bitcast(I32), 0)
         nc.vector.memset(cqs[:].bitcast(I32), 0)
         nc.vector.memset(bqs[:].bitcast(I32), 0)
         nc.vector.memset(s2w[:].bitcast(I32), 0)
         nc.sync.dma_start(out=xc[:], in_=twz.rearrange("w z d -> (w z) d"))
-        nc.scalar.dma_start(out=sc[:], in_=scale_v)
-        nc.sync.dma_start(out=byt0[:], in_=bytes_v[:, 0:NB0, :])
         nc.scalar.dma_start(out=xb[:], in_=tzh.rearrange("z h d -> (z h) d"))
+        nc.sync.dma_start(out=byt0[:], in_=bytes_v[:, 0:NB0, :])
+        nc.scalar.dma_start(out=sc[:], in_=scale_v)
         nc.sync.dma_start(out=w1raw[:], in_=w1_words[0].rearrange("p n t -> p (n t)").bitcast(I32))
         for q in range(4):
             load_rows(s1raw, w1_scales, q, nc.sync)
@@ -374,16 +400,16 @@ def tile_tpvformersoftplusoccupancydecoder_d1p_kernel(
             load_rows(s2w, w2_scales, q, nc.sync)
         nc.sync.dma_start(out=b2t[:], in_=b2.partition_broadcast(P))
 
-        warm_up(3)
+        warm_up(4)
         scaled(nc.vector, nxc[:], xc[:], -1.0)
+        scaled(nc.vector, nxb[:], xb[:], -1.0)
         scaled(nc.vector, nsc[:], sc[:], -1.0)
         c_bank = turn("c", [nxc])
+        b_bank = turn("b", [nxb])
         for q in range(4):
             widen(0, q, q < 2)
-        scaled(nc.vector, nxb[:], xb[:], -1.0)
         warm_up(1)
         turn(("a", 0), [xa[0]])
-        b_bank = turn("b", [nxb])
         gc = grp.tile([P, P, 4], BF16, name="gc", align_bytes=64)
         nc.scalar.copy(
             out=words_of(gc[:]).rearrange("p (z w u) -> p z w u", z=Z, u=2),
@@ -394,177 +420,176 @@ def tile_tpvformersoftplusoccupancydecoder_d1p_kernel(
         turn(("a", 1), [xa[1]])
         warm_up(1)
         nc.vector.tensor_copy(out=w1p[:], in_=w1raw[:].rearrange("p (m t) -> p t m", t=4))
-        copy_a(0, 1)
         gb = grp.tile([P, P, 4], BF16, name="gb", align_bytes=64)
         nc.scalar.copy(
             out=words_of(gb[:]).rearrange("p (j z a u) -> p j z a u", z=Z, a=4, u=2),
             in_=b_bank[:, 0:256].rearrange("p (u z j a) -> p j z a u", u=2, z=Z, a=4),
         )
         release("b")
+        copy_a(0, 1)
         copy_a(1, 1)
         quant(cq[:], cqs[:], gc[:])
         nc.vector.tensor_copy(out=s1p[:], in_=s1raw[:].rearrange("p (m t) -> p t m", t=4))
+        quant(bq[:], bqs[:], gb[:])
         spread_c()
         quant_a(0, 1)
-        quant(bq[:], bqs[:], gb[:])
-        project(0, 0, False)
         bb = take("bb")
         for t in range(4):
             nc.tensor.matmul_mx(
                 out=bb[:, P * t : P * (t + 1)], lhsT=w1p[:, t, :].bitcast(FP8X4), lhsT_scale=s1p[:, t, :],
                 rhs=bq[:].bitcast(FP8X4), rhs_scale=bqs[:], start=True, stop=True,
             )
-        for t in range(1, 4):
+        for t in range(4):
             project(0, t, False)
         scaled(nc.vector, nb1[:], b1t[:], -1.0)
-        quant_a(1, 1)
         spread_b_bytes(1, 1)
+        bias_b(0, 1)
+        quant_a(1, 1)
+        spread_b_scales(1, 1)
         for j in range(2, 6):
             widen_s(j)
-        nc.vector.tensor_tensor(
-            out=bp[:], in0=bb[:].rearrange("p (t j r) -> p t j r", t=4, r=16)[:, :, 0:4, :],
-            in1=nb1[:].unsqueeze(2).unsqueeze(3).to_broadcast([P, 4, 4, 16]), op=ALU.add,
-        )
-        release("bb")
 
         add_b(0, 0)
-        spread_b_scales(1, 1)
-        spread_b(1, 1)
-        clip(0, 0, 1)
+        sigm3(0, 0)
         add_b(0, 1)
+        sigm3(0, 1)
+        spread_b(1, 1)
         for t in range(4):
             project(1, t)
-        sigm2(0, 0, 1)
         add_b(0, 2)
-        clip(0, 1, 2)
-        sigm(1, 0)
-        sigm2(0, 1, 2)
+        sigm3(0, 2)
         add_b(0, 3)
-        clip(0, 2, 3)
-        sigm(1, 1)
-        sigm2(0, 2, 3)
-        widen_v(6)
-        clip(0, 3, 4)
-        sigm(1, 2)
-        sigm2(0, 3, 4)
-        sigm(1, 3)
+        sigm3(0, 3)
+        bias_b(2, 4)
+        release("bb")
+        for t in range(4):
+            sigm(1, t)
         turn(("a", 2), [xa[2], xa[3]])
         turn(("a", 4), [xa[4], xa[5]])
+        widen_v(6)
         widen_v(7)
         turn(("a", 6), [xa[6], xa[7]])
+        warm_up(1)
         scaled(nc.vector, gk[:], gt[:], 1.0 / KNEE)
         scaled(nc.vector, ng[:], gt[:], -1.0)
         spread_b_bytes(4, 4)
-        copy_a(2, 2, True)
+        for t in range(4):
+            factor(0, t)
         spread_b_scales(4, 4)
+        spread_b(4, 2)
+        copy_a(2, 2, True)
+        spread_b(6, 2)
         quant_a(2, 2)
         for t in range(2):
             project(3, t, False)
-        for t in range(4):
-            factor(0, t)
         copy_a(4, 2, True)
         project(3, 2, False)
-        spread_b(4, 2)
+        for t in range(4):
+            scaled(nc.vector, dg[:, t, :], ident[:], ng[:, t : t + 1])
         quant_a(4, 2)
+        copy_a(6, 2, True)
+        project(3, 3, False)
         loga(0, 0, 4, 0, HV)
         loga(1, 0, 2)
         loga(1, 2, 4)
         loga(0, 0, 4, HV, NV)
+        floor(0, 0)
         product_g(0, 0)
         add_b(3, 0)
-        project(3, 3, False)
-        add_b(3, 1)
         project(4, 0)
-        add_b(3, 2)
+        add_b(3, 1)
         project(4, 1)
-        add_b(3, 3)
+        add_b(3, 2)
         project(2, 0, False)
-        copy_a(6, 2, True)
-        project(2, 1, False)
-        lower(1, 0)
+        add_b(3, 3)
         project(4, 2)
+        lower(1, 0)
+        project(2, 1, False)
+        lower(1, 1)
+        project(2, 2, False)
         clip(3, 0, 4)
+        floor(0, 1)
         quant_v(0, 0)
         product_g(0, 1)
-        lower(1, 1)
+
+        sigm(4, 0, True)
+        project(4, 3)
+        sigm(4, 1, True)
+        project(5, 0)
+        sigm2(3, 0, 4)
+        add_b(2, 0)
+        project(2, 3, False)
+        add_b(2, 1)
+        decode(0, 0)
+        add_b(2, 2)
         place_g()
         lower(1, 2)
-        project(4, 3)
-        lower(1, 3)
-        decode(0, 0)
-        add_b(2, 0)
-        project(5, 0)
-        add_b(2, 1)
-        project(2, 2, False)
-        finish(0, 0)
-        project(2, 3, False)
-
-        sigm2(3, 0, 4)
-        sigm(4, 0, True)
-        sigm(4, 1, True)
-        sigm(4, 2, True)
         project(5, 1)
+        lower(1, 3)
         project(5, 2)
-        project(5, 3)
-        for j, t in [(4, 3), (5, 0), (5, 1), (5, 2), (5, 3)]:
-            sigm(j, t)
-        quant_a(6, 2)
-        for t in range(4):
-            factor(3, t)
-        quant_v(0, 1)
-        product_g(1, 0)
-        product_v(1, 1)
-        add_b(2, 2)
-        decode(0, 1)
         add_b(2, 3)
-        finish(0, 1)
-        spread_b(6, 2)
+        sigm(4, 2, True)
+        project(5, 3)
+        for j, t in [(4, 3), (5, 0), (5, 1), (5, 2)]:
+            sigm(j, t)
         clip(2, 0, 4)
+        quant_a(6, 2)
+        quant_v(0, 1)
+        product_g(1, 0, 64, HV)
+        decode(0, 1)
+        sigm2(2, 0, 4)
+        sigm(5, 3)
+        finish(0, 0)
+        project(4, 0)
+        product_v(1, 1)
+        finish(0, 1)
+        product_v(1, 0, 0, 64)
         quant_v(1, 1)
         decode(1, 1)
-        quant_v(1, 0)
-        decode(1, 0)
         for t in range(4):
-            scaled(nc.vector, dg[:, t, :], ident[:], ng[:, t : t + 1])
-        finish(1, 1)
-        project(4, 0)
-        finish(1, 0)
-        project(4, 1)
+            factor(3, t)
+        for t in range(4):
+            factor(2, t)
+        quant_v(1, 0)
         loga(3, 0, 4, 0, HV)
         loga(5, 0, 2)
         loga(5, 2, 4)
+        loga(3, 0, 4, HV, NV)
         loga(4, 0, 2)
         loga(4, 2, 4)
-        loga(3, 0, 4, HV, NV)
+        loga(2, 0, 4, 0, HV)
+        loga(2, 0, 4, HV, NV)
         product_g(3, 0)
-        for t in range(4):
-            lower(5, t)
+        finish(1, 1)
+        decode(1, 0)
+        lower(5, 0)
+        project(4, 1)
+        finish(1, 0)
         project(4, 2)
-        for t in range(3):
-            project(6, t)
-        factor(2, 0)
-        factor(2, 1)
+        lower(5, 1)
+        project(6, 0)
+        lower(5, 2)
+        project(6, 1)
+        lower(5, 3)
         quant_v(3, 0)
-        product_g(5, 0)
-        lower(4, 0)
-        decode(3, 0)
-        lower(4, 1)
-        project(6, 3)
-        lower(4, 3)
-        project(7, 0)
-        lower(4, 2)
-        product_v(5, 1)
-        factor(2, 2)
-        factor(2, 3)
-        quant_v(5, 1)
-        decode(5, 1)
-        quant_v(5, 0)
         product_g(3, 1)
-        finish(3, 0)
+        decode(3, 0)
+        product_v(5, 0)
+        lower(4, 0)
+        lower(4, 1)
+        lower(4, 3)
+        lower(4, 2)
+        project(6, 2)
+        project(6, 3)
+        project(7, 0)
+        quant_v(5, 0)
         decode(5, 0)
-        product_v(4, 1)
+        quant_v(3, 1)
+        product_g(2, 0)
+        finish(3, 0)
+        decode(3, 1)
+        product_v(5, 1)
 
-        sigm2(2, 0, 4)
         sigm(6, 0, True)
         sigm(6, 1, True)
         sigm(6, 2, True)
@@ -573,59 +598,58 @@ def tile_tpvformersoftplusoccupancydecoder_d1p_kernel(
         project(7, 3)
         for j, t in [(6, 3), (7, 0), (7, 1), (7, 2), (7, 3)]:
             sigm(j, t)
-        finish(5, 1)
         finish(5, 0)
-        quant_v(4, 1)
-        decode(4, 1)
-        quant_v(3, 1)
-        decode(3, 1)
-        product_g(4, 0, 128, HV)
-        product_v(4, 0, 0, 128)
-        finish(4, 1)
         finish(3, 1)
-        project(6, 0)
-        quant_v(4, 0)
-        decode(4, 0)
-        loga(2, 0, 4, 0, HV)
-        loga(7, 0, 2)
-        loga(7, 2, 4)
-        loga(6, 0, 2)
-        loga(6, 2, 4)
-        loga(2, 0, 4, HV, NV)
-        product_g(2, 0)
-        finish(4, 0)
-        project(6, 1)
-        for t in range(4):
-            lower(7, t)
-        project(6, 2)
-        gain_pe(7, 0)
-        gain_pe(7, 1)
+        product_v(4, 0, 0, 128)
+        quant_v(5, 1)
+        decode(5, 1)
         quant_v(2, 0)
-        product_g(7, 1)
+        product_g(2, 1)
         decode(2, 0)
-        for t in (0, 1, 3, 2):
-            lower(6, t)
-        gain_pe(6, 0)
-        gain_pe(6, 1)
-        weave(7, 0)
-        weave(7, 1)
+        product_v(4, 0, 128, HV)
+        finish(5, 1)
+        project(6, 0)
+        product_v(4, 1)
         finish(2, 0)
+        project(6, 1)
+        quant_v(4, 0)
+        quant_v(4, 1)
+        quant_v(2, 1)
+        for j, t in [(7, 0), (7, 1), (7, 2), (7, 3), (6, 3), (6, 0), (6, 1), (6, 2)]:
+            loga(j, t, t + 1)
+        lower(7, 0)
+        project(6, 2)
+        lower(7, 1)
+        decode(4, 0)
+        lower(7, 2)
+        decode(4, 1)
+        lower(7, 3)
+        product_g(7, 0)
+        gain_pe(7, 2)
+        lower(6, 3)
+        gain_pe(7, 3)
+        lower(6, 0)
+        decode(2, 1)
+        lower(6, 1)
+        lower(6, 2)
+        gain_pe(6, 0)
+        weave(7, 2)
+        weave(7, 3)
+        finish(4, 0)
+        product_v(6, 1)
         quant_v(7, 0)
         decode(7, 0)
         quant_v(7, 1)
-        product_g(2, 1)
         decode(7, 1)
-        product_v(6, 1)
+        gain_s(6, 1)
         weave(6, 0)
-        weave(6, 1)
-        finish(7, 0)
-        finish(7, 1)
+        finish(4, 1)
         quant_v(6, 1)
         decode(6, 1)
+        finish(2, 1)
         quant_v(6, 0)
         decode(6, 0)
-        quant_v(2, 1)
-        decode(2, 1)
+        finish(7, 0)
+        finish(7, 1)
         finish(6, 1)
-        finish(6, 0)
-        finish_z(2, 1)
+        finish_z(6, 0)

@@ -60,6 +60,7 @@ def tile_tpvformersoftplusoccupancydecoder_d1p_kernel(
         nb1 = keep.tile([P, 4], F32, name="nb1")
         gk = keep.tile([P, 4], F32, name="gk")
         ng = keep.tile([P, 4], F32, name="ng")
+        ngw = keep.tile([P, 4, WI], F32, name="ngw")
         b2t = keep.tile([P, E], BF16, name="b2t")
         cq = keep.tile([P, P], I32, name="cq", align_bytes=64)
         cqs = keep.tile([P, P], U8, name="cqs", align_bytes=64)
@@ -282,15 +283,15 @@ def tile_tpvformersoftplusoccupancydecoder_d1p_kernel(
         def walk(ap):
             return ap.rearrange("p t (c i) -> p c t i", i=WI)
 
-        def product_v(j, hf, c0=0, c1=HV, psum_g=True):
+        def product_v(j, hf, c0=0, c1=HV):
             if (j, hf) not in vts:
                 vts[j, hf] = vpool.tile([P, HV, 4], BF16, name="vv", align_bytes=64)
             cols = slice(HV * hf + c0, HV * hf + c1)
             if j in big:
                 other = walk(big[j][:, :, cols])
             else:
-                gsrc = held["g"][0][:, 0:4] if psum_g else ng[:]
-                other = gsrc.unsqueeze(1).unsqueeze(3).to_broadcast([P, (c1 - c0) // WI, 4, WI])
+                gsrc = held["g"][0][:, 0 : 4 * WI].rearrange("p (t i) -> p t i", i=WI)
+                other = gsrc.unsqueeze(1).to_broadcast([P, (c1 - c0) // WI, 4, WI])
             nc.vector.tensor_tensor(
                 out=vts[j, hf][:, c0:c1].rearrange("p (c i) t -> p c t i", i=WI),
                 in0=walk(soft[j][:, :, cols]), in1=other, op=ALU.mult,
@@ -374,7 +375,9 @@ def tile_tpvformersoftplusoccupancydecoder_d1p_kernel(
 
         def place_g():
             bank = take("g")
-            nc.tensor.matmul(out=bank[:, 0:4], lhsT=ident[:], rhs=ng[:], start=True, stop=True)
+            nc.tensor.matmul(
+                out=bank[:, 0 : 4 * WI], lhsT=ident[:], rhs=ngw[:].rearrange("p t i -> p (t i)"), start=True, stop=True
+            )
 
 
         nc.vector.memset(zero[:], 0.0)
@@ -472,6 +475,7 @@ def tile_tpvformersoftplusoccupancydecoder_d1p_kernel(
         warm_up(1)
         scaled(nc.vector, gk[:], gt[:], 1.0 / KNEE)
         scaled(nc.vector, ng[:], gt[:], -1.0)
+        scaled(nc.vector, ngw[:], gt[:].unsqueeze(2).to_broadcast([P, 4, WI]), -1.0)
         spread_b_bytes(4, 4)
         for t in range(4):
             factor(0, t)

@@ -23,7 +23,7 @@ HV = 256
 KNEE = 16.0
 EPS = 2.0 ** -60
 WI = 4
-NB0 = 2
+NB0 = 4
 
 
 def tile_tpvformersoftplusoccupancydecoder_d1p_kernel(
@@ -62,6 +62,7 @@ def tile_tpvformersoftplusoccupancydecoder_d1p_kernel(
         ng = keep.tile([P, 4], F32, name="ng")
         ngw = keep.tile([P, 4, WI], F32, name="ngw")
         b2t = keep.tile([P, E], BF16, name="b2t")
+        b2c = [keep.tile([P, 1], BF16, name="b2c%d" % c) for c in range(2)]
         cq = keep.tile([P, P], I32, name="cq", align_bytes=64)
         cqs = keep.tile([P, P], U8, name="cqs", align_bytes=64)
         bq = keep.tile([P, P], I32, name="bq", align_bytes=64)
@@ -73,7 +74,7 @@ def tile_tpvformersoftplusoccupancydecoder_d1p_kernel(
         bs4 = keep.tile([P, P, 4], U8, name="bs4", align_bytes=64)
         ac = keep.tile([P, NU * P], U32, name="ac", align_bytes=64)
         as_ = keep.tile([P, NU * P], U8, name="as_", align_bytes=64)
-        bp = keep.tile([P, 4, 4, 16], F32, name="bp")
+        bp = keep.tile([P, 4, NU, 16], F32, name="bp")
         dg = keep.tile([P, 4, P], F32, name="dg")
         zero = keep.tile([P, P], F32, name="zero")
         dum = keep.tile([P, 1], F32, name="dum")
@@ -208,6 +209,53 @@ def tile_tpvformersoftplusoccupancydecoder_d1p_kernel(
                 in1=nb1[:].unsqueeze(2).unsqueeze(3).to_broadcast([P, 4, j1 - j0, 16]), op=ALU.add,
             )
 
+        def project_half(j, hf, tp, with_b):
+            bank = take((j, hf, tp))
+            acols = slice(P * j, P * (j + 1))
+            ccols = slice(HV * hf, HV * (hf + 1))
+            ucols = slice(NV * j + HV * hf, NV * j + HV * (hf + 1))
+            for s in range(2):
+                lhs, lhs_s = w1p[:, 2 * tp + s, :].bitcast(FP8X4), s1p[:, 2 * tp + s, :]
+                dst = bank[:, HV * s : HV * (s + 1)]
+                nc.tensor.matmul_mx(out=dst, lhsT=lhs, lhsT_scale=lhs_s, rhs=crc[:, ccols].bitcast(FP8X4), rhs_scale=crs[:, ccols], start=True, stop=False)
+                for z in range(2):
+                    nc.tensor.matmul_mx(
+                        out=dst[:, P * z : P * (z + 1)], lhsT=lhs, lhsT_scale=lhs_s,
+                        rhs=ac[:, acols].bitcast(FP8X4), rhs_scale=as_[:, acols], start=False, stop=z == 1 and not with_b,
+                    )
+                if with_b:
+                    nc.tensor.matmul_mx(out=dst, lhsT=lhs, lhsT_scale=lhs_s, rhs=brc[:, ucols].bitcast(FP8X4), rhs_scale=brs[:, ucols], start=False, stop=True)
+
+        def add_half(j, hf, tp):
+            bank = held[j, hf, tp][0]
+            if j not in nsum:
+                nsum[j] = keep.tile([P, 4, NV], F32, name="nsum%d" % j)
+            nc.vector.tensor_tensor(
+                out=nsum[j][:, 2 * tp : 2 * tp + 2, HV * hf : HV * (hf + 1)].rearrange("p s (r w) -> p s r w", w=W),
+                in0=bank[:].rearrange("p (s r w) -> p s r w", s=2, w=W),
+                in1=bp[:, 2 * tp : 2 * tp + 2, j, 8 * hf : 8 * hf + 8].unsqueeze(3).to_broadcast([P, 2, 8, W]),
+                op=ALU.add,
+            )
+            release((j, hf, tp))
+
+        def sigm_half(j, hf, t, last=False):
+            bank = held[j, hf, t // 2][0]
+            nc.scalar.activation(
+                out=soft[j][:, t, HV * hf : HV * (hf + 1)], in_=bank[:, HV * (t % 2) : HV * (t % 2 + 1)],
+                func=AF.Sigmoid, bias=nb1[:, t : t + 1],
+            )
+            if last:
+                release((j, hf, t // 2))
+
+        def lower_half(j, hf, t):
+            bank = held[j, hf, t // 2][0]
+            e = soft[j][:, t, HV * hf : HV * (hf + 1)]
+            nc.vector.scalar_tensor_tensor(
+                out=e, in0=bank[:, HV * (t % 2) : HV * (t % 2 + 1)], scalar=nb1[:, t : t + 1], in1=e, op0=ALU.add, op1=ALU.min
+            )
+            if t % 2 == 1:
+                release((j, hf, t // 2))
+
         def add_b(j, t):
             bank = held[j, t][0]
             if j not in nsum:
@@ -220,18 +268,19 @@ def tile_tpvformersoftplusoccupancydecoder_d1p_kernel(
             )
             release((j, t))
 
-        def clip(j, t0, t1):
+        def clip(j, t0, t1, c0=0, c1=NV):
             nc.vector.tensor_scalar(
-                out=soft[j][:, t0:t1, :], in0=nsum[j][:, t0:t1, :], scalar1=-KNEE, scalar2=None, op0=ALU.max
+                out=soft[j][:, t0:t1, c0:c1], in0=nsum[j][:, t0:t1, c0:c1], scalar1=-KNEE, scalar2=None, op0=ALU.max
             )
 
-        def factor(j, t):
-            big[j] = nsum[j]
-            e = nsum[j][:, t, :]
+        def factor(j, t, c0=0, c1=NV):
+            for hf in range(c0 // HV, c1 // HV):
+                big[j, hf] = nsum[j]
+            e = nsum[j][:, t, c0:c1]
             nc.vector.tensor_scalar(out=e, in0=e, scalar1=-KNEE, scalar2=gk[:, t : t + 1], op0=ALU.min, op1=ALU.mult)
 
-        def sigm2(j, t0, t1):
-            e = soft[j][:, t0:t1, :]
+        def sigm2(j, t0, t1, c0=0, c1=NV):
+            e = soft[j][:, t0:t1, c0:c1]
             nc.scalar.activation(out=e, in_=e, func=AF.Sigmoid)
 
         def sigm3(j, t):
@@ -287,8 +336,8 @@ def tile_tpvformersoftplusoccupancydecoder_d1p_kernel(
             if (j, hf) not in vts:
                 vts[j, hf] = vpool.tile([P, HV, 4], BF16, name="vv", align_bytes=64)
             cols = slice(HV * hf + c0, HV * hf + c1)
-            if j in big:
-                other = walk(big[j][:, :, cols])
+            if (j, hf) in big:
+                other = walk(big[j, hf][:, :, cols])
             else:
                 gsrc = held["g"][0][:, 0 : 4 * WI].rearrange("p (t i) -> p t i", i=WI)
                 other = gsrc.unsqueeze(1).to_broadcast([P, (c1 - c0) // WI, 4, WI])
@@ -301,8 +350,8 @@ def tile_tpvformersoftplusoccupancydecoder_d1p_kernel(
             if (j, hf) not in vts:
                 vts[j, hf] = one.tile([P, HV, 4], BF16, name="vg", align_bytes=64)
             cols = slice(HV * hf + c0, HV * hf + c1)
-            if j in big:
-                other = walk(big[j][:, :, cols])
+            if (j, hf) in big:
+                other = walk(big[j, hf][:, :, cols])
             else:
                 other = ng[:].unsqueeze(1).unsqueeze(3).to_broadcast([P, (c1 - c0) // WI, 4, WI])
             nc.gpsimd.tensor_tensor(
@@ -326,8 +375,10 @@ def tile_tpvformersoftplusoccupancydecoder_d1p_kernel(
             nc.scalar.copy(out=vts[j, hf][:, c0 : c0 + P], in_=bank[:].rearrange("p (t n) -> p n t", t=4))
             release((j, "g", q))
 
+        flats = {}
+
         def gain_s(j, q):
-            hf, c0 = q // 2, P * (q % 2)
+            hf = q // 2
             if (j, hf) not in vts:
                 vts[j, hf] = vpool.tile([P, HV, 4], BF16, name="vv", align_bytes=64)
             flat = grp.tile([P, 4, P], BF16, name="flat")
@@ -335,7 +386,11 @@ def tile_tpvformersoftplusoccupancydecoder_d1p_kernel(
                 nc.scalar.activation(
                     out=flat[:, t, :], in_=soft[j][:, t, P * q : P * (q + 1)], func=AF.Copy, scale=ng[:, t : t + 1]
                 )
-            nc.scalar.copy(out=vts[j, hf][:, c0 : c0 + P], in_=flat[:].rearrange("p t n -> p n t"))
+            flats[j, q] = flat
+
+        def weave_s(j, q):
+            hf, c0 = q // 2, P * (q % 2)
+            nc.scalar.copy(out=vts[j, hf][:, c0 : c0 + P], in_=flats[j, q][:].rearrange("p t n -> p n t"))
 
         def quant_v(j, hf):
             vc = vpool.tile([P, HV], U32, name="vc", align_bytes=64)
@@ -361,6 +416,43 @@ def tile_tpvformersoftplusoccupancydecoder_d1p_kernel(
                 out=ot[:], in0=held[j, "o", hf][0][:].rearrange("p (z e) -> p z e", z=2),
                 in1=b2t[:].unsqueeze(1).to_broadcast([P, 2, E]), op=ALU.add,
             )
+            release((j, "o", hf))
+            nc.sync.dma_start(out=out_v[:, j, 2 * hf : 2 * hf + 2], in_=ot[:])
+
+        turned = {}
+
+        def decode_t(j, hf):
+            vc, vs = vqs[j, hf]
+            ob = take((j, "t", hf))
+            for c in range(2):
+                cols = slice(P * c, P * (c + 1))
+                nc.tensor.matmul_mx(
+                    out=ob[:, HV * c : HV * (c + 1)],
+                    lhsT=w2w[:, cols].bitcast(FP8X4), lhsT_scale=s2w[:, cols],
+                    rhs=vc[:].bitcast(FP8X4), rhs_scale=vs[:],
+                    start=True, stop=True,
+                )
+
+        def bias_t(j, hf):
+            ob = held[j, "t", hf][0]
+            turned[j, hf] = grp.tile([P, 2, HV], F32, name="turned")
+            for c in range(2):
+                nc.scalar.activation(
+                    out=turned[j, hf][:, c, :], in_=ob[:, HV * c : HV * (c + 1)], func=AF.Identity, bias=b2c[c][:]
+                )
+            release((j, "t", hf))
+
+        def turn_back(j, hf):
+            ob = take((j, "o", hf))
+            for zz in range(2):
+                for c in range(2):
+                    nc.tensor.transpose(
+                        ob[:, E * zz + P * c : E * zz + P * (c + 1)], turned[j, hf][:, c, P * zz : P * (zz + 1)], ident[:]
+                    )
+
+        def finish_s(j, hf):
+            ot = opool.tile([P, 2, E], F32, name="ot")
+            nc.scalar.copy(out=ot[:].rearrange("p z e -> p (z e)"), in_=held[j, "o", hf][0][:])
             release((j, "o", hf))
             nc.sync.dma_start(out=out_v[:, j, 2 * hf : 2 * hf + 2], in_=ot[:])
 
@@ -402,6 +494,8 @@ def tile_tpvformersoftplusoccupancydecoder_d1p_kernel(
         for q in range(4):
             load_rows(s2w, w2_scales, q, nc.sync)
         nc.sync.dma_start(out=b2t[:], in_=b2.partition_broadcast(P))
+        for c in range(2):
+            nc.sync.dma_start(out=b2c[c][:], in_=b2[P * c : P * (c + 1)].rearrange("(p o) -> p o", o=1))
 
         warm_up(4)
         scaled(nc.vector, nxc[:], xc[:], -1.0)
@@ -423,6 +517,7 @@ def tile_tpvformersoftplusoccupancydecoder_d1p_kernel(
         turn(("a", 1), [xa[1]])
         warm_up(1)
         nc.vector.tensor_copy(out=w1p[:], in_=w1raw[:].rearrange("p (m t) -> p t m", t=4))
+        widen_v(2)
         gb = grp.tile([P, P, 4], BF16, name="gb", align_bytes=64)
         nc.scalar.copy(
             out=words_of(gb[:]).rearrange("p (j z a u) -> p j z a u", z=Z, a=4, u=2),
@@ -446,10 +541,14 @@ def tile_tpvformersoftplusoccupancydecoder_d1p_kernel(
             project(0, t, False)
         scaled(nc.vector, nb1[:], b1t[:], -1.0)
         spread_b_bytes(1, 1)
+        widen(3, 0, True)
+        widen(3, 1, True)
         bias_b(0, 1)
         quant_a(1, 1)
         spread_b_scales(1, 1)
-        for j in range(2, 6):
+        widen(3, 2, True)
+        widen(3, 3, True)
+        for j in range(4, 8):
             widen_s(j)
 
         add_b(0, 0)
@@ -469,8 +568,6 @@ def tile_tpvformersoftplusoccupancydecoder_d1p_kernel(
             sigm(1, t)
         turn(("a", 2), [xa[2], xa[3]])
         turn(("a", 4), [xa[4], xa[5]])
-        widen_v(6)
-        widen_v(7)
         turn(("a", 6), [xa[6], xa[7]])
         warm_up(1)
         scaled(nc.vector, gk[:], gt[:], 1.0 / KNEE)
@@ -515,23 +612,22 @@ def tile_tpvformersoftplusoccupancydecoder_d1p_kernel(
         floor(0, 1)
         quant_v(0, 0)
         product_g(0, 1)
-
         sigm(4, 0, True)
         project(4, 3)
         sigm(4, 1, True)
-        project(5, 0)
+        project(2, 3, False)
         sigm2(3, 0, 4)
         add_b(2, 0)
-        project(2, 3, False)
+        project(5, 0)
         add_b(2, 1)
         decode(0, 0)
         add_b(2, 2)
         place_g()
         lower(1, 2)
         project(5, 1)
-        lower(1, 3)
-        project(5, 2)
         add_b(2, 3)
+        project(5, 2)
+        lower(1, 3)
         sigm(4, 2, True)
         project(5, 3)
         for j, t in [(4, 3), (5, 0), (5, 1), (5, 2)]:
@@ -556,7 +652,8 @@ def tile_tpvformersoftplusoccupancydecoder_d1p_kernel(
             factor(2, t)
         quant_v(1, 0)
         loga(3, 0, 4, 0, HV)
-        loga(5, 0, 2)
+        loga(5, 0, 1)
+        loga(5, 1, 2)
         loga(5, 2, 4)
         loga(3, 0, 4, HV, NV)
         loga(4, 0, 2)
@@ -568,9 +665,9 @@ def tile_tpvformersoftplusoccupancydecoder_d1p_kernel(
         decode(1, 0)
         lower(5, 0)
         project(4, 1)
-        finish(1, 0)
-        project(4, 2)
         lower(5, 1)
+        project(4, 2)
+        finish(1, 0)
         project(6, 0)
         lower(5, 2)
         project(6, 1)
@@ -611,9 +708,9 @@ def tile_tpvformersoftplusoccupancydecoder_d1p_kernel(
         product_g(2, 1)
         decode(2, 0)
         product_v(4, 0, 128, HV)
+        product_v(4, 1)
         finish(5, 1)
         project(6, 0)
-        product_v(4, 1)
         finish(2, 0)
         project(6, 1)
         quant_v(4, 0)
@@ -624,7 +721,7 @@ def tile_tpvformersoftplusoccupancydecoder_d1p_kernel(
         lower(7, 0)
         project(6, 2)
         lower(7, 1)
-        decode(4, 0)
+        decode_t(4, 0)
         lower(7, 2)
         decode(4, 1)
         lower(7, 3)
@@ -636,24 +733,27 @@ def tile_tpvformersoftplusoccupancydecoder_d1p_kernel(
         decode(2, 1)
         lower(6, 1)
         lower(6, 2)
+        bias_t(4, 0)
+        turn_back(4, 0)
         gain_pe(6, 0)
         weave(7, 2)
+        gain_s(6, 1)
         weave(7, 3)
-        finish(4, 0)
+        finish(4, 1)
+        finish_s(4, 0)
+        weave_s(6, 1)
+        weave(6, 0)
         product_v(6, 1)
         quant_v(7, 0)
         decode(7, 0)
         quant_v(7, 1)
         decode(7, 1)
-        gain_s(6, 1)
-        weave(6, 0)
-        finish(4, 1)
         quant_v(6, 1)
         decode(6, 1)
         finish(2, 1)
+        finish(7, 0)
         quant_v(6, 0)
         decode(6, 0)
-        finish(7, 0)
         finish(7, 1)
         finish(6, 1)
         finish_z(6, 0)

@@ -23,7 +23,7 @@ HV = 256
 KNEE = 16.0
 EPS = 2.0 ** -60
 WI = 4
-NB0 = 4
+NB0 = 2
 
 
 def tile_tpvformersoftplusoccupancydecoder_d1p_kernel(
@@ -517,7 +517,6 @@ def tile_tpvformersoftplusoccupancydecoder_d1p_kernel(
         turn(("a", 1), [xa[1]])
         warm_up(1)
         nc.vector.tensor_copy(out=w1p[:], in_=w1raw[:].rearrange("p (m t) -> p t m", t=4))
-        widen_v(2)
         gb = grp.tile([P, P, 4], BF16, name="gb", align_bytes=64)
         nc.scalar.copy(
             out=words_of(gb[:]).rearrange("p (j z a u) -> p j z a u", z=Z, a=4, u=2),
@@ -541,14 +540,10 @@ def tile_tpvformersoftplusoccupancydecoder_d1p_kernel(
             project(0, t, False)
         scaled(nc.vector, nb1[:], b1t[:], -1.0)
         spread_b_bytes(1, 1)
-        widen(3, 0, True)
-        widen(3, 1, True)
         bias_b(0, 1)
         quant_a(1, 1)
         spread_b_scales(1, 1)
-        widen(3, 2, True)
-        widen(3, 3, True)
-        for j in range(4, 8):
+        for j in range(2, 6):
             widen_s(j)
 
         add_b(0, 0)
@@ -568,6 +563,8 @@ def tile_tpvformersoftplusoccupancydecoder_d1p_kernel(
             sigm(1, t)
         turn(("a", 2), [xa[2], xa[3]])
         turn(("a", 4), [xa[4], xa[5]])
+        widen_v(6)
+        widen_v(7)
         turn(("a", 6), [xa[6], xa[7]])
         warm_up(1)
         scaled(nc.vector, gk[:], gt[:], 1.0 / KNEE)

@@ -472,17 +472,17 @@ def tile_tpvformersoftplusoccupancydecoder_d1p_kernel(
             )
 
 
+        nc.vector.memset(s1raw[:].bitcast(I32), 0)
         nc.vector.memset(zero[:], 0.0)
         nc.vector.memset(dum[:], 0.0)
-        nc.vector.memset(s1raw[:].bitcast(I32), 0)
         nc.vector.memset(cqs[:].bitcast(I32), 0)
         nc.vector.memset(bqs[:].bitcast(I32), 0)
         nc.vector.memset(s2w[:].bitcast(I32), 0)
         nc.sync.dma_start(out=xc[:], in_=twz.rearrange("w z d -> (w z) d"))
         nc.scalar.dma_start(out=xb[:], in_=tzh.rearrange("z h d -> (z h) d"))
-        nc.sync.dma_start(out=byt0[:], in_=bytes_v[:, 0:NB0, :])
-        nc.scalar.dma_start(out=sc[:], in_=scale_v)
         nc.sync.dma_start(out=w1raw[:], in_=w1_words[0].rearrange("p n t -> p (n t)").bitcast(I32))
+        nc.scalar.dma_start(out=sc[:], in_=scale_v)
+        nc.sync.dma_start(out=byt0[:], in_=bytes_v[:, 0:NB0, :])
         for q in range(4):
             load_rows(s1raw, w1_scales, q, nc.sync)
         nc.scalar.activation(out=dum[:], in_=dum[:], func=AF.Sigmoid)
@@ -500,11 +500,11 @@ def tile_tpvformersoftplusoccupancydecoder_d1p_kernel(
         warm_up(4)
         scaled(nc.vector, nxc[:], xc[:], -1.0)
         scaled(nc.vector, nxb[:], xb[:], -1.0)
-        scaled(nc.vector, nsc[:], sc[:], -1.0)
         c_bank = turn("c", [nxc])
         b_bank = turn("b", [nxb])
-        for q in range(4):
-            widen(0, q, q < 2)
+        scaled(nc.vector, nsc[:], sc[:], -1.0)
+        nc.vector.tensor_copy(out=w1p[:], in_=w1raw[:].rearrange("p (m t) -> p t m", t=4))
+        widen_v(0)
         warm_up(1)
         turn(("a", 0), [xa[0]])
         gc = grp.tile([P, P, 4], BF16, name="gc", align_bytes=64)
@@ -516,7 +516,6 @@ def tile_tpvformersoftplusoccupancydecoder_d1p_kernel(
         widen_v(1)
         turn(("a", 1), [xa[1]])
         warm_up(1)
-        nc.vector.tensor_copy(out=w1p[:], in_=w1raw[:].rearrange("p (m t) -> p t m", t=4))
         gb = grp.tile([P, P, 4], BF16, name="gb", align_bytes=64)
         nc.scalar.copy(
             out=words_of(gb[:]).rearrange("p (j z a u) -> p j z a u", z=Z, a=4, u=2),

@@ -76,7 +76,7 @@ def tile_tpvformersoftplusoccupancydecoder_d1p_kernel(
         as_ = keep.tile([P, NU * P], U8, name="as_", align_bytes=64)
         bp = keep.tile([P, 4, NU, 16], F32, name="bp")
         dg = keep.tile([P, 4, P], F32, name="dg")
-        zero = keep.tile([P, P], F32, name="zero")
+        zero = keep.tile([P, HV], F32, name="zero")
         dum = keep.tile([P, 1], F32, name="dum")
         soft = [keep.tile([P, 4, NV], F32, name="soft%d" % j) for j in range(NU)]
         big, nsum = {}, {}
@@ -105,12 +105,18 @@ def tile_tpvformersoftplusoccupancydecoder_d1p_kernel(
         def release(key):
             free.append(held.pop(key)[1])
 
+        def halves(tile):
+            return tile[:].rearrange("p (u m e) -> p m u e", u=2, e=2)
+
         def widen(j, q, vec):
             cols = slice(128 * q, 128 * q + 128)
             src = (byt0[:, j, cols] if j < NB0 else byt1[:, j - NB0, cols]).bitcast(FP8)
             s = nsc[:, j, q : q + 1]
             if vec:
-                nc.vector.tensor_scalar(out=xa[j][:, cols], in0=src, scalar1=s, scalar2=None, op0=ALU.mult)
+                nc.vector.tensor_scalar(
+                    out=halves(xa[j])[:, 32 * q : 32 * q + 32], in0=src.rearrange("p (m u e) -> p m u e", u=2, e=2),
+                    scalar1=s, scalar2=None, op0=ALU.mult,
+                )
             else:
                 nc.scalar.activation(out=xa[j][:, cols], in_=src, func=AF.Copy, scale=s)
 
@@ -122,18 +128,19 @@ def tile_tpvformersoftplusoccupancydecoder_d1p_kernel(
             for q in range(4):
                 widen(j, q, False)
 
-        def turn(key, srcs):
+        def turn(key, srcs, sorted_words=False):
             bank = take(key)
             for s, src in enumerate(srcs):
                 words = src[:].bitcast(F32)
                 for u in range(2):
-                    nc.tensor.transpose(bank[:, 256 * s + P * u : 256 * s + P * u + P], words[:, u : 2 * P : 2], ident[:])
+                    part = words[:, P * u : P * (u + 1)] if sorted_words else words[:, u : 2 * P : 2]
+                    nc.tensor.transpose(bank[:, 256 * s + P * u : 256 * s + P * u + P], part, ident[:])
             return bank
 
         def warm_up(count):
             bank = take("warm")
             for i in range(count):
-                nc.tensor.matmul(out=bank[:, P * i : P * (i + 1)], lhsT=zero[:], rhs=zero[:], start=True, stop=True)
+                nc.tensor.matmul(out=bank[:, HV * i : HV * (i + 1)], lhsT=zero[:, 0:P], rhs=zero[:], start=True, stop=True)
             release("warm")
 
         def words_of(tile):
@@ -497,16 +504,16 @@ def tile_tpvformersoftplusoccupancydecoder_d1p_kernel(
         for c in range(2):
             nc.sync.dma_start(out=b2c[c][:], in_=b2[P * c : P * (c + 1)].rearrange("(p o) -> p o", o=1))
 
-        warm_up(4)
-        scaled(nc.vector, nxc[:], xc[:], -1.0)
-        scaled(nc.vector, nxb[:], xb[:], -1.0)
-        c_bank = turn("c", [nxc])
-        b_bank = turn("b", [nxb])
+        warm_up(2)
+        scaled(nc.vector, halves(nxc), xc[:].rearrange("p (m u e) -> p m u e", u=2, e=2), -1.0)
+        scaled(nc.vector, halves(nxb), xb[:].rearrange("p (m u e) -> p m u e", u=2, e=2), -1.0)
+        c_bank = turn("c", [nxc], True)
+        b_bank = turn("b", [nxb], True)
         scaled(nc.vector, nsc[:], sc[:], -1.0)
         nc.vector.tensor_copy(out=w1p[:], in_=w1raw[:].rearrange("p (m t) -> p t m", t=4))
         widen_v(0)
         warm_up(1)
-        turn(("a", 0), [xa[0]])
+        turn(("a", 0), [xa[0]], True)
         gc = grp.tile([P, P, 4], BF16, name="gc", align_bytes=64)
         nc.scalar.copy(
             out=words_of(gc[:]).rearrange("p (z w u) -> p z w u", z=Z, u=2),
@@ -514,7 +521,7 @@ def tile_tpvformersoftplusoccupancydecoder_d1p_kernel(
         )
         release("c")
         widen_v(1)
-        turn(("a", 1), [xa[1]])
+        turn(("a", 1), [xa[1]], True)
         warm_up(1)
         gb = grp.tile([P, P, 4], BF16, name="gb", align_bytes=64)
         nc.scalar.copy(
@@ -542,7 +549,7 @@ def tile_tpvformersoftplusoccupancydecoder_d1p_kernel(
         bias_b(0, 1)
         quant_a(1, 1)
         spread_b_scales(1, 1)
-        for j in range(2, 6):
+        for j in range(4, 8):
             widen_s(j)
 
         add_b(0, 0)
@@ -560,12 +567,12 @@ def tile_tpvformersoftplusoccupancydecoder_d1p_kernel(
         release("bb")
         for t in range(4):
             sigm(1, t)
-        turn(("a", 2), [xa[2], xa[3]])
+        widen_v(2)
+        widen_v(3)
+        turn(("a", 2), [xa[2], xa[3]], True)
         turn(("a", 4), [xa[4], xa[5]])
-        widen_v(6)
-        widen_v(7)
-        turn(("a", 6), [xa[6], xa[7]])
         warm_up(1)
+        turn(("a", 6), [xa[6], xa[7]])
         scaled(nc.vector, gk[:], gt[:], 1.0 / KNEE)
         scaled(nc.vector, ng[:], gt[:], -1.0)
         scaled(nc.vector, ngw[:], gt[:].unsqueeze(2).to_broadcast([P, 4, WI]), -1.0)

@@ -85,6 +85,8 @@ def tile_tpvformersoftplusoccupancydecoder_d1p_kernel(
         scale_v = thw_scale.rearrange("(j a) w q -> (a w) j q", a=4)
         out_v = out.rearrange("(j a) w z e -> (a w) j z e", a=4)
 
+        out_w = out.rearrange("(j a) w z e -> j w a (z e)", a=4)
+
         def load_rows(tile, scales, q, eng):
             eng.dma_start(
                 out=tile[32 * q : 32 * q + 4, :].bitcast(I32),
@@ -268,9 +270,9 @@ def tile_tpvformersoftplusoccupancydecoder_d1p_kernel(
             if j not in nsum:
                 nsum[j] = keep.tile([P, 4, NV], F32, name="nsum%d" % j)
             nc.vector.tensor_tensor(
-                out=nsum[j][:, t, :].rearrange("p (r w) -> p r w", w=W),
-                in0=bank[:].rearrange("p (r w) -> p r w", w=W),
-                in1=bp[:, t, j, :].unsqueeze(2).to_broadcast([P, 16, W]),
+                out=nsum[j][:, t, :].rearrange("p (z w a) -> p z w a", z=Z, a=4),
+                in0=bank[:].rearrange("p (z a w) -> p z w a", z=Z, a=4),
+                in1=bp[:, t, j, :].rearrange("p (z a) -> p z a", a=4).unsqueeze(2).to_broadcast([P, Z, W, 4]),
                 op=ALU.add,
             )
             release((j, t))
@@ -424,7 +426,10 @@ def tile_tpvformersoftplusoccupancydecoder_d1p_kernel(
                 in1=b2t[:].unsqueeze(1).to_broadcast([P, 2, E]), op=ALU.add,
             )
             release((j, "o", hf))
-            nc.sync.dma_start(out=out_v[:, j, 2 * hf : 2 * hf + 2], in_=ot[:])
+            if j in nsum:
+                nc.sync.dma_start(out=out_w[j, :, :, 2 * E * hf : 2 * E * (hf + 1)], in_=ot[:].rearrange("p z e -> p (z e)"))
+            else:
+                nc.sync.dma_start(out=out_v[:, j, 2 * hf : 2 * hf + 2], in_=ot[:])
 
         turned = {}
 

@@ -76,7 +76,7 @@ def tile_tpvformersoftplusoccupancydecoder_d1p_kernel(
         as_ = keep.tile([P, NU * P], U8, name="as_", align_bytes=64)
         bp = keep.tile([P, 4, NU, 16], F32, name="bp")
         dg = keep.tile([P, 4, P], F32, name="dg")
-        zero = keep.tile([P, HV], F32, name="zero")
+        zero = keep.tile([P, 3 * P], F32, name="zero")
         dum = keep.tile([P, 1], F32, name="dum")
         soft = [keep.tile([P, 4, NV], F32, name="soft%d" % j) for j in range(NU)]
         big, nsum = {}, {}
@@ -139,10 +139,12 @@ def tile_tpvformersoftplusoccupancydecoder_d1p_kernel(
                     nc.tensor.transpose(bank[:, 256 * s + P * u : 256 * s + P * u + P], part, ident[:])
             return bank
 
-        def warm_up(count):
+        def warm_up(count, width=HV):
             bank = take("warm")
             for i in range(count):
-                nc.tensor.matmul(out=bank[:, HV * i : HV * (i + 1)], lhsT=zero[:, 0:P], rhs=zero[:], start=True, stop=True)
+                nc.tensor.matmul(
+                    out=bank[:, HV * i : HV * i + width], lhsT=zero[:, 0:P], rhs=zero[:, 0:width], start=True, stop=True
+                )
             release("warm")
 
         def words_of(tile):
@@ -492,9 +494,9 @@ def tile_tpvformersoftplusoccupancydecoder_d1p_kernel(
         nc.vector.memset(s2w[:].bitcast(I32), 0)
         nc.sync.dma_start(out=xc[:], in_=twz.rearrange("w z d -> (w z) d"))
         nc.scalar.dma_start(out=xb[:], in_=tzh.rearrange("z h d -> (z h) d"))
-        nc.sync.dma_start(out=w1raw[:], in_=w1_words[0].rearrange("p n t -> p (n t)").bitcast(I32))
-        nc.scalar.dma_start(out=sc[:], in_=scale_v)
         nc.sync.dma_start(out=byt0[:], in_=bytes_v[:, 0:NB0, :])
+        nc.scalar.dma_start(out=sc[:], in_=scale_v)
+        nc.sync.dma_start(out=w1raw[:], in_=w1_words[0].rearrange("p n t -> p (n t)").bitcast(I32))
         for q in range(4):
             load_rows(s1raw, w1_scales, q, nc.sync)
         nc.scalar.activation(out=dum[:], in_=dum[:], func=AF.Sigmoid)
@@ -515,9 +517,8 @@ def tile_tpvformersoftplusoccupancydecoder_d1p_kernel(
         c_bank = turn("c", [nxc], True)
         b_bank = turn("b", [nxb], True)
         scaled(nc.vector, nsc[:], sc[:], -1.0)
-        nc.vector.tensor_copy(out=w1p[:], in_=w1raw[:].rearrange("p (m t) -> p t m", t=4))
         widen_v(0)
-        warm_up(1)
+        warm_up(1, 3 * P)
         turn(("a", 0), [xa[0]], True)
         gc = grp.tile([P, P, 4], BF16, name="gc", align_bytes=64)
         nc.scalar.copy(
@@ -526,8 +527,9 @@ def tile_tpvformersoftplusoccupancydecoder_d1p_kernel(
         )
         release("c")
         widen_v(1)
+        nc.vector.tensor_copy(out=w1p[:], in_=w1raw[:].rearrange("p (m t) -> p t m", t=4))
         turn(("a", 1), [xa[1]], True)
-        warm_up(1)
+        warm_up(1, 3 * P)
         gb = grp.tile([P, P, 4], BF16, name="gb", align_bytes=64)
         nc.scalar.copy(
             out=words_of(gb[:]).rearrange("p (j z a u) -> p j z a u", z=Z, a=4, u=2),
@@ -557,11 +559,16 @@ def tile_tpvformersoftplusoccupancydecoder_d1p_kernel(
         for j in range(4, 8):
             widen_s(j)
 
+        spread_b(1, 1)
+        scaled(nc.vector, ng[:], gt[:], -1.0)
+        nc.gpsimd.tensor_tensor(
+            out=dg[:], in0=ident[:].unsqueeze(1).to_broadcast([P, 4, P]),
+            in1=ng[:].unsqueeze(2).to_broadcast([P, 4, P]), op=ALU.mult,
+        )
         add_b(0, 0)
         sigm3(0, 0)
         add_b(0, 1)
         sigm3(0, 1)
-        spread_b(1, 1)
         for t in range(4):
             project(1, t)
         add_b(0, 2)
@@ -579,7 +586,6 @@ def tile_tpvformersoftplusoccupancydecoder_d1p_kernel(
         warm_up(1)
         turn(("a", 6), [xa[6], xa[7]])
         scaled(nc.vector, gk[:], gt[:], 1.0 / KNEE)
-        scaled(nc.vector, ng[:], gt[:], -1.0)
         scaled(nc.vector, ngw[:], gt[:].unsqueeze(2).to_broadcast([P, 4, WI]), -1.0)
         spread_b_bytes(4, 4)
         for t in range(4):
@@ -593,8 +599,6 @@ def tile_tpvformersoftplusoccupancydecoder_d1p_kernel(
             project(3, t, False)
         copy_a(4, 2, True)
         project(3, 2, False)
-        for t in range(4):
-            scaled(nc.vector, dg[:, t, :], ident[:], ng[:, t : t + 1])
         quant_a(4, 2)
         copy_a(6, 2, True)
         project(3, 3, False)

@@ -32,10 +32,10 @@ def tile_tpvformersoftplusoccupancydecoder_d1p_kernel(
     nc = tc.nc
     with ExitStack() as ctx:
         keep = ctx.enter_context(tc.tile_pool(name="keep", bufs=1))
-        grp = ctx.enter_context(tc.tile_pool(name="grp", bufs=2))
-        vpool = ctx.enter_context(tc.tile_pool(name="vpool", bufs=4))
+        grp = ctx.enter_context(tc.tile_pool(name="grp", bufs=3))
+        vpool = ctx.enter_context(tc.tile_pool(name="vpool", bufs=7))
         one = ctx.enter_context(tc.tile_pool(name="one", bufs=1))
-        opool = ctx.enter_context(tc.tile_pool(name="opool", bufs=8))
+        opool = ctx.enter_context(tc.tile_pool(name="opool", bufs=16))
         psum = ctx.enter_context(tc.psum_pool(name="psum", bufs=1))
         ctx.enter_context(tc.manual_schedule())
 
@@ -356,6 +356,24 @@ def tile_tpvformersoftplusoccupancydecoder_d1p_kernel(
                 out=vts[j, hf][:, c0:c1].rearrange("p (c i) t -> p c t i", i=WI),
                 in0=walk(soft[j][:, :, cols]), in1=other, op=ALU.mult,
             )
+
+        whole = {}
+
+        def product_unit(j, c0, c1):
+            if j not in whole:
+                whole[j] = keep.tile([P, NV, 4], BF16, name="whole%d" % j, align_bytes=64)
+            gsrc = held["g"][0][:, 0 : 4 * WI].rearrange("p (t i) -> p t i", i=WI)
+            nc.vector.tensor_tensor(
+                out=whole[j][:, c0:c1].rearrange("p (c i) t -> p c t i", i=WI), in0=walk(soft[j][:, :, c0:c1]),
+                in1=gsrc.unsqueeze(1).to_broadcast([P, (c1 - c0) // WI, 4, WI]), op=ALU.mult,
+            )
+
+        def quant_unit(j):
+            vc = keep.tile([P, NV], U32, name="vc%d" % j, align_bytes=64)
+            vs = keep.tile([P, NV], U8, name="vs%d" % j, align_bytes=64)
+            quant(vc[:], vs[:], whole[j][:])
+            for hf in range(2):
+                vqs[j, hf] = (vc[:, HV * hf : HV * (hf + 1)], vs[:, HV * hf : HV * (hf + 1)])
 
         def product_g(j, hf, c0=0, c1=HV):
             if (j, hf) not in vts:
@@ -713,20 +731,18 @@ def tile_tpvformersoftplusoccupancydecoder_d1p_kernel(
             sigm(j, t)
         finish(5, 0)
         finish(3, 1)
-        product_v(4, 0, 0, 128)
+        product_unit(4, 0, P)
         quant_v(5, 1)
         decode(5, 1)
         quant_v(2, 0)
         product_g(2, 1)
         decode(2, 0)
-        product_v(4, 0, 128, HV)
-        product_v(4, 1)
+        product_unit(4, P, NV)
         finish(5, 1)
         project(6, 0)
         finish(2, 0)
         project(6, 1)
-        quant_v(4, 0)
-        quant_v(4, 1)
+        quant_unit(4)
         quant_v(2, 1)
         for j, t in [(7, 0), (7, 1), (7, 2), (7, 3), (6, 3), (6, 0), (6, 1), (6, 2)]:
             loga(j, t, t + 1)

@@ -20,10 +20,12 @@ P = 128
 NU = 8
 NV = 512
 HV = 256
-KNEE = 16.0
+FLOOR = 2.0 ** -23
+KNEE = 23 * 0.6931471805599453
 EPS = 2.0 ** -60
 WI = 4
 NB0 = 2
+NVW = 4
 
 
 def tile_tpvformersoftplusoccupancydecoder_d1p_kernel(
@@ -35,7 +37,7 @@ def tile_tpvformersoftplusoccupancydecoder_d1p_kernel(
         grp = ctx.enter_context(tc.tile_pool(name="grp", bufs=3))
         vpool = ctx.enter_context(tc.tile_pool(name="vpool", bufs=7))
         one = ctx.enter_context(tc.tile_pool(name="one", bufs=1))
-        opool = ctx.enter_context(tc.tile_pool(name="opool", bufs=16))
+        opool = ctx.enter_context(tc.tile_pool(name="opool", bufs=10))
         psum = ctx.enter_context(tc.psum_pool(name="psum", bufs=1))
         ctx.enter_context(tc.manual_schedule())
 
@@ -77,6 +79,8 @@ def tile_tpvformersoftplusoccupancydecoder_d1p_kernel(
         bp = keep.tile([P, 4, NU, 16], F32, name="bp")
         dg = keep.tile([P, 4, P], F32, name="dg")
         zero = keep.tile([P, 3 * P], F32, name="zero")
+        flr = keep.tile([P, 1], F32, name="flr")
+        flr2 = keep.tile([P, 1], F32, name="flr2")
         dum = keep.tile([P, 1], F32, name="dum")
         soft = [keep.tile([P, 4, NV], F32, name="soft%d" % j) for j in range(NU)]
         big, nsum = {}, {}
@@ -130,14 +134,24 @@ def tile_tpvformersoftplusoccupancydecoder_d1p_kernel(
             for q in range(4):
                 widen(j, q, False)
 
-        def turn(key, srcs, sorted_words=False):
+        def turn(key, srcs, ordered):
             bank = take(key)
-            for s, src in enumerate(srcs):
+            for s, (src, sorted_words) in enumerate(zip(srcs, ordered)):
                 words = src[:].bitcast(F32)
                 for u in range(2):
                     part = words[:, P * u : P * (u + 1)] if sorted_words else words[:, u : 2 * P : 2]
                     nc.tensor.transpose(bank[:, 256 * s + P * u : 256 * s + P * u + P], part, ident[:])
             return bank
+
+        def turn_a(first, count):
+            tiles = range(first, first + count)
+            turn(("a", first), [xa[j] for j in tiles], [j < NVW for j in tiles])
+
+        def make_diag():
+            nc.gpsimd.tensor_tensor(
+                out=dg[:], in0=ident[:].unsqueeze(1).to_broadcast([P, 4, P]),
+                in1=ng[:].unsqueeze(2).to_broadcast([P, 4, P]), op=ALU.mult,
+            )
 
         def warm_up(count, width=HV):
             bank = take("warm")
@@ -357,6 +371,34 @@ def tile_tpvformersoftplusoccupancydecoder_d1p_kernel(
                 in0=walk(soft[j][:, :, cols]), in1=other, op=ALU.mult,
             )
 
+        def product_s(j, hf):
+            vts[j, hf] = vpool.tile([P, HV, 4], BF16, name="vv", align_bytes=64)
+            cols = slice(HV * hf, HV * (hf + 1))
+            nc.vector.tensor_tensor(
+                out=vts[j, hf][:].rearrange("p (c i) t -> p c t i", i=WI),
+                in0=walk(soft[j][:, :, cols]), in1=walk(big[j, hf][:, :, cols]), op=ALU.mult,
+            )
+
+        parts = {}
+
+        def product_q(j, q, eng):
+            pool, name = (one, "vg") if eng is nc.gpsimd else (vpool, "vv")
+            parts[j, q] = pool.tile([P, HV, 4], BF16, name=name, align_bytes=64)
+            cols = slice(P * q, P * (q + 1))
+            eng.tensor_tensor(
+                out=parts[j, q][:, 0:P].rearrange("p (c i) t -> p c t i", i=WI),
+                in0=walk(soft[j][:, :, cols]), in1=walk(big[j, q // 2][:, :, cols]), op=ALU.mult,
+            )
+
+        def quant_q(j, q):
+            if (j, q // 2) not in vqs:
+                vc = vpool.tile([P, HV], U32, name="vc", align_bytes=64)
+                vs = vpool.tile([P, HV], U8, name="vs", align_bytes=64)
+                vqs[j, q // 2] = (vc, vs)
+            vc, vs = vqs[j, q // 2]
+            cols = slice(P * (q % 2), P * (q % 2 + 1))
+            quant(vc[:, cols], vs[:, cols], parts[j, q][:, 0:P])
+
         whole = {}
 
         def product_unit(j, c0, c1):
@@ -439,6 +481,12 @@ def tile_tpvformersoftplusoccupancydecoder_d1p_kernel(
                     start=True, stop=True,
                 )
 
+        def store(j, hf, ot):
+            if j in nsum:
+                nc.sync.dma_start(out=out_w[j, :, :, 2 * E * hf : 2 * E * (hf + 1)], in_=ot[:].rearrange("p z e -> p (z e)"))
+            else:
+                nc.sync.dma_start(out=out_v[:, j, 2 * hf : 2 * hf + 2], in_=ot[:])
+
         def finish(j, hf):
             ot = opool.tile([P, 2, E], F32, name="ot")
             nc.vector.tensor_tensor(
@@ -446,10 +494,7 @@ def tile_tpvformersoftplusoccupancydecoder_d1p_kernel(
                 in1=b2t[:].unsqueeze(1).to_broadcast([P, 2, E]), op=ALU.add,
             )
             release((j, "o", hf))
-            if j in nsum:
-                nc.sync.dma_start(out=out_w[j, :, :, 2 * E * hf : 2 * E * (hf + 1)], in_=ot[:].rearrange("p z e -> p (z e)"))
-            else:
-                nc.sync.dma_start(out=out_v[:, j, 2 * hf : 2 * hf + 2], in_=ot[:])
+            store(j, hf, ot)
 
         turned = {}
 
@@ -486,7 +531,7 @@ def tile_tpvformersoftplusoccupancydecoder_d1p_kernel(
             ot = opool.tile([P, 2, E], F32, name="ot")
             nc.scalar.copy(out=ot[:].rearrange("p z e -> p (z e)"), in_=held[j, "o", hf][0][:])
             release((j, "o", hf))
-            nc.sync.dma_start(out=out_v[:, j, 2 * hf : 2 * hf + 2], in_=ot[:])
+            store(j, hf, ot)
 
         def finish_z(j, hf):
             ot = opool.tile([P, 2, E], F32, name="ot")
@@ -496,6 +541,10 @@ def tile_tpvformersoftplusoccupancydecoder_d1p_kernel(
                 )
                 eng.dma_start(out=out_v[:, j, 2 * hf + zz], in_=ot[:, zz, :])
             release((j, "o", hf))
+
+        def clip_s(j, eng, c0=0, c1=NV, low=FLOOR):
+            e = soft[j][:, :, c0:c1]
+            eng.tensor_scalar(out=e, in0=e, scalar1=1.0, scalar2=low, op0=ALU.min, op1=ALU.max)
 
         def place_g():
             bank = take("g")
@@ -532,12 +581,12 @@ def tile_tpvformersoftplusoccupancydecoder_d1p_kernel(
         warm_up(2)
         scaled(nc.vector, halves(nxc), xc[:].rearrange("p (m u e) -> p m u e", u=2, e=2), -1.0)
         scaled(nc.vector, halves(nxb), xb[:].rearrange("p (m u e) -> p m u e", u=2, e=2), -1.0)
-        c_bank = turn("c", [nxc], True)
-        b_bank = turn("b", [nxb], True)
+        c_bank = turn("c", [nxc], [True])
+        b_bank = turn("b", [nxb], [True])
         scaled(nc.vector, nsc[:], sc[:], -1.0)
         widen_v(0)
         warm_up(1, 3 * P)
-        turn(("a", 0), [xa[0]], True)
+        turn_a(0, 1)
         gc = grp.tile([P, P, 4], BF16, name="gc", align_bytes=64)
         nc.scalar.copy(
             out=words_of(gc[:]).rearrange("p (z w u) -> p z w u", z=Z, u=2),
@@ -546,7 +595,7 @@ def tile_tpvformersoftplusoccupancydecoder_d1p_kernel(
         release("c")
         widen_v(1)
         nc.vector.tensor_copy(out=w1p[:], in_=w1raw[:].rearrange("p (m t) -> p t m", t=4))
-        turn(("a", 1), [xa[1]], True)
+        turn_a(1, 1)
         warm_up(1, 3 * P)
         gb = grp.tile([P, P, 4], BF16, name="gb", align_bytes=64)
         nc.scalar.copy(
@@ -567,221 +616,220 @@ def tile_tpvformersoftplusoccupancydecoder_d1p_kernel(
                 out=bb[:, P * t : P * (t + 1)], lhsT=w1p[:, t, :].bitcast(FP8X4), lhsT_scale=s1p[:, t, :],
                 rhs=bq[:].bitcast(FP8X4), rhs_scale=bqs[:], start=True, stop=True,
             )
-        for t in range(4):
-            project(0, t, False)
         scaled(nc.vector, nb1[:], b1t[:], -1.0)
-        spread_b_bytes(1, 1)
-        bias_b(0, 1)
+        widen_v(2)
+        bias_b(0, 2)
         quant_a(1, 1)
-        spread_b_scales(1, 1)
         for j in range(4, 8):
             widen_s(j)
-
-        spread_b(1, 1)
+        project(0, 0, False)
+        project(0, 1, False)
+        turn_a(2, 1)
+        project(0, 2, False)
+        project(0, 3, False)
+        spread_b_bytes(2, 1)
+        spread_b_scales(2, 1)
+        spread_b(2, 1)
         scaled(nc.vector, ng[:], gt[:], -1.0)
-        nc.gpsimd.tensor_tensor(
-            out=dg[:], in0=ident[:].unsqueeze(1).to_broadcast([P, 4, P]),
-            in1=ng[:].unsqueeze(2).to_broadcast([P, 4, P]), op=ALU.mult,
-        )
+        make_diag()
         add_b(0, 0)
-        sigm3(0, 0)
         add_b(0, 1)
-        sigm3(0, 1)
-        for t in range(4):
-            project(1, t)
+        copy_a(2, 1, True)
         add_b(0, 2)
-        sigm3(0, 2)
+        for t in range(4):
+            project(1, t, False)
         add_b(0, 3)
-        sigm3(0, 3)
-        bias_b(2, 4)
+        quant_a(2, 1)
+        for t in range(4):
+            sigm3(0, t)
+        clip_s(0, nc.gpsimd, 0, HV)
+        for t in range(4):
+            add_b(1, t)
+            sigm3(1, t)
+            project(2, t)
+        bias_b(3, 5)
         release("bb")
         for t in range(4):
-            sigm(1, t)
-        widen_v(2)
+            sigm(2, t)
         widen_v(3)
-        turn(("a", 2), [xa[2], xa[3]], True)
-        turn(("a", 4), [xa[4], xa[5]])
-        warm_up(1)
-        turn(("a", 6), [xa[6], xa[7]])
+        turn_a(3, 2)
+        turn_a(5, 2)
+        turn_a(7, 1)
+        clip_s(0, nc.vector, HV, NV)
         scaled(nc.vector, gk[:], gt[:], 1.0 / KNEE)
         scaled(nc.vector, ngw[:], gt[:].unsqueeze(2).to_broadcast([P, 4, WI]), -1.0)
-        spread_b_bytes(4, 4)
+        spread_b_bytes(5, 3)
+        spread_b_scales(5, 3)
+        spread_b(5, 3)
+        copy_a(3, 2, True)
+        copy_a(5, 2, True)
+        quant_a(3, 2)
+        copy_a(7, 1, True)
+        quant_a(5, 2)
+        for t in range(4):
+            project(3, t, False)
+        quant_a(7, 1)
         for t in range(4):
             factor(0, t)
-        spread_b_scales(4, 4)
-        spread_b(4, 2)
-        copy_a(2, 2, True)
-        spread_b(6, 2)
-        quant_a(2, 2)
-        for t in range(2):
-            project(3, t, False)
-        copy_a(4, 2, True)
-        project(3, 2, False)
-        quant_a(4, 2)
-        copy_a(6, 2, True)
-        project(3, 3, False)
         loga(0, 0, 4, 0, HV)
-        loga(1, 0, 2)
-        loga(1, 2, 4)
+        loga(2, 0, 2)
+        loga(2, 2, 4)
         loga(0, 0, 4, HV, NV)
-        floor(0, 0)
+        loga(1, 0, 4, 0, HV)
+        loga(1, 0, 4, HV, NV)
         product_g(0, 0)
-        add_b(3, 0)
-        project(4, 0)
-        add_b(3, 1)
-        project(4, 1)
-        add_b(3, 2)
-        project(2, 0, False)
-        add_b(3, 3)
-        project(4, 2)
-        lower(1, 0)
-        project(2, 1, False)
-        lower(1, 1)
-        project(2, 2, False)
-        clip(3, 0, 4)
-        floor(0, 1)
+        for t in range(4):
+            add_b(3, t)
+            project(4, t, False)
+        lower(2, 0)
+        project(5, 0)
+        lower(2, 1)
+        project(5, 1)
+        for t in range(4):
+            factor(1, t)
         quant_v(0, 0)
         product_g(0, 1)
-        sigm(4, 0, True)
-        project(4, 3)
-        sigm(4, 1, True)
-        project(2, 3, False)
-        sigm2(3, 0, 4)
-        add_b(2, 0)
-        project(5, 0)
-        add_b(2, 1)
-        decode(0, 0)
-        add_b(2, 2)
-        place_g()
-        lower(1, 2)
-        project(5, 1)
-        add_b(2, 3)
+        lower(2, 2)
         project(5, 2)
-        lower(1, 3)
-        sigm(4, 2, True)
+        lower(2, 3)
         project(5, 3)
-        for j, t in [(4, 3), (5, 0), (5, 1), (5, 2)]:
-            sigm(j, t)
-        clip(2, 0, 4)
-        quant_a(6, 2)
-        quant_v(0, 1)
-        product_g(1, 0, 64, HV)
-        decode(0, 1)
-        sigm2(2, 0, 4)
-        sigm(5, 3)
-        finish(0, 0)
-        project(4, 0)
-        product_v(1, 1)
-        finish(0, 1)
-        product_v(1, 0, 0, 64)
-        quant_v(1, 1)
-        decode(1, 1)
-        for t in range(4):
-            factor(3, t)
-        for t in range(4):
-            factor(2, t)
-        quant_v(1, 0)
-        loga(3, 0, 4, 0, HV)
-        loga(5, 0, 1)
-        loga(5, 1, 2)
-        loga(5, 2, 4)
-        loga(3, 0, 4, HV, NV)
-        loga(4, 0, 2)
-        loga(4, 2, 4)
-        loga(2, 0, 4, 0, HV)
-        loga(2, 0, 4, HV, NV)
-        product_g(3, 0)
-        finish(1, 1)
-        decode(1, 0)
-        lower(5, 0)
-        project(4, 1)
-        lower(5, 1)
-        project(4, 2)
-        finish(1, 0)
+        add_b(4, 0)
+        place_g()
+        add_b(4, 1)
+        decode(0, 0)
+        add_b(4, 2)
         project(6, 0)
-        lower(5, 2)
+        add_b(4, 3)
         project(6, 1)
-        lower(5, 3)
-        quant_v(3, 0)
-        product_g(3, 1)
-        decode(3, 0)
-        product_v(5, 0)
-        lower(4, 0)
-        lower(4, 1)
-        lower(4, 3)
-        lower(4, 2)
+        floor(1, 0)
+        quant_v(0, 1)
+        product_g(1, 0)
+        for t in range(4):
+            sigm3(3, t)
+        for t in range(4):
+            sigm(5, t, True)
+        finish(0, 0)
+        decode(0, 1)
         project(6, 2)
         project(6, 3)
         project(7, 0)
-        quant_v(5, 0)
-        decode(5, 0)
-        quant_v(3, 1)
-        product_g(2, 0)
-        finish(3, 0)
-        decode(3, 1)
-        product_v(5, 1)
-
+        project(7, 1)
+        product_v(2, 0)
+        finish(0, 1)
+        product_v(2, 1)
+        floor(1, 1)
+        quant_v(2, 0)
+        quant_v(2, 1)
+        decode(2, 0)
+        product_s(1, 1)
+        quant_v(1, 0)
+        quant_v(1, 1)
+        nc.vector.memset(flr[:], FLOOR)
+        clip_s(3, nc.gpsimd, 0, 3 * P, flr[:])
         sigm(6, 0, True)
         sigm(6, 1, True)
-        sigm(6, 2, True)
-        project(7, 1)
+        for t in range(4):
+            sigm3(4, t)
         project(7, 2)
+        decode(2, 1)
+        sigm(6, 2, True)
         project(7, 3)
-        for j, t in [(6, 3), (7, 0), (7, 1), (7, 2), (7, 3)]:
-            sigm(j, t)
-        finish(5, 0)
-        finish(3, 1)
-        product_unit(4, 0, P)
-        quant_v(5, 1)
-        decode(5, 1)
-        quant_v(2, 0)
-        product_g(2, 1)
-        decode(2, 0)
-        product_unit(4, P, NV)
-        finish(5, 1)
-        project(6, 0)
         finish(2, 0)
+        decode(1, 0)
+        finish(2, 1)
+        decode(1, 1)
+        finish(1, 0)
+        project(6, 0)
+        sigm(6, 3)
+        for t in range(4):
+            sigm(7, t)
+        finish(1, 1)
         project(6, 1)
-        quant_unit(4)
-        quant_v(2, 1)
-        for j, t in [(7, 0), (7, 1), (7, 2), (7, 3), (6, 3), (6, 0), (6, 1), (6, 2)]:
-            loga(j, t, t + 1)
+        clip_s(3, nc.vector, 3 * P, NV)
+        clip_s(4, nc.vector)
+        for t in range(4):
+            factor(4, t)
+        for t in range(4):
+            factor(3, t)
+        loga(3, 0, 4, 0, HV)
+        product_g(3, 0)
+        for t in range(4):
+            loga(7, t, t + 1)
+        loga(6, 3, 4)
+        loga(3, 0, 4, HV, NV)
+        loga(6, 0, 2)
+        loga(6, 2, 3)
+        loga(4, 0, 4, 0, HV)
+        loga(5, 0, 2)
+        loga(5, 2, 4)
+        loga(4, 0, 4, HV, NV)
         lower(7, 0)
         project(6, 2)
         lower(7, 1)
-        decode_t(4, 0)
+        project(5, 0)
         lower(7, 2)
-        decode(4, 1)
+        project(5, 1)
         lower(7, 3)
-        product_g(7, 0)
-        gain_pe(7, 2)
         lower(6, 3)
-        gain_pe(7, 3)
+        product_v(7, 0)
+        quant_v(3, 0)
+        quant_v(7, 0)
+        product_g(3, 1)
+        decode(3, 0)
+        decode(7, 0)
         lower(6, 0)
-        decode(2, 1)
+        project(5, 2)
+        finish(3, 0)
+        project(5, 3)
         lower(6, 1)
         lower(6, 2)
-        bias_t(4, 0)
-        turn_back(4, 0)
         gain_pe(6, 0)
-        weave(7, 2)
-        gain_s(6, 1)
-        weave(7, 3)
-        finish(4, 1)
-        finish_s(4, 0)
-        weave_s(6, 1)
-        weave(6, 0)
-        product_v(6, 1)
-        quant_v(7, 0)
-        decode(7, 0)
-        quant_v(7, 1)
-        decode(7, 1)
-        quant_v(6, 1)
-        decode(6, 1)
-        finish(2, 1)
+        gain_pe(6, 1)
         finish(7, 0)
+        product_v(7, 1, 0, P)
+        quant_v(3, 1)
+        product_g(4, 0)
+        decode(3, 1)
+        product_v(7, 1, P, HV)
+        for t in range(4):
+            lower(5, t)
+        weave(6, 0)
+        weave(6, 1)
+        gain_s(6, 2)
+        weave_s(6, 2)
+        gain_s(6, 3)
+        weave_s(6, 3)
+        gain_pe(5, 0)
+        finish(3, 1)
+        quant_v(7, 1)
+        product_q(4, 2, nc.vector)
+        quant_v(4, 0)
         quant_v(6, 0)
-        decode(6, 0)
+        product_q(4, 3, nc.gpsimd)
+        decode(7, 1)
+        decode(4, 0)
+        decode_t(6, 0)
+        gain_pe(5, 1)
         finish(7, 1)
-        finish(6, 1)
-        finish_z(6, 0)
+        product_v(5, 1)
+        finish(4, 0)
+        bias_t(6, 0)
+        weave(5, 0)
+        weave(5, 1)
+        turn_back(6, 0)
+        finish_s(6, 0)
+        quant_v(6, 1)
+        decode_t(6, 1)
+        quant_q(4, 2)
+        quant_q(4, 3)
+        decode(4, 1)
+        quant_v(5, 1)
+        decode(5, 1)
+        quant_v(5, 0)
+        decode(5, 0)
+        bias_t(6, 1)
+        turn_back(6, 1)
+        finish(4, 1)
+        finish(5, 1)
+        finish_s(6, 1)
+        finish_z(5, 0)

@@ -459,6 +459,17 @@ def tile_tpvformersoftplusoccupancydecoder_d1p_kernel(
                 )
             flats[j, q] = flat
 
+        def gain_h(j, hf):
+            vts[j, hf] = vpool.tile([P, HV, 4], BF16, name="vv", align_bytes=64)
+            flats[j, hf] = keep.tile([P, 4, HV], BF16, name="flat%d_%d" % (j, hf))
+            for t in range(4):
+                nc.scalar.activation(
+                    out=flats[j, hf][:, t, :], in_=soft[j][:, t, HV * hf : HV * (hf + 1)], func=AF.Copy, scale=ng[:, t : t + 1]
+                )
+
+        def weave_h(j, hf):
+            nc.scalar.copy(out=vts[j, hf][:], in_=flats[j, hf][:].rearrange("p t n -> p n t"))
+
         def weave_s(j, q):
             hf, c0 = q // 2, P * (q % 2)
             nc.scalar.copy(out=vts[j, hf][:, c0 : c0 + P], in_=flats[j, q][:].rearrange("p t n -> p n t"))
@@ -794,42 +805,42 @@ def tile_tpvformersoftplusoccupancydecoder_d1p_kernel(
         for t in range(4):
             lower(5, t)
         weave(6, 0)
+        gain_h(6, 1)
         weave(6, 1)
-        gain_s(6, 2)
-        weave_s(6, 2)
-        gain_s(6, 3)
-        weave_s(6, 3)
+        weave_h(6, 1)
         gain_pe(5, 0)
+        gain_pe(5, 1)
         finish(3, 1)
         quant_v(7, 1)
         product_q(4, 2, nc.vector)
-        quant_v(4, 0)
         quant_v(6, 0)
+        quant_v(4, 0)
+        quant_v(6, 1)
         product_q(4, 3, nc.gpsimd)
         decode(7, 1)
-        decode(4, 0)
         decode_t(6, 0)
-        gain_pe(5, 1)
-        finish(7, 1)
-        product_v(5, 1)
-        finish(4, 0)
-        bias_t(6, 0)
+        decode(4, 0)
+        decode_t(6, 1)
+        gain_pe(5, 2)
         weave(5, 0)
         weave(5, 1)
+        bias_t(6, 0)
+        bias_t(6, 1)
         turn_back(6, 0)
+        product_v(5, 1, P, HV)
+        finish(7, 1)
+        turn_back(6, 1)
+        finish(4, 0)
+        weave(5, 2)
         finish_s(6, 0)
-        quant_v(6, 1)
-        decode_t(6, 1)
+        finish_s(6, 1)
+        quant_v(5, 0)
+        decode(5, 0)
         quant_q(4, 2)
         quant_q(4, 3)
         decode(4, 1)
         quant_v(5, 1)
         decode(5, 1)
-        quant_v(5, 0)
-        decode(5, 0)
-        bias_t(6, 1)
-        turn_back(6, 1)
+        finish(5, 0)
         finish(4, 1)
-        finish(5, 1)
-        finish_s(6, 1)
-        finish_z(5, 0)
+        finish_z(5, 1)

@@ -65,15 +65,12 @@ def tile_tpvformersoftplusoccupancydecoder_d1p_kernel(
         ngw = keep.tile([P, 4, WI], F32, name="ngw")
         b2t = keep.tile([P, E], BF16, name="b2t")
         b2c = [keep.tile([P, 1], BF16, name="b2c%d" % c) for c in range(2)]
-        cq = keep.tile([P, P], I32, name="cq", align_bytes=64)
-        cqs = keep.tile([P, P], U8, name="cqs", align_bytes=64)
         bq = keep.tile([P, P], I32, name="bq", align_bytes=64)
         bqs = keep.tile([P, P], U8, name="bqs", align_bytes=64)
         crc = keep.tile([P, NV], I32, name="crc", align_bytes=64)
         crs = keep.tile([P, NV], U8, name="crs", align_bytes=64)
         brc = keep.tile([P, NU * NV], I32, name="brc", align_bytes=64)
         brs = keep.tile([P, NU * NV], U8, name="brs", align_bytes=64)
-        bs4 = keep.tile([P, P, 4], U8, name="bs4", align_bytes=64)
         ac = keep.tile([P, NU * P], U32, name="ac", align_bytes=64)
         as_ = keep.tile([P, NU * P], U8, name="as_", align_bytes=64)
         bp = keep.tile([P, 4, NU, 16], F32, name="bp")
@@ -85,11 +82,10 @@ def tile_tpvformersoftplusoccupancydecoder_d1p_kernel(
         soft = [keep.tile([P, 4, NV], F32, name="soft%d" % j) for j in range(NU)]
         big, nsum = {}, {}
 
-        bytes_v = thw_bytes.rearrange("(j a) w k -> (a w) j k", a=4)
-        scale_v = thw_scale.rearrange("(j a) w q -> (a w) j q", a=4)
-        out_v = out.rearrange("(j a) w z e -> (a w) j z e", a=4)
+        bytes_v = thw_bytes.rearrange("h (q j) k -> (h q) j k", j=NU)
+        scale_v = thw_scale.rearrange("h (q j) s -> (h q) j s", j=NU)
+        out_v = out.rearrange("h (q j) z e -> (h q) j z e", j=NU)
 
-        out_w = out.rearrange("(j a) w z e -> j w a (z e)", a=4)
 
         def load_rows(tile, scales, q, eng):
             eng.dma_start(
@@ -183,35 +179,18 @@ def tile_tpvformersoftplusoccupancydecoder_d1p_kernel(
             cols = slice(first * P, (first + count) * P)
             quant(ac[:, cols], as_[:, cols], grouped[first][:, 0 : count * P])
 
-        def spread_c():
-            nc.vector.tensor_copy(
-                out=crc[:].rearrange("p (z a w) -> p z a w", z=Z, a=4),
-                in_=cq[:].rearrange("p (z w) -> p z w", z=Z).unsqueeze(2).to_broadcast([P, Z, 4, W]),
-            )
-            nc.vector.tensor_copy(
-                out=crs[:].bitcast(I32).rearrange("p (z a w) -> p z a w", z=Z, a=4),
-                in_=cqs[:].bitcast(I32).rearrange("p (z w) -> p z w", z=Z).unsqueeze(2).to_broadcast([P, Z, 4, W // 4]),
-            )
-
-        def spread_b_bytes(first, count):
-            rows = slice(16 * first, 16 * (first + count))
-            for i in range(4):
-                nc.vector.tensor_copy(out=bs4[:, rows, i], in_=bqs[:, rows])
-
         def spread_b_scales(first, count):
-            rows = slice(16 * first, 16 * (first + count))
             cols = slice(NV * first, NV * (first + count))
             nc.vector.tensor_copy(
-                out=brs[:, cols].bitcast(I32).rearrange("p (r w) -> p r w", w=W // 4),
-                in_=bs4[:, rows].rearrange("p r i -> p (r i)").bitcast(I32).unsqueeze(2).to_broadcast([P, 16 * count, W // 4]),
+                out=brs[:, cols].bitcast(I32).rearrange("p (r h) -> p r h", h=H),
+                in_=bqs[:].bitcast(I32)[:, Z * first : Z * (first + count)].unsqueeze(2).to_broadcast([P, Z * count, H]),
             )
 
         def spread_b(first, count):
-            rows = slice(16 * first, 16 * (first + count))
             cols = slice(NV * first, NV * (first + count))
             nc.vector.tensor_copy(
-                out=brc[:, cols].rearrange("p (r w) -> p r w", w=W),
-                in_=bq[:, rows].unsqueeze(2).to_broadcast([P, 16 * count, W]),
+                out=brc[:, cols].rearrange("p (r h q) -> p r h q", h=H, q=4),
+                in_=bq[:, 16 * first : 16 * (first + count)].rearrange("p (r q) -> p r q", q=4).unsqueeze(2).to_broadcast([P, Z * count, H, 4]),
             )
 
         def project(j, t, with_b=True):
@@ -286,9 +265,9 @@ def tile_tpvformersoftplusoccupancydecoder_d1p_kernel(
             if j not in nsum:
                 nsum[j] = keep.tile([P, 4, NV], F32, name="nsum%d" % j)
             nc.vector.tensor_tensor(
-                out=nsum[j][:, t, :].rearrange("p (z w a) -> p z w a", z=Z, a=4),
-                in0=bank[:].rearrange("p (z a w) -> p z w a", z=Z, a=4),
-                in1=bp[:, t, j, :].rearrange("p (z a) -> p z a", a=4).unsqueeze(2).to_broadcast([P, Z, W, 4]),
+                out=nsum[j][:, t, :].rearrange("p (z h q) -> p z h q", z=Z, q=4),
+                in0=bank[:].rearrange("p (z h q) -> p z h q", z=Z, q=4),
+                in1=bp[:, t, j, :].rearrange("p (z q) -> p z q", q=4).unsqueeze(2).to_broadcast([P, Z, H, 4]),
                 op=ALU.add,
             )
             release((j, t))
@@ -493,10 +472,7 @@ def tile_tpvformersoftplusoccupancydecoder_d1p_kernel(
                 )
 
         def store(j, hf, ot):
-            if j in nsum:
-                nc.sync.dma_start(out=out_w[j, :, :, 2 * E * hf : 2 * E * (hf + 1)], in_=ot[:].rearrange("p z e -> p (z e)"))
-            else:
-                nc.sync.dma_start(out=out_v[:, j, 2 * hf : 2 * hf + 2], in_=ot[:])
+            nc.sync.dma_start(out=out_v[:, j, 2 * hf : 2 * hf + 2], in_=ot[:])
 
         def finish(j, hf):
             ot = opool.tile([P, 2, E], F32, name="ot")
@@ -567,11 +543,10 @@ def tile_tpvformersoftplusoccupancydecoder_d1p_kernel(
         nc.vector.memset(s1raw[:].bitcast(I32), 0)
         nc.vector.memset(zero[:], 0.0)
         nc.vector.memset(dum[:], 0.0)
-        nc.vector.memset(cqs[:].bitcast(I32), 0)
         nc.vector.memset(bqs[:].bitcast(I32), 0)
         nc.vector.memset(s2w[:].bitcast(I32), 0)
-        nc.sync.dma_start(out=xc[:], in_=twz.rearrange("w z d -> (w z) d"))
-        nc.scalar.dma_start(out=xb[:], in_=tzh.rearrange("z h d -> (z h) d"))
+        nc.sync.dma_start(out=xc[:], in_=tzh.rearrange("z h d -> (z h) d"))
+        nc.scalar.dma_start(out=xb[:], in_=twz.rearrange("w z d -> (w z) d"))
         nc.sync.dma_start(out=byt0[:], in_=bytes_v[:, 0:NB0, :])
         nc.scalar.dma_start(out=sc[:], in_=scale_v)
         nc.sync.dma_start(out=w1raw[:], in_=w1_words[0].rearrange("p n t -> p (n t)").bitcast(I32))
@@ -598,10 +573,10 @@ def tile_tpvformersoftplusoccupancydecoder_d1p_kernel(
         widen_v(0)
         warm_up(1, 3 * P)
         turn_a(0, 1)
-        gc = grp.tile([P, P, 4], BF16, name="gc", align_bytes=64)
+        gc = keep.tile([P, NV, 4], BF16, name="gc", align_bytes=64)
         nc.scalar.copy(
-            out=words_of(gc[:]).rearrange("p (z w u) -> p z w u", z=Z, u=2),
-            in_=c_bank[:, 0:256].rearrange("p (u w z) -> p z w u", u=2, z=Z),
+            out=words_of(gc[:]).rearrange("p (r q u) -> p r q u", q=4, u=2),
+            in_=c_bank[:, 0:256].rearrange("p (u r) -> p r u", u=2).unsqueeze(2).to_broadcast([P, P, 4, 2]),
         )
         release("c")
         widen_v(1)
@@ -610,16 +585,15 @@ def tile_tpvformersoftplusoccupancydecoder_d1p_kernel(
         warm_up(1, 3 * P)
         gb = grp.tile([P, P, 4], BF16, name="gb", align_bytes=64)
         nc.scalar.copy(
-            out=words_of(gb[:]).rearrange("p (j z a u) -> p j z a u", z=Z, a=4, u=2),
-            in_=b_bank[:, 0:256].rearrange("p (u z j a) -> p j z a u", u=2, z=Z, a=4),
+            out=words_of(gb[:]).rearrange("p (j z q u) -> p j z q u", z=Z, q=4, u=2),
+            in_=b_bank[:, 0:256].rearrange("p (u q j z) -> p j z q u", u=2, q=4, z=Z),
         )
         release("b")
         copy_a(0, 1)
         copy_a(1, 1)
-        quant(cq[:], cqs[:], gc[:])
         nc.vector.tensor_copy(out=s1p[:], in_=s1raw[:].rearrange("p (m t) -> p t m", t=4))
+        quant(crc[:], crs[:], gc[:])
         quant(bq[:], bqs[:], gb[:])
-        spread_c()
         quant_a(0, 1)
         bb = take("bb")
         for t in range(4):
@@ -638,7 +612,6 @@ def tile_tpvformersoftplusoccupancydecoder_d1p_kernel(
         turn_a(2, 1)
         project(0, 2, False)
         project(0, 3, False)
-        spread_b_bytes(2, 1)
         spread_b_scales(2, 1)
         spread_b(2, 1)
         scaled(nc.vector, ng[:], gt[:], -1.0)
@@ -669,9 +642,10 @@ def tile_tpvformersoftplusoccupancydecoder_d1p_kernel(
         clip_s(0, nc.vector, HV, NV)
         scaled(nc.vector, gk[:], gt[:], 1.0 / KNEE)
         scaled(nc.vector, ngw[:], gt[:].unsqueeze(2).to_broadcast([P, 4, WI]), -1.0)
-        spread_b_bytes(5, 3)
         spread_b_scales(5, 3)
         spread_b(5, 3)
+        factor(0, 0)
+        factor(0, 1)
         copy_a(3, 2, True)
         copy_a(5, 2, True)
         quant_a(3, 2)
@@ -680,8 +654,8 @@ def tile_tpvformersoftplusoccupancydecoder_d1p_kernel(
         for t in range(4):
             project(3, t, False)
         quant_a(7, 1)
-        for t in range(4):
-            factor(0, t)
+        factor(0, 2)
+        factor(0, 3)
         loga(0, 0, 4, 0, HV)
         loga(2, 0, 2)
         loga(2, 2, 4)

@@ -20,12 +20,16 @@ P = 128
 NU = 8
 NV = 512
 HV = 256
+NQ = W // NU
+NC = Z * NQ
 FLOOR = 2.0 ** -23
 KNEE = 23 * 0.6931471805599453
 EPS = 2.0 ** -60
-WI = 4
-NB0 = 2
-NVW = 4
+RUN = 4
+STORED = (0, 1, 3, 4)
+FIRST = 2
+ON_VECTOR = (0, 1, 2, 3)
+WARM = 256
 
 
 def tile_tpvformersoftplusoccupancydecoder_d1p_kernel(
@@ -42,15 +46,15 @@ def tile_tpvformersoftplusoccupancydecoder_d1p_kernel(
         ctx.enter_context(tc.manual_schedule())
 
         ident = keep.tile([P, P], F32, name="ident")
-        byt0 = keep.tile([P, NB0, D], U8, name="byt0")
-        byt1 = keep.tile([P, NU - NB0, D], U8, name="byt1")
+        bytes_first = keep.tile([P, FIRST, D], U8, name="bytes_first")
+        bytes_rest = keep.tile([P, NU - FIRST, D], U8, name="bytes_rest")
         sc = keep.tile([P, NU, 4], F32, name="sc")
         nsc = keep.tile([P, NU, 4], F32, name="nsc")
         xa = [keep.tile([P, D], BF16, name="xa%d" % j, align_bytes=64) for j in range(NU)]
-        xc = keep.tile([P, D], BF16, name="xc", align_bytes=64)
         xb = keep.tile([P, D], BF16, name="xb", align_bytes=64)
-        nxc = keep.tile([P, D], BF16, name="nxc", align_bytes=64)
+        xc = keep.tile([P, D], BF16, name="xc", align_bytes=64)
         nxb = keep.tile([P, D], BF16, name="nxb", align_bytes=64)
+        nxc = keep.tile([P, D], BF16, name="nxc", align_bytes=64)
         w1raw = keep.tile([P, F], I32, name="w1raw", align_bytes=64)
         s1raw = keep.tile([P, F], U8, name="s1raw", align_bytes=64)
         w1p = keep.tile([P, 4, P], I32, name="w1p", align_bytes=64)
@@ -62,39 +66,30 @@ def tile_tpvformersoftplusoccupancydecoder_d1p_kernel(
         nb1 = keep.tile([P, 4], F32, name="nb1")
         gk = keep.tile([P, 4], F32, name="gk")
         ng = keep.tile([P, 4], F32, name="ng")
-        ngw = keep.tile([P, 4, WI], F32, name="ngw")
+        ng_run = keep.tile([P, 4, RUN], F32, name="ng_run")
         b2t = keep.tile([P, E], BF16, name="b2t")
-        b2c = [keep.tile([P, 1], BF16, name="b2c%d" % c) for c in range(2)]
-        bq = keep.tile([P, P], I32, name="bq", align_bytes=64)
-        bqs = keep.tile([P, P], U8, name="bqs", align_bytes=64)
-        crc = keep.tile([P, NV], I32, name="crc", align_bytes=64)
-        crs = keep.tile([P, NV], U8, name="crs", align_bytes=64)
-        brc = keep.tile([P, NU * NV], I32, name="brc", align_bytes=64)
-        brs = keep.tile([P, NU * NV], U8, name="brs", align_bytes=64)
-        ac = keep.tile([P, NU * P], U32, name="ac", align_bytes=64)
-        as_ = keep.tile([P, NU * P], U8, name="as_", align_bytes=64)
-        bp = keep.tile([P, 4, NU, 16], F32, name="bp")
-        dg = keep.tile([P, 4, P], F32, name="dg")
-        zero = keep.tile([P, 3 * P], F32, name="zero")
-        flr = keep.tile([P, 1], F32, name="flr")
-        flr2 = keep.tile([P, 1], F32, name="flr2")
-        dum = keep.tile([P, 1], F32, name="dum")
+        b2c = [keep.tile([P, 1], BF16, name="b2c%d" % i) for i in range(2)]
+        c_codes = keep.tile([P, P], I32, name="c_codes", align_bytes=64)
+        c_scales = keep.tile([P, P], U8, name="c_scales", align_bytes=64)
+        b_codes = keep.tile([P, NV], I32, name="b_codes", align_bytes=64)
+        b_scales = keep.tile([P, NV], U8, name="b_scales", align_bytes=64)
+        c_codes_rep = keep.tile([P, NU * NV], I32, name="c_codes_rep", align_bytes=64)
+        c_scales_rep = keep.tile([P, NU * NV], U8, name="c_scales_rep", align_bytes=64)
+        a_codes = keep.tile([P, NU * P], U32, name="a_codes", align_bytes=64)
+        a_scales = keep.tile([P, NU * P], U8, name="a_scales", align_bytes=64)
+        c_bias = keep.tile([P, 4, NU, NC], F32, name="c_bias")
+        diag = keep.tile([P, 4, P], F32, name="diag")
+        zero = keep.tile([P, WARM], F32, name="zero")
+        floor_col = keep.tile([P, 1], F32, name="floor_col")
+        dummy = keep.tile([P, 1], F32, name="dummy")
+        b_grouped = keep.tile([P, NV, 4], BF16, name="b_grouped", align_bytes=64)
         soft = [keep.tile([P, 4, NV], F32, name="soft%d" % j) for j in range(NU)]
-        big, nsum = {}, {}
+        stored = {}
+        grouped, woven, quarters, flats, codes, turned = {}, {}, {}, {}, {}, {}
 
         bytes_v = thw_bytes.rearrange("h (q j) k -> (h q) j k", j=NU)
         scale_v = thw_scale.rearrange("h (q j) s -> (h q) j s", j=NU)
         out_v = out.rearrange("h (q j) z e -> (h q) j z e", j=NU)
-
-
-        def load_rows(tile, scales, q, eng):
-            eng.dma_start(
-                out=tile[32 * q : 32 * q + 4, :].bitcast(I32),
-                in_=scales[0, 4 * q : 4 * q + 4, :].bitcast(I32),
-            )
-
-        def scaled(eng, dst, src, factor):
-            eng.tensor_scalar(out=dst, in0=src, scalar1=factor, scalar2=0.0, op0=ALU.mult, op1=ALU.add)
 
         free = list(range(8))
         held = {}
@@ -107,49 +102,48 @@ def tile_tpvformersoftplusoccupancydecoder_d1p_kernel(
         def release(key):
             free.append(held.pop(key)[1])
 
-        def halves(tile):
+        def load_rows(tile, scales, quad):
+            nc.sync.dma_start(
+                out=tile[32 * quad : 32 * quad + 4, :].bitcast(I32),
+                in_=scales[0, 4 * quad : 4 * quad + 4, :].bitcast(I32),
+            )
+
+        def scaled(dst, src, factor):
+            nc.vector.tensor_scalar(out=dst, in0=src, scalar1=factor, scalar2=0.0, op0=ALU.mult, op1=ALU.add)
+
+        def sorted_words(tile):
             return tile[:].rearrange("p (u m e) -> p m u e", u=2, e=2)
 
-        def widen(j, q, vec):
-            cols = slice(128 * q, 128 * q + 128)
-            src = (byt0[:, j, cols] if j < NB0 else byt1[:, j - NB0, cols]).bitcast(FP8)
-            s = nsc[:, j, q : q + 1]
-            if vec:
-                nc.vector.tensor_scalar(
-                    out=halves(xa[j])[:, 32 * q : 32 * q + 32], in0=src.rearrange("p (m u e) -> p m u e", u=2, e=2),
-                    scalar1=s, scalar2=None, op0=ALU.mult,
-                )
-            else:
-                nc.scalar.activation(out=xa[j][:, cols], in_=src, func=AF.Copy, scale=s)
+        def negate(dst, src):
+            scaled(sorted_words(dst), src[:].rearrange("p (m u e) -> p m u e", u=2, e=2), -1.0)
 
-        def widen_v(j):
-            for q in range(4):
-                widen(j, q, True)
-
-        def widen_s(j):
-            for q in range(4):
-                widen(j, q, False)
+        def widen(j):
+            for s in range(4):
+                cols = slice(P * s, P * (s + 1))
+                src = (bytes_first[:, j, cols] if j < FIRST else bytes_rest[:, j - FIRST, cols]).bitcast(FP8)
+                if j in ON_VECTOR:
+                    nc.vector.tensor_scalar(
+                        out=sorted_words(xa[j])[:, 32 * s : 32 * (s + 1)],
+                        in0=src.rearrange("p (m u e) -> p m u e", u=2, e=2),
+                        scalar1=nsc[:, j, s : s + 1], scalar2=None, op0=ALU.mult,
+                    )
+                else:
+                    nc.scalar.activation(out=xa[j][:, cols], in_=src, func=AF.Copy, scale=nsc[:, j, s : s + 1])
 
         def turn(key, srcs, ordered):
             bank = take(key)
-            for s, (src, sorted_words) in enumerate(zip(srcs, ordered)):
+            for s, (src, is_sorted) in enumerate(zip(srcs, ordered)):
                 words = src[:].bitcast(F32)
                 for u in range(2):
-                    part = words[:, P * u : P * (u + 1)] if sorted_words else words[:, u : 2 * P : 2]
-                    nc.tensor.transpose(bank[:, 256 * s + P * u : 256 * s + P * u + P], part, ident[:])
+                    part = words[:, P * u : P * (u + 1)] if is_sorted else words[:, u : 2 * P : 2]
+                    nc.tensor.transpose(bank[:, HV * s + P * u : HV * s + P * (u + 1)], part, ident[:])
             return bank
 
         def turn_a(first, count):
             tiles = range(first, first + count)
-            turn(("a", first), [xa[j] for j in tiles], [j < NVW for j in tiles])
+            turn(("a", first), [xa[j] for j in tiles], [j in ON_VECTOR for j in tiles])
 
-        def make_diag():
-            nc.gpsimd.tensor_tensor(
-                out=dg[:], in0=ident[:].unsqueeze(1).to_broadcast([P, 4, P]),
-                in1=ng[:].unsqueeze(2).to_broadcast([P, 4, P]), op=ALU.mult,
-            )
-
-        def warm_up(count, width=HV):
+        def warm_up(count, width):
             bank = take("warm")
             for i in range(count):
                 nc.tensor.matmul(
@@ -160,661 +154,550 @@ def tile_tpvformersoftplusoccupancydecoder_d1p_kernel(
         def words_of(tile):
             return tile.rearrange("p r e -> p (r e)").bitcast(F32)
 
-        grouped = {}
-
-        def copy_a(first, count, vec=False):
-            bank = held["a", first][0]
-            ga = grp.tile([P, 2 * P, 4], BF16, name="ga", align_bytes=64)
-            (nc.vector.tensor_copy if vec else nc.scalar.copy)(
-                out=words_of(ga[:, 0 : count * P]).rearrange("p (s r u) -> p s r u", s=count, u=2),
-                in_=bank[:, 0 : count * 256].rearrange("p (s u r) -> p s r u", s=count, u=2),
+        def copy_a(first, count, copy):
+            grouped[first] = grp.tile([P, 2 * P, 4], BF16, name="ga", align_bytes=64)
+            copy(
+                out=words_of(grouped[first][:, 0 : count * P]).rearrange("p (s r u) -> p s r u", s=count, u=2),
+                in_=held["a", first][0][:, 0 : count * HV].rearrange("p (s u r) -> p s r u", s=count, u=2),
             )
             release(("a", first))
-            grouped[first] = ga
 
-        def quant(codes, scales, src):
-            nc.vector.quantize_mx(out=codes.bitcast(FP8X4), scales=scales, in_=src.rearrange("p r e -> p (r e)"))
+        def quant(words, scales, src):
+            nc.vector.quantize_mx(out=words.bitcast(FP8X4), scales=scales, in_=src.rearrange("p r e -> p (r e)"))
 
         def quant_a(first, count):
             cols = slice(first * P, (first + count) * P)
-            quant(ac[:, cols], as_[:, cols], grouped[first][:, 0 : count * P])
+            quant(a_codes[:, cols], a_scales[:, cols], grouped[first][:, 0 : count * P])
 
-        def spread_b_scales(first, count):
-            cols = slice(NV * first, NV * (first + count))
+        def repeat_c_scales(first, count):
             nc.vector.tensor_copy(
-                out=brs[:, cols].bitcast(I32).rearrange("p (r h) -> p r h", h=H),
-                in_=bqs[:].bitcast(I32)[:, Z * first : Z * (first + count)].unsqueeze(2).to_broadcast([P, Z * count, H]),
+                out=c_scales_rep[:, NV * first : NV * (first + count)].bitcast(I32).rearrange("p (r h) -> p r h", h=H),
+                in_=c_scales[:].bitcast(I32)[:, Z * first : Z * (first + count)].unsqueeze(2).to_broadcast([P, Z * count, H]),
             )
 
-        def spread_b(first, count):
-            cols = slice(NV * first, NV * (first + count))
+        def repeat_c_codes(first, count):
             nc.vector.tensor_copy(
-                out=brc[:, cols].rearrange("p (r h q) -> p r h q", h=H, q=4),
-                in_=bq[:, 16 * first : 16 * (first + count)].rearrange("p (r q) -> p r q", q=4).unsqueeze(2).to_broadcast([P, Z * count, H, 4]),
+                out=c_codes_rep[:, NV * first : NV * (first + count)].rearrange("p (r h q) -> p r h q", h=H, q=NQ),
+                in_=c_codes[:, NC * first : NC * (first + count)]
+                .rearrange("p (r q) -> p r q", q=NQ).unsqueeze(2).to_broadcast([P, Z * count, H, NQ]),
             )
 
-        def project(j, t, with_b=True):
+        def project(j, t):
             bank = take((j, t))
             lhs, lhs_s = w1p[:, t, :].bitcast(FP8X4), s1p[:, t, :]
             ucols = slice(NV * j, NV * (j + 1))
             acols = slice(P * j, P * (j + 1))
-            nc.tensor.matmul_mx(out=bank[:], lhsT=lhs, lhsT_scale=lhs_s, rhs=crc[:].bitcast(FP8X4), rhs_scale=crs[:], start=True, stop=False)
+            nc.tensor.matmul_mx(
+                out=bank[:], lhsT=lhs, lhsT_scale=lhs_s, rhs=b_codes[:].bitcast(FP8X4), rhs_scale=b_scales[:],
+                start=True, stop=False,
+            )
             for z in range(Z):
                 nc.tensor.matmul_mx(
                     out=bank[:, P * z : P * (z + 1)], lhsT=lhs, lhsT_scale=lhs_s,
-                    rhs=ac[:, acols].bitcast(FP8X4), rhs_scale=as_[:, acols], start=False, stop=z == Z - 1 and not with_b,
+                    rhs=a_codes[:, acols].bitcast(FP8X4), rhs_scale=a_scales[:, acols],
+                    start=False, stop=z == Z - 1 and j in STORED,
                 )
-            if with_b:
-                nc.tensor.matmul_mx(out=bank[:], lhsT=lhs, lhsT_scale=lhs_s, rhs=brc[:, ucols].bitcast(FP8X4), rhs_scale=brs[:, ucols], start=False, stop=True)
+            if j not in STORED:
+                nc.tensor.matmul_mx(
+                    out=bank[:], lhsT=lhs, lhsT_scale=lhs_s,
+                    rhs=c_codes_rep[:, ucols].bitcast(FP8X4), rhs_scale=c_scales_rep[:, ucols], start=False, stop=True,
+                )
 
-        def bias_b(j0, j1):
+        def bias_c(j0, j1):
             nc.vector.tensor_tensor(
-                out=bp[:, :, j0:j1, :], in0=held["bb"][0][:].rearrange("p (t j r) -> p t j r", t=4, r=16)[:, :, j0:j1, :],
-                in1=nb1[:].unsqueeze(2).unsqueeze(3).to_broadcast([P, 4, j1 - j0, 16]), op=ALU.add,
+                out=c_bias[:, :, j0:j1, :],
+                in0=held["c proj"][0][:].rearrange("p (t j r) -> p t j r", t=4, r=NC)[:, :, j0:j1, :],
+                in1=nb1[:].unsqueeze(2).unsqueeze(3).to_broadcast([P, 4, j1 - j0, NC]), op=ALU.add,
             )
 
-        def project_half(j, hf, tp, with_b):
-            bank = take((j, hf, tp))
-            acols = slice(P * j, P * (j + 1))
-            ccols = slice(HV * hf, HV * (hf + 1))
-            ucols = slice(NV * j + HV * hf, NV * j + HV * (hf + 1))
-            for s in range(2):
-                lhs, lhs_s = w1p[:, 2 * tp + s, :].bitcast(FP8X4), s1p[:, 2 * tp + s, :]
-                dst = bank[:, HV * s : HV * (s + 1)]
-                nc.tensor.matmul_mx(out=dst, lhsT=lhs, lhsT_scale=lhs_s, rhs=crc[:, ccols].bitcast(FP8X4), rhs_scale=crs[:, ccols], start=True, stop=False)
-                for z in range(2):
-                    nc.tensor.matmul_mx(
-                        out=dst[:, P * z : P * (z + 1)], lhsT=lhs, lhsT_scale=lhs_s,
-                        rhs=ac[:, acols].bitcast(FP8X4), rhs_scale=as_[:, acols], start=False, stop=z == 1 and not with_b,
-                    )
-                if with_b:
-                    nc.tensor.matmul_mx(out=dst, lhsT=lhs, lhsT_scale=lhs_s, rhs=brc[:, ucols].bitcast(FP8X4), rhs_scale=brs[:, ucols], start=False, stop=True)
-
-        def add_half(j, hf, tp):
-            bank = held[j, hf, tp][0]
-            if j not in nsum:
-                nsum[j] = keep.tile([P, 4, NV], F32, name="nsum%d" % j)
+        def add_c(j, t):
+            if j not in stored:
+                stored[j] = keep.tile([P, 4, NV], F32, name="stored%d" % j)
             nc.vector.tensor_tensor(
-                out=nsum[j][:, 2 * tp : 2 * tp + 2, HV * hf : HV * (hf + 1)].rearrange("p s (r w) -> p s r w", w=W),
-                in0=bank[:].rearrange("p (s r w) -> p s r w", s=2, w=W),
-                in1=bp[:, 2 * tp : 2 * tp + 2, j, 8 * hf : 8 * hf + 8].unsqueeze(3).to_broadcast([P, 2, 8, W]),
-                op=ALU.add,
-            )
-            release((j, hf, tp))
-
-        def sigm_half(j, hf, t, last=False):
-            bank = held[j, hf, t // 2][0]
-            nc.scalar.activation(
-                out=soft[j][:, t, HV * hf : HV * (hf + 1)], in_=bank[:, HV * (t % 2) : HV * (t % 2 + 1)],
-                func=AF.Sigmoid, bias=nb1[:, t : t + 1],
-            )
-            if last:
-                release((j, hf, t // 2))
-
-        def lower_half(j, hf, t):
-            bank = held[j, hf, t // 2][0]
-            e = soft[j][:, t, HV * hf : HV * (hf + 1)]
-            nc.vector.scalar_tensor_tensor(
-                out=e, in0=bank[:, HV * (t % 2) : HV * (t % 2 + 1)], scalar=nb1[:, t : t + 1], in1=e, op0=ALU.add, op1=ALU.min
-            )
-            if t % 2 == 1:
-                release((j, hf, t // 2))
-
-        def add_b(j, t):
-            bank = held[j, t][0]
-            if j not in nsum:
-                nsum[j] = keep.tile([P, 4, NV], F32, name="nsum%d" % j)
-            nc.vector.tensor_tensor(
-                out=nsum[j][:, t, :].rearrange("p (z h q) -> p z h q", z=Z, q=4),
-                in0=bank[:].rearrange("p (z h q) -> p z h q", z=Z, q=4),
-                in1=bp[:, t, j, :].rearrange("p (z q) -> p z q", q=4).unsqueeze(2).to_broadcast([P, Z, H, 4]),
+                out=stored[j][:, t, :].rearrange("p (z h q) -> p z h q", z=Z, q=NQ),
+                in0=held[j, t][0][:].rearrange("p (z h q) -> p z h q", z=Z, q=NQ),
+                in1=c_bias[:, t, j, :].rearrange("p (z q) -> p z q", q=NQ).unsqueeze(2).to_broadcast([P, Z, H, NQ]),
                 op=ALU.add,
             )
             release((j, t))
 
-        def clip(j, t0, t1, c0=0, c1=NV):
-            nc.vector.tensor_scalar(
-                out=soft[j][:, t0:t1, c0:c1], in0=nsum[j][:, t0:t1, c0:c1], scalar1=-KNEE, scalar2=None, op0=ALU.max
-            )
+        def sigmoid(j, t, give_back=False):
+            if j in STORED:
+                nc.scalar.activation(out=soft[j][:, t, :], in_=stored[j][:, t, :], func=AF.Sigmoid)
+            else:
+                nc.scalar.activation(out=soft[j][:, t, :], in_=held[j, t][0][:], func=AF.Sigmoid, bias=nb1[:, t : t + 1])
+            if give_back:
+                release((j, t))
 
-        def factor(j, t, c0=0, c1=NV):
-            for hf in range(c0 // HV, c1 // HV):
-                big[j, hf] = nsum[j]
-            e = nsum[j][:, t, c0:c1]
-            nc.vector.tensor_scalar(out=e, in0=e, scalar1=-KNEE, scalar2=gk[:, t : t + 1], op0=ALU.min, op1=ALU.mult)
+        def sigmoid_unit(j):
+            nc.scalar.activation(out=soft[j][:], in_=stored[j][:], func=AF.Sigmoid)
 
-        def sigm2(j, t0, t1, c0=0, c1=NV):
-            e = soft[j][:, t0:t1, c0:c1]
-            nc.scalar.activation(out=e, in_=e, func=AF.Sigmoid)
+        def hold_sigmoid(j, eng, c0, c1, low=FLOOR):
+            e = soft[j][:, :, c0:c1]
+            eng.tensor_scalar(out=e, in0=e, scalar1=1.0, scalar2=low, op0=ALU.min, op1=ALU.max)
 
-        def sigm3(j, t):
-            nc.scalar.activation(out=soft[j][:, t, :], in_=nsum[j][:, t, :], func=AF.Sigmoid)
-
-        def floor(j, hf):
+        def hold_log(j, hf):
             e = soft[j][:, :, HV * hf : HV * (hf + 1)]
             nc.vector.tensor_scalar(out=e, in0=e, scalar1=-KNEE, scalar2=None, op0=ALU.max)
 
-        def sigm(j, t, last=False):
-            nc.scalar.activation(out=soft[j][:, t, :], in_=held[j, t][0][:], func=AF.Sigmoid, bias=nb1[:, t : t + 1])
-            if last:
-                release((j, t))
+        def factor(j, t):
+            e = stored[j][:, t, :]
+            nc.vector.tensor_scalar(out=e, in0=e, scalar1=-KNEE, scalar2=gk[:, t : t + 1], op0=ALU.min, op1=ALU.mult)
 
-        def knee(j, t):
-            bank = held[j, t][0]
-            if j not in big:
-                big[j] = keep.tile([P, 4, NV], F32, name="big%d" % j)
-            nc.vector.tensor_scalar(
-                out=big[j][:, t, :], in0=bank[:], scalar1=nb1[:, t : t + 1], scalar2=-KNEE, op0=ALU.add, op1=ALU.min
+        def log_slots(j, t0, t1):
+            e = soft[j][:, t0:t1, :]
+            nc.scalar.activation(out=e, in_=e, func=AF.Ln, bias=EPS)
+
+        def log_half(j, hf):
+            e = soft[j][:, :, HV * hf : HV * (hf + 1)]
+            nc.scalar.activation(out=e, in_=e, func=AF.Ln, bias=EPS)
+
+        def guard(j, t):
+            e = soft[j][:, t, :]
+            nc.vector.scalar_tensor_tensor(
+                out=e, in0=held[j, t][0][:], scalar=nb1[:, t : t + 1], in1=e, op0=ALU.add, op1=ALU.min
             )
             release((j, t))
 
-        def knee2(j):
-            big[j] = keep.tile([P, 4, NV], F32, name="big%d" % j)
-            nc.vector.tensor_scalar(out=big[j][:], in0=nsum[j][:], scalar1=-KNEE, scalar2=None, op0=ALU.min)
-
-        def loga(j, t0=0, t1=4, c0=0, c1=NV):
-            e = soft[j][:, t0:t1, c0:c1]
-            nc.scalar.activation(out=e, in_=e, func=AF.Ln, bias=EPS)
-
-        def gain(j, t, c0=0, c1=NV):
-            e = soft[j][:, t, c0:c1]
-            nc.vector.tensor_scalar(out=e, in0=e, scalar1=-KNEE, scalar2=gk[:, t : t + 1], op0=ALU.max, op1=ALU.mult)
-
-        def lower(j, t, c0=0, c1=NV):
-            bank = held[j, t][0]
-            e = soft[j][:, t, c0:c1]
-            nc.vector.scalar_tensor_tensor(out=e, in0=bank[:, c0:c1], scalar=nb1[:, t : t + 1], in1=e, op0=ALU.add, op1=ALU.min)
-            if c1 == NV:
-                release((j, t))
-
-        def lower2(j, c0=0, c1=NV):
-            e = soft[j][:, :, c0:c1]
-            nc.vector.tensor_tensor(out=e, in0=e, in1=nsum[j][:, :, c0:c1], op=ALU.min)
-
-        vts, vqs = {}, {}
-
         def walk(ap):
-            return ap.rearrange("p t (c i) -> p c t i", i=WI)
+            return ap.rearrange("p t (c i) -> p c t i", i=RUN)
 
-        def product_v(j, hf, c0=0, c1=HV):
-            if (j, hf) not in vts:
-                vts[j, hf] = vpool.tile([P, HV, 4], BF16, name="vv", align_bytes=64)
-            cols = slice(HV * hf + c0, HV * hf + c1)
-            if (j, hf) in big:
-                other = walk(big[j, hf][:, :, cols])
-            else:
-                gsrc = held["g"][0][:, 0 : 4 * WI].rearrange("p (t i) -> p t i", i=WI)
-                other = gsrc.unsqueeze(1).to_broadcast([P, (c1 - c0) // WI, 4, WI])
+        def weave_out(tile, c0, c1):
+            return tile[:, c0:c1].rearrange("p (c i) t -> p c t i", i=RUN)
+
+        def new_half(eng):
+            if eng is nc.gpsimd:
+                return one.tile([P, HV, 4], BF16, name="vg", align_bytes=64)
+            return vpool.tile([P, HV, 4], BF16, name="vv", align_bytes=64)
+
+        def product_kept(j, hf, c0=0, c1=HV):
+            if (j, hf) not in woven:
+                woven[j, hf] = new_half(nc.vector)
+            gain = held["g"][0][:, 0 : 4 * RUN].rearrange("p (t i) -> p t i", i=RUN)
             nc.vector.tensor_tensor(
-                out=vts[j, hf][:, c0:c1].rearrange("p (c i) t -> p c t i", i=WI),
-                in0=walk(soft[j][:, :, cols]), in1=other, op=ALU.mult,
+                out=weave_out(woven[j, hf], c0, c1), in0=walk(soft[j][:, :, HV * hf + c0 : HV * hf + c1]),
+                in1=gain.unsqueeze(1).to_broadcast([P, (c1 - c0) // RUN, 4, RUN]), op=ALU.mult,
             )
 
-        def product_s(j, hf):
-            vts[j, hf] = vpool.tile([P, HV, 4], BF16, name="vv", align_bytes=64)
+        def product_stored(j, hf, eng):
+            woven[j, hf] = new_half(eng)
             cols = slice(HV * hf, HV * (hf + 1))
-            nc.vector.tensor_tensor(
-                out=vts[j, hf][:].rearrange("p (c i) t -> p c t i", i=WI),
-                in0=walk(soft[j][:, :, cols]), in1=walk(big[j, hf][:, :, cols]), op=ALU.mult,
-            )
-
-        parts = {}
-
-        def product_q(j, q, eng):
-            pool, name = (one, "vg") if eng is nc.gpsimd else (vpool, "vv")
-            parts[j, q] = pool.tile([P, HV, 4], BF16, name=name, align_bytes=64)
-            cols = slice(P * q, P * (q + 1))
             eng.tensor_tensor(
-                out=parts[j, q][:, 0:P].rearrange("p (c i) t -> p c t i", i=WI),
-                in0=walk(soft[j][:, :, cols]), in1=walk(big[j, q // 2][:, :, cols]), op=ALU.mult,
+                out=weave_out(woven[j, hf], 0, HV), in0=walk(soft[j][:, :, cols]), in1=walk(stored[j][:, :, cols]), op=ALU.mult
             )
 
-        def quant_q(j, q):
-            if (j, q // 2) not in vqs:
-                vc = vpool.tile([P, HV], U32, name="vc", align_bytes=64)
-                vs = vpool.tile([P, HV], U8, name="vs", align_bytes=64)
-                vqs[j, q // 2] = (vc, vs)
-            vc, vs = vqs[j, q // 2]
-            cols = slice(P * (q % 2), P * (q % 2 + 1))
-            quant(vc[:, cols], vs[:, cols], parts[j, q][:, 0:P])
-
-        whole = {}
-
-        def product_unit(j, c0, c1):
-            if j not in whole:
-                whole[j] = keep.tile([P, NV, 4], BF16, name="whole%d" % j, align_bytes=64)
-            gsrc = held["g"][0][:, 0 : 4 * WI].rearrange("p (t i) -> p t i", i=WI)
-            nc.vector.tensor_tensor(
-                out=whole[j][:, c0:c1].rearrange("p (c i) t -> p c t i", i=WI), in0=walk(soft[j][:, :, c0:c1]),
-                in1=gsrc.unsqueeze(1).to_broadcast([P, (c1 - c0) // WI, 4, WI]), op=ALU.mult,
+        def product_quarter(j, z, eng):
+            quarters[j, z] = new_half(eng)
+            cols = slice(P * z, P * (z + 1))
+            eng.tensor_tensor(
+                out=weave_out(quarters[j, z], 0, P), in0=walk(soft[j][:, :, cols]), in1=walk(stored[j][:, :, cols]), op=ALU.mult
             )
 
-        def quant_unit(j):
-            vc = keep.tile([P, NV], U32, name="vc%d" % j, align_bytes=64)
-            vs = keep.tile([P, NV], U8, name="vs%d" % j, align_bytes=64)
-            quant(vc[:], vs[:], whole[j][:])
-            for hf in range(2):
-                vqs[j, hf] = (vc[:, HV * hf : HV * (hf + 1)], vs[:, HV * hf : HV * (hf + 1)])
-
-        def product_g(j, hf, c0=0, c1=HV):
-            if (j, hf) not in vts:
-                vts[j, hf] = one.tile([P, HV, 4], BF16, name="vg", align_bytes=64)
-            cols = slice(HV * hf + c0, HV * hf + c1)
-            if (j, hf) in big:
-                other = walk(big[j, hf][:, :, cols])
-            else:
-                other = ng[:].unsqueeze(1).unsqueeze(3).to_broadcast([P, (c1 - c0) // WI, 4, WI])
-            nc.gpsimd.tensor_tensor(
-                out=vts[j, hf][:, c0:c1].rearrange("p (c i) t -> p c t i", i=WI),
-                in0=walk(soft[j][:, :, cols]), in1=other, op=ALU.mult,
-            )
-
-        def gain_pe(j, q):
-            bank = take((j, "g", q))
+        def gain_diag(j, z):
+            bank = take((j, "gain", z))
             for t in range(4):
                 nc.tensor.matmul(
-                    out=bank[:, P * t : P * (t + 1)], lhsT=dg[:, t, :], rhs=soft[j][:, t, P * q : P * (q + 1)],
+                    out=bank[:, P * t : P * (t + 1)], lhsT=diag[:, t, :], rhs=soft[j][:, t, P * z : P * (z + 1)],
                     start=True, stop=True,
                 )
 
-        def weave(j, q):
-            bank = held[j, "g", q][0]
-            hf, c0 = q // 2, P * (q % 2)
-            if (j, hf) not in vts:
-                vts[j, hf] = vpool.tile([P, HV, 4], BF16, name="vv", align_bytes=64)
-            nc.scalar.copy(out=vts[j, hf][:, c0 : c0 + P], in_=bank[:].rearrange("p (t n) -> p n t", t=4))
-            release((j, "g", q))
+        def weave_diag(j, z):
+            hf, c0 = z // 2, P * (z % 2)
+            if (j, hf) not in woven:
+                woven[j, hf] = new_half(nc.scalar)
+            nc.scalar.copy(
+                out=woven[j, hf][:, c0 : c0 + P], in_=held[j, "gain", z][0][:].rearrange("p (t n) -> p n t", t=4)
+            )
+            release((j, "gain", z))
 
-        flats = {}
-
-        def gain_s(j, q):
-            hf = q // 2
-            if (j, hf) not in vts:
-                vts[j, hf] = vpool.tile([P, HV, 4], BF16, name="vv", align_bytes=64)
-            flat = grp.tile([P, 4, P], BF16, name="flat")
-            for t in range(4):
-                nc.scalar.activation(
-                    out=flat[:, t, :], in_=soft[j][:, t, P * q : P * (q + 1)], func=AF.Copy, scale=ng[:, t : t + 1]
-                )
-            flats[j, q] = flat
-
-        def gain_h(j, hf):
-            vts[j, hf] = vpool.tile([P, HV, 4], BF16, name="vv", align_bytes=64)
+        def gain_scalar(j, hf):
+            woven[j, hf] = new_half(nc.scalar)
             flats[j, hf] = keep.tile([P, 4, HV], BF16, name="flat%d_%d" % (j, hf))
             for t in range(4):
                 nc.scalar.activation(
                     out=flats[j, hf][:, t, :], in_=soft[j][:, t, HV * hf : HV * (hf + 1)], func=AF.Copy, scale=ng[:, t : t + 1]
                 )
 
-        def weave_h(j, hf):
-            nc.scalar.copy(out=vts[j, hf][:], in_=flats[j, hf][:].rearrange("p t n -> p n t"))
+        def weave_scalar(j, hf):
+            nc.scalar.copy(out=woven[j, hf][:], in_=flats[j, hf][:].rearrange("p t n -> p n t"))
 
-        def weave_s(j, q):
-            hf, c0 = q // 2, P * (q % 2)
-            nc.scalar.copy(out=vts[j, hf][:, c0 : c0 + P], in_=flats[j, q][:].rearrange("p t n -> p n t"))
-
-        def quant_v(j, hf):
+        def new_codes(j, hf):
             vc = vpool.tile([P, HV], U32, name="vc", align_bytes=64)
             vs = vpool.tile([P, HV], U8, name="vs", align_bytes=64)
-            vqs[j, hf] = (vc, vs)
-            quant(vc[:], vs[:], vts[j, hf][:])
+            codes[j, hf] = (vc, vs)
+
+        def quant_v(j, hf):
+            new_codes(j, hf)
+            quant(codes[j, hf][0][:], codes[j, hf][1][:], woven[j, hf][:])
+
+        def quant_quarter(j, z):
+            if (j, z // 2) not in codes:
+                new_codes(j, z // 2)
+            vc, vs = codes[j, z // 2]
+            cols = slice(P * (z % 2), P * (z % 2 + 1))
+            quant(vc[:, cols], vs[:, cols], quarters[j, z][:, 0:P])
 
         def decode(j, hf):
-            vc, vs = vqs[j, hf]
-            ob = take((j, "o", hf))
+            vc, vs = codes[j, hf]
+            bank = take((j, "out", hf))
             for zz in range(2):
                 cols = slice(P * zz, P * (zz + 1))
                 nc.tensor.matmul_mx(
-                    out=ob[:, E * zz : E * (zz + 1)],
-                    lhsT=vc[:, cols].bitcast(FP8X4), lhsT_scale=vs[:, cols],
-                    rhs=w2w[:].bitcast(FP8X4), rhs_scale=s2w[:],
-                    start=True, stop=True,
+                    out=bank[:, E * zz : E * (zz + 1)], lhsT=vc[:, cols].bitcast(FP8X4), lhsT_scale=vs[:, cols],
+                    rhs=w2w[:].bitcast(FP8X4), rhs_scale=s2w[:], start=True, stop=True,
                 )
-
-        def store(j, hf, ot):
-            nc.sync.dma_start(out=out_v[:, j, 2 * hf : 2 * hf + 2], in_=ot[:])
 
         def finish(j, hf):
             ot = opool.tile([P, 2, E], F32, name="ot")
             nc.vector.tensor_tensor(
-                out=ot[:], in0=held[j, "o", hf][0][:].rearrange("p (z e) -> p z e", z=2),
+                out=ot[:], in0=held[j, "out", hf][0][:].rearrange("p (z e) -> p z e", z=2),
                 in1=b2t[:].unsqueeze(1).to_broadcast([P, 2, E]), op=ALU.add,
             )
-            release((j, "o", hf))
-            store(j, hf, ot)
+            release((j, "out", hf))
+            nc.sync.dma_start(out=out_v[:, j, 2 * hf : 2 * hf + 2], in_=ot[:])
 
-        turned = {}
-
-        def decode_t(j, hf):
-            vc, vs = vqs[j, hf]
-            ob = take((j, "t", hf))
-            for c in range(2):
-                cols = slice(P * c, P * (c + 1))
-                nc.tensor.matmul_mx(
-                    out=ob[:, HV * c : HV * (c + 1)],
-                    lhsT=w2w[:, cols].bitcast(FP8X4), lhsT_scale=s2w[:, cols],
-                    rhs=vc[:].bitcast(FP8X4), rhs_scale=vs[:],
-                    start=True, stop=True,
-                )
-
-        def bias_t(j, hf):
-            ob = held[j, "t", hf][0]
-            turned[j, hf] = grp.tile([P, 2, HV], F32, name="turned")
-            for c in range(2):
-                nc.scalar.activation(
-                    out=turned[j, hf][:, c, :], in_=ob[:, HV * c : HV * (c + 1)], func=AF.Identity, bias=b2c[c][:]
-                )
-            release((j, "t", hf))
-
-        def turn_back(j, hf):
-            ob = take((j, "o", hf))
-            for zz in range(2):
-                for c in range(2):
-                    nc.tensor.transpose(
-                        ob[:, E * zz + P * c : E * zz + P * (c + 1)], turned[j, hf][:, c, P * zz : P * (zz + 1)], ident[:]
-                    )
-
-        def finish_s(j, hf):
-            ot = opool.tile([P, 2, E], F32, name="ot")
-            nc.scalar.copy(out=ot[:].rearrange("p z e -> p (z e)"), in_=held[j, "o", hf][0][:])
-            release((j, "o", hf))
-            store(j, hf, ot)
-
-        def finish_z(j, hf):
+        def finish_last(j, hf):
             ot = opool.tile([P, 2, E], F32, name="ot")
             for zz, eng in enumerate((nc.scalar, nc.sync)):
                 nc.vector.tensor_tensor(
-                    out=ot[:, zz, :], in0=held[j, "o", hf][0][:, E * zz : E * (zz + 1)], in1=b2t[:], op=ALU.add
+                    out=ot[:, zz, :], in0=held[j, "out", hf][0][:, E * zz : E * (zz + 1)], in1=b2t[:], op=ALU.add
                 )
                 eng.dma_start(out=out_v[:, j, 2 * hf + zz], in_=ot[:, zz, :])
-            release((j, "o", hf))
+            release((j, "out", hf))
 
-        def clip_s(j, eng, c0=0, c1=NV, low=FLOOR):
-            e = soft[j][:, :, c0:c1]
-            eng.tensor_scalar(out=e, in0=e, scalar1=1.0, scalar2=low, op0=ALU.min, op1=ALU.max)
+        def decode_turned(j, hf):
+            vc, vs = codes[j, hf]
+            bank = take((j, "turned", hf))
+            for i in range(2):
+                cols = slice(P * i, P * (i + 1))
+                nc.tensor.matmul_mx(
+                    out=bank[:, HV * i : HV * (i + 1)], lhsT=w2w[:, cols].bitcast(FP8X4), lhsT_scale=s2w[:, cols],
+                    rhs=vc[:].bitcast(FP8X4), rhs_scale=vs[:], start=True, stop=True,
+                )
 
-        def place_g():
-            bank = take("g")
-            nc.tensor.matmul(
-                out=bank[:, 0 : 4 * WI], lhsT=ident[:], rhs=ngw[:].rearrange("p t i -> p (t i)"), start=True, stop=True
+        def bias_turned(j, hf):
+            bank = held[j, "turned", hf][0]
+            turned[j, hf] = grp.tile([P, 2, HV], F32, name="turned")
+            for i in range(2):
+                nc.scalar.activation(
+                    out=turned[j, hf][:, i, :], in_=bank[:, HV * i : HV * (i + 1)], func=AF.Identity, bias=b2c[i][:]
+                )
+            release((j, "turned", hf))
+
+        def turn_back(j, hf):
+            bank = take((j, "out", hf))
+            for zz in range(2):
+                for i in range(2):
+                    nc.tensor.transpose(
+                        bank[:, E * zz + P * i : E * zz + P * (i + 1)], turned[j, hf][:, i, P * zz : P * (zz + 1)], ident[:]
+                    )
+
+        def finish_scalar(j, hf):
+            ot = opool.tile([P, 2, E], F32, name="ot")
+            nc.scalar.copy(out=ot[:].rearrange("p z e -> p (z e)"), in_=held[j, "out", hf][0][:])
+            release((j, "out", hf))
+            nc.sync.dma_start(out=out_v[:, j, 2 * hf : 2 * hf + 2], in_=ot[:])
+
+        def copy_b(bank, hf):
+            rows = slice(P // 2 * hf, P // 2 * (hf + 1))
+            nc.scalar.copy(
+                out=words_of(b_grouped[:, HV * hf : HV * (hf + 1)]).rearrange("p (r q u) -> p r q u", q=NQ, u=2),
+                in_=bank[:, 0:HV].rearrange("p (u r) -> p r u", u=2)[:, rows].unsqueeze(2).to_broadcast([P, P // 2, NQ, 2]),
             )
 
+        def quant_b(hf):
+            cols = slice(HV * hf, HV * (hf + 1))
+            quant(b_codes[:, cols], b_scales[:, cols], b_grouped[:, cols])
+
+        def copy_c(bank):
+            tile = grp.tile([P, P, 4], BF16, name="gc", align_bytes=64)
+            nc.scalar.copy(
+                out=words_of(tile[:]).rearrange("p (j z q u) -> p j z q u", z=Z, q=NQ, u=2),
+                in_=bank[:, 0:HV].rearrange("p (u q j z) -> p j z q u", u=2, q=NQ, z=Z),
+            )
+            release("c")
+            return tile
+
+        def project_c():
+            bank = take("c proj")
+            for t in range(4):
+                nc.tensor.matmul_mx(
+                    out=bank[:, P * t : P * (t + 1)], lhsT=w1p[:, t, :].bitcast(FP8X4), lhsT_scale=s1p[:, t, :],
+                    rhs=c_codes[:].bitcast(FP8X4), rhs_scale=c_scales[:], start=True, stop=True,
+                )
+
+        def make_diag():
+            nc.gpsimd.tensor_tensor(
+                out=diag[:], in0=ident[:].unsqueeze(1).to_broadcast([P, 4, P]),
+                in1=ng[:].unsqueeze(2).to_broadcast([P, 4, P]), op=ALU.mult,
+            )
+
+        def place_gain():
+            nc.tensor.matmul(
+                out=take("g")[:, 0 : 4 * RUN], lhsT=ident[:], rhs=ng_run[:].rearrange("p t i -> p (t i)"), start=True, stop=True
+            )
 
         nc.vector.memset(s1raw[:].bitcast(I32), 0)
         nc.vector.memset(zero[:], 0.0)
-        nc.vector.memset(dum[:], 0.0)
-        nc.vector.memset(bqs[:].bitcast(I32), 0)
+        nc.vector.memset(dummy[:], 0.0)
+        nc.vector.memset(c_scales[:].bitcast(I32), 0)
         nc.vector.memset(s2w[:].bitcast(I32), 0)
-        nc.sync.dma_start(out=xc[:], in_=tzh.rearrange("z h d -> (z h) d"))
-        nc.scalar.dma_start(out=xb[:], in_=twz.rearrange("w z d -> (w z) d"))
-        nc.sync.dma_start(out=byt0[:], in_=bytes_v[:, 0:NB0, :])
+        nc.sync.dma_start(out=xb[:], in_=tzh.rearrange("z h d -> (z h) d"))
         nc.scalar.dma_start(out=sc[:], in_=scale_v)
+        nc.sync.dma_start(out=bytes_first[:], in_=bytes_v[:, 0:FIRST, :])
+        nc.scalar.dma_start(out=xc[:], in_=twz.rearrange("w z d -> (w z) d"))
         nc.sync.dma_start(out=w1raw[:], in_=w1_words[0].rearrange("p n t -> p (n t)").bitcast(I32))
-        for q in range(4):
-            load_rows(s1raw, w1_scales, q, nc.sync)
-        nc.scalar.activation(out=dum[:], in_=dum[:], func=AF.Sigmoid)
+        for quad in range(4):
+            load_rows(s1raw, w1_scales, quad)
+        nc.scalar.activation(out=dummy[:], in_=dummy[:], func=AF.Sigmoid)
         nc.sync.dma_start(out=b1t[:], in_=b1.rearrange("(p t) -> p t", t=4))
-        nc.sync.dma_start(out=byt1[:], in_=bytes_v[:, NB0:NU, :])
+        nc.sync.dma_start(out=bytes_rest[:], in_=bytes_v[:, FIRST:NU, :])
         nc.sync.dma_start(out=gt[:], in_=g.rearrange("(p t) -> p t", t=4))
         make_identity(nc, ident[:])
         nc.sync.dma_start(out=w2w[:], in_=w2_words[0].rearrange("p n t -> p (n t)").bitcast(I32))
-        for q in range(4):
-            load_rows(s2w, w2_scales, q, nc.sync)
+        for quad in range(4):
+            load_rows(s2w, w2_scales, quad)
         nc.sync.dma_start(out=b2t[:], in_=b2.partition_broadcast(P))
-        for c in range(2):
-            nc.sync.dma_start(out=b2c[c][:], in_=b2[P * c : P * (c + 1)].rearrange("(p o) -> p o", o=1))
+        for i in range(2):
+            nc.sync.dma_start(out=b2c[i][:], in_=b2[P * i : P * (i + 1)].rearrange("(p o) -> p o", o=1))
 
-        warm_up(2)
-        scaled(nc.vector, halves(nxc), xc[:].rearrange("p (m u e) -> p m u e", u=2, e=2), -1.0)
-        scaled(nc.vector, halves(nxb), xb[:].rearrange("p (m u e) -> p m u e", u=2, e=2), -1.0)
-        c_bank = turn("c", [nxc], [True])
+        warm_up(2, WARM)
+        scaled(nsc[:], sc[:], -1.0)
+        negate(nxb, xb)
         b_bank = turn("b", [nxb], [True])
-        scaled(nc.vector, nsc[:], sc[:], -1.0)
-        widen_v(0)
-        warm_up(1, 3 * P)
+        widen(0)
         turn_a(0, 1)
-        gc = keep.tile([P, NV, 4], BF16, name="gc", align_bytes=64)
-        nc.scalar.copy(
-            out=words_of(gc[:]).rearrange("p (r q u) -> p r q u", q=4, u=2),
-            in_=c_bank[:, 0:256].rearrange("p (u r) -> p r u", u=2).unsqueeze(2).to_broadcast([P, P, 4, 2]),
-        )
-        release("c")
-        widen_v(1)
+        negate(nxc, xc)
+        c_bank = turn("c", [nxc], [True])
+        warm_up(1, WARM)
+        copy_b(b_bank, 0)
+        copy_b(b_bank, 1)
+        release("b")
+        widen(1)
         nc.vector.tensor_copy(out=w1p[:], in_=w1raw[:].rearrange("p (m t) -> p t m", t=4))
         turn_a(1, 1)
-        warm_up(1, 3 * P)
-        gb = grp.tile([P, P, 4], BF16, name="gb", align_bytes=64)
-        nc.scalar.copy(
-            out=words_of(gb[:]).rearrange("p (j z q u) -> p j z q u", z=Z, q=4, u=2),
-            in_=b_bank[:, 0:256].rearrange("p (u q j z) -> p j z q u", u=2, q=4, z=Z),
-        )
-        release("b")
-        copy_a(0, 1)
-        copy_a(1, 1)
+        warm_up(1, WARM)
+        copy_a(0, 1, nc.scalar.copy)
+        c_grouped = copy_c(c_bank)
+        copy_a(1, 1, nc.scalar.copy)
+        quant_b(0)
         nc.vector.tensor_copy(out=s1p[:], in_=s1raw[:].rearrange("p (m t) -> p t m", t=4))
-        quant(crc[:], crs[:], gc[:])
-        quant(bq[:], bqs[:], gb[:])
+        quant_b(1)
         quant_a(0, 1)
-        bb = take("bb")
-        for t in range(4):
-            nc.tensor.matmul_mx(
-                out=bb[:, P * t : P * (t + 1)], lhsT=w1p[:, t, :].bitcast(FP8X4), lhsT_scale=s1p[:, t, :],
-                rhs=bq[:].bitcast(FP8X4), rhs_scale=bqs[:], start=True, stop=True,
-            )
-        scaled(nc.vector, nb1[:], b1t[:], -1.0)
-        widen_v(2)
-        bias_b(0, 2)
+        quant(c_codes[:], c_scales[:], c_grouped[:])
+        project(0, 0)
+        project_c()
+        scaled(nb1[:], b1t[:], -1.0)
+        widen(2)
         quant_a(1, 1)
-        for j in range(4, 8):
-            widen_s(j)
-        project(0, 0, False)
-        project(0, 1, False)
-        turn_a(2, 1)
-        project(0, 2, False)
-        project(0, 3, False)
-        spread_b_scales(2, 1)
-        spread_b(2, 1)
-        scaled(nc.vector, ng[:], gt[:], -1.0)
+        repeat_c_scales(2, 1)
+        repeat_c_codes(2, 1)
+        scaled(ng[:], gt[:], -1.0)
         make_diag()
-        add_b(0, 0)
-        add_b(0, 1)
-        copy_a(2, 1, True)
-        add_b(0, 2)
+        bias_c(0, 2)
+        for j in range(4, 8):
+            widen(j)
+        project(0, 1)
+        turn_a(2, 1)
+        project(0, 2)
+        project(0, 3)
+        add_c(0, 0)
+        add_c(0, 1)
+        copy_a(2, 1, nc.vector.tensor_copy)
+        add_c(0, 2)
         for t in range(4):
-            project(1, t, False)
-        add_b(0, 3)
+            project(1, t)
+        add_c(0, 3)
         quant_a(2, 1)
         for t in range(4):
-            sigm3(0, t)
-        clip_s(0, nc.gpsimd, 0, HV)
+            sigmoid(0, t)
+        hold_sigmoid(0, nc.gpsimd, 0, HV)
         for t in range(4):
-            add_b(1, t)
-            sigm3(1, t)
+            add_c(1, t)
+            sigmoid(1, t)
             project(2, t)
-        bias_b(3, 5)
-        release("bb")
+        bias_c(3, 5)
+        release("c proj")
         for t in range(4):
-            sigm(2, t)
-        widen_v(3)
+            sigmoid(2, t)
+        widen(3)
         turn_a(3, 2)
         turn_a(5, 2)
         turn_a(7, 1)
-        clip_s(0, nc.vector, HV, NV)
-        scaled(nc.vector, gk[:], gt[:], 1.0 / KNEE)
-        scaled(nc.vector, ngw[:], gt[:].unsqueeze(2).to_broadcast([P, 4, WI]), -1.0)
-        spread_b_scales(5, 3)
-        spread_b(5, 3)
+        hold_sigmoid(0, nc.vector, HV, NV)
+        scaled(gk[:], gt[:], 1.0 / KNEE)
+        scaled(ng_run[:], gt[:].unsqueeze(2).to_broadcast([P, 4, RUN]), -1.0)
+        repeat_c_scales(5, 3)
+        repeat_c_codes(5, 3)
         factor(0, 0)
         factor(0, 1)
-        copy_a(3, 2, True)
-        copy_a(5, 2, True)
+        copy_a(3, 2, nc.vector.tensor_copy)
+        copy_a(5, 2, nc.vector.tensor_copy)
         quant_a(3, 2)
-        copy_a(7, 1, True)
+        copy_a(7, 1, nc.vector.tensor_copy)
         quant_a(5, 2)
         for t in range(4):
-            project(3, t, False)
+            project(3, t)
         quant_a(7, 1)
         factor(0, 2)
         factor(0, 3)
-        loga(0, 0, 4, 0, HV)
-        loga(2, 0, 2)
-        loga(2, 2, 4)
-        loga(0, 0, 4, HV, NV)
-        loga(1, 0, 4, 0, HV)
-        loga(1, 0, 4, HV, NV)
-        product_g(0, 0)
+        log_half(0, 0)
+        log_slots(2, 0, 2)
+        log_slots(2, 2, 4)
+        log_half(0, 1)
+        log_half(1, 0)
+        log_half(1, 1)
+        product_stored(0, 0, nc.gpsimd)
         for t in range(4):
-            add_b(3, t)
-            project(4, t, False)
-        lower(2, 0)
+            add_c(3, t)
+            project(4, t)
+        guard(2, 0)
         project(5, 0)
-        lower(2, 1)
+        guard(2, 1)
         project(5, 1)
         for t in range(4):
             factor(1, t)
         quant_v(0, 0)
-        product_g(0, 1)
-        lower(2, 2)
+        product_stored(0, 1, nc.gpsimd)
+        guard(2, 2)
         project(5, 2)
-        lower(2, 3)
+        guard(2, 3)
         project(5, 3)
-        add_b(4, 0)
-        place_g()
-        add_b(4, 1)
+        add_c(4, 0)
+        place_gain()
+        add_c(4, 1)
         decode(0, 0)
-        add_b(4, 2)
+        add_c(4, 2)
         project(6, 0)
-        add_b(4, 3)
+        add_c(4, 3)
         project(6, 1)
-        floor(1, 0)
+        hold_log(1, 0)
         quant_v(0, 1)
-        product_g(1, 0)
+        product_stored(1, 0, nc.gpsimd)
+        sigmoid_unit(3)
         for t in range(4):
-            sigm3(3, t)
-        for t in range(4):
-            sigm(5, t, True)
+            sigmoid(5, t, True)
         finish(0, 0)
         decode(0, 1)
         project(6, 2)
         project(6, 3)
         project(7, 0)
         project(7, 1)
-        product_v(2, 0)
+        product_kept(2, 0)
         finish(0, 1)
-        product_v(2, 1)
-        floor(1, 1)
+        product_kept(2, 1)
+        hold_log(1, 1)
         quant_v(2, 0)
         quant_v(2, 1)
         decode(2, 0)
-        product_s(1, 1)
+        product_stored(1, 1, nc.vector)
         quant_v(1, 0)
         quant_v(1, 1)
-        nc.vector.memset(flr[:], FLOOR)
-        clip_s(3, nc.gpsimd, 0, 3 * P, flr[:])
-        sigm(6, 0, True)
-        sigm(6, 1, True)
-        for t in range(4):
-            sigm3(4, t)
+        nc.vector.memset(floor_col[:], FLOOR)
+        hold_sigmoid(3, nc.gpsimd, 0, 3 * P, floor_col[:])
+        sigmoid(6, 0, True)
+        sigmoid(6, 1, True)
+        sigmoid_unit(4)
         project(7, 2)
         decode(2, 1)
-        sigm(6, 2, True)
-        project(7, 3)
+        sigmoid(6, 2, True)
         finish(2, 0)
         decode(1, 0)
+        project(7, 3)
         finish(2, 1)
         decode(1, 1)
         finish(1, 0)
         project(6, 0)
-        sigm(6, 3)
+        sigmoid(6, 3)
         for t in range(4):
-            sigm(7, t)
+            sigmoid(7, t)
         finish(1, 1)
         project(6, 1)
-        clip_s(3, nc.vector, 3 * P, NV)
-        clip_s(4, nc.vector)
+        hold_sigmoid(3, nc.vector, 3 * P, NV)
+        hold_sigmoid(4, nc.vector, 0, NV)
         for t in range(4):
             factor(4, t)
         for t in range(4):
             factor(3, t)
-        loga(3, 0, 4, 0, HV)
-        product_g(3, 0)
+        log_half(3, 0)
+        product_stored(3, 0, nc.gpsimd)
         for t in range(4):
-            loga(7, t, t + 1)
-        loga(6, 3, 4)
-        loga(3, 0, 4, HV, NV)
-        loga(6, 0, 2)
-        loga(6, 2, 3)
-        loga(4, 0, 4, 0, HV)
-        loga(5, 0, 2)
-        loga(5, 2, 4)
-        loga(4, 0, 4, HV, NV)
-        lower(7, 0)
+            log_slots(7, t, t + 1)
+        log_slots(6, 3, 4)
+        log_half(3, 1)
+        log_slots(6, 0, 2)
+        log_slots(6, 2, 3)
+        log_half(4, 0)
+        log_slots(5, 0, 2)
+        log_slots(5, 2, 4)
+        log_half(4, 1)
+        guard(7, 0)
         project(6, 2)
-        lower(7, 1)
+        guard(7, 1)
         project(5, 0)
-        lower(7, 2)
-        project(5, 1)
-        lower(7, 3)
-        lower(6, 3)
-        product_v(7, 0)
+        guard(7, 2)
+        guard(7, 3)
+        guard(6, 3)
+        product_kept(7, 0)
         quant_v(3, 0)
         quant_v(7, 0)
-        product_g(3, 1)
+        product_stored(3, 1, nc.gpsimd)
         decode(3, 0)
         decode(7, 0)
-        lower(6, 0)
+        project(5, 1)
+        guard(6, 0)
         project(5, 2)
         finish(3, 0)
         project(5, 3)
-        lower(6, 1)
-        lower(6, 2)
-        gain_pe(6, 0)
-        gain_pe(6, 1)
+        guard(6, 1)
+        guard(6, 2)
+        gain_diag(6, 0)
+        gain_diag(6, 1)
         finish(7, 0)
-        product_v(7, 1, 0, P)
+        product_kept(7, 1, 0, P)
         quant_v(3, 1)
-        product_g(4, 0)
+        product_stored(4, 0, nc.gpsimd)
         decode(3, 1)
-        product_v(7, 1, P, HV)
+        product_kept(7, 1, P, HV)
         for t in range(4):
-            lower(5, t)
-        weave(6, 0)
-        gain_h(6, 1)
-        weave(6, 1)
-        weave_h(6, 1)
-        gain_pe(5, 0)
-        gain_pe(5, 1)
+            guard(5, t)
+        weave_diag(6, 0)
+        gain_scalar(6, 1)
+        weave_diag(6, 1)
+        weave_scalar(6, 1)
+        gain_diag(5, 0)
+        gain_diag(5, 1)
         finish(3, 1)
         quant_v(7, 1)
-        product_q(4, 2, nc.vector)
+        product_quarter(4, 2, nc.vector)
         quant_v(6, 0)
         quant_v(4, 0)
         quant_v(6, 1)
-        product_q(4, 3, nc.gpsimd)
+        product_quarter(4, 3, nc.gpsimd)
         decode(7, 1)
-        decode_t(6, 0)
+        decode_turned(6, 0)
         decode(4, 0)
-        decode_t(6, 1)
-        gain_pe(5, 2)
-        weave(5, 0)
-        weave(5, 1)
-        bias_t(6, 0)
-        bias_t(6, 1)
+        decode_turned(6, 1)
+        gain_diag(5, 2)
+        weave_diag(5, 0)
+        weave_diag(5, 1)
+        bias_turned(6, 0)
+        bias_turned(6, 1)
         turn_back(6, 0)
-        product_v(5, 1, P, HV)
+        product_kept(5, 1, P, HV)
         finish(7, 1)
         turn_back(6, 1)
         finish(4, 0)
-        weave(5, 2)
-        finish_s(6, 0)
-        finish_s(6, 1)
+        weave_diag(5, 2)
+        finish_scalar(6, 0)
+        finish_scalar(6, 1)
         quant_v(5, 0)
         decode(5, 0)
-        quant_q(4, 2)
-        quant_q(4, 3)
+        quant_quarter(4, 2)
+        quant_quarter(4, 3)
         decode(4, 1)
         quant_v(5, 1)
         decode(5, 1)
         finish(5, 0)
         finish(4, 1)
-        finish_z(5, 1)
+        finish_last(5, 1)

@@ -27,9 +27,10 @@ KNEE = 23 * 0.6931471805599453
 EPS = 2.0 ** -60
 RUN = 4
 STORED = (0, 1, 3, 4)
-FIRST = 2
-ON_VECTOR = (0, 1, 2, 3)
+FIRST = 3
+ON_VECTOR = (0, 1, 2, 3, 4)
 WARM = 256
+G_HOLD = 208
 
 
 def tile_tpvformersoftplusoccupancydecoder_d1p_kernel(
@@ -475,11 +476,12 @@ def tile_tpvformersoftplusoccupancydecoder_d1p_kernel(
         release("b")
         widen(1)
         nc.vector.tensor_copy(out=w1p[:], in_=w1raw[:].rearrange("p (m t) -> p t m", t=4))
-        turn_a(1, 1)
+        widen(2)
+        turn_a(1, 2)
         warm_up(1, WARM)
         copy_a(0, 1, nc.scalar.copy)
         c_grouped = copy_c(c_bank)
-        copy_a(1, 1, nc.scalar.copy)
+        copy_a(1, 2, nc.scalar.copy)
         quant_b(0)
         nc.vector.tensor_copy(out=s1p[:], in_=s1raw[:].rearrange("p (m t) -> p t m", t=4))
         quant_b(1)
@@ -488,30 +490,26 @@ def tile_tpvformersoftplusoccupancydecoder_d1p_kernel(
         project(0, 0)
         project_c()
         scaled(nb1[:], b1t[:], -1.0)
-        widen(2)
-        quant_a(1, 1)
         repeat_c_scales(2, 1)
         repeat_c_codes(2, 1)
+        quant_a(1, 2)
         scaled(ng[:], gt[:], -1.0)
         make_diag()
         bias_c(0, 2)
-        for j in range(4, 8):
+        for j in range(5, NU):
             widen(j)
         project(0, 1)
-        turn_a(2, 1)
         project(0, 2)
         project(0, 3)
         add_c(0, 0)
         add_c(0, 1)
-        copy_a(2, 1, nc.vector.tensor_copy)
         add_c(0, 2)
         for t in range(4):
             project(1, t)
         add_c(0, 3)
-        quant_a(2, 1)
         for t in range(4):
             sigmoid(0, t)
-        hold_sigmoid(0, nc.gpsimd, 0, HV)
+        hold_sigmoid(0, nc.gpsimd, 0, G_HOLD)
         for t in range(4):
             add_c(1, t)
             sigmoid(1, t)
@@ -521,19 +519,20 @@ def tile_tpvformersoftplusoccupancydecoder_d1p_kernel(
         for t in range(4):
             sigmoid(2, t)
         widen(3)
+        widen(4)
         turn_a(3, 2)
         turn_a(5, 2)
         turn_a(7, 1)
-        hold_sigmoid(0, nc.vector, HV, NV)
+        hold_sigmoid(0, nc.vector, G_HOLD, NV)
         scaled(gk[:], gt[:], 1.0 / KNEE)
         scaled(ng_run[:], gt[:].unsqueeze(2).to_broadcast([P, 4, RUN]), -1.0)
         repeat_c_scales(5, 3)
         repeat_c_codes(5, 3)
-        factor(0, 0)
-        factor(0, 1)
         copy_a(3, 2, nc.vector.tensor_copy)
-        copy_a(5, 2, nc.vector.tensor_copy)
+        factor(0, 0)
         quant_a(3, 2)
+        copy_a(5, 2, nc.vector.tensor_copy)
+        factor(0, 1)
         copy_a(7, 1, nc.vector.tensor_copy)
         quant_a(5, 2)
         for t in range(4):

@@ -103,8 +103,8 @@ def tile_tpvformersoftplusoccupancydecoder_d1p_kernel(
         def release(key):
             free.append(held.pop(key)[1])
 
-        def load_rows(tile, scales, quad):
-            nc.sync.dma_start(
+        def load_rows(tile, scales, quad, eng):
+            eng.dma_start(
                 out=tile[32 * quad : 32 * quad + 4, :].bitcast(I32),
                 in_=scales[0, 4 * quad : 4 * quad + 4, :].bitcast(I32),
             )
@@ -449,7 +449,7 @@ def tile_tpvformersoftplusoccupancydecoder_d1p_kernel(
         nc.scalar.dma_start(out=xc[:], in_=twz.rearrange("w z d -> (w z) d"))
         nc.sync.dma_start(out=w1raw[:], in_=w1_words[0].rearrange("p n t -> p (n t)").bitcast(I32))
         for quad in range(4):
-            load_rows(s1raw, w1_scales, quad)
+            load_rows(s1raw, w1_scales, quad, nc.sync)
         nc.scalar.activation(out=dummy[:], in_=dummy[:], func=AF.Sigmoid)
         nc.sync.dma_start(out=b1t[:], in_=b1.rearrange("(p t) -> p t", t=4))
         nc.sync.dma_start(out=bytes_rest[:], in_=bytes_v[:, FIRST:NU, :])
@@ -457,7 +457,7 @@ def tile_tpvformersoftplusoccupancydecoder_d1p_kernel(
         make_identity(nc, ident[:])
         nc.sync.dma_start(out=w2w[:], in_=w2_words[0].rearrange("p n t -> p (n t)").bitcast(I32))
         for quad in range(4):
-            load_rows(s2w, w2_scales, quad)
+            load_rows(s2w, w2_scales, quad, nc.sync)
         nc.sync.dma_start(out=b2t[:], in_=b2.partition_broadcast(P))
         for i in range(2):
             nc.sync.dma_start(out=b2c[i][:], in_=b2[P * i : P * (i + 1)].rearrange("(p o) -> p o", o=1))
@@ -677,19 +677,17 @@ def tile_tpvformersoftplusoccupancydecoder_d1p_kernel(
         decode_turned(6, 0)
         decode(4, 0)
         decode_turned(6, 1)
-        gain_diag(5, 2)
         weave_diag(5, 0)
         weave_diag(5, 1)
         bias_turned(6, 0)
-        bias_turned(6, 1)
         turn_back(6, 0)
-        product_kept(5, 1, P, HV)
-        finish(7, 1)
+        bias_turned(6, 1)
         turn_back(6, 1)
+        finish(7, 1)
         finish(4, 0)
-        weave_diag(5, 2)
         finish_scalar(6, 0)
         finish_scalar(6, 1)
+        product_kept(5, 1)
         quant_v(5, 0)
         decode(5, 0)
         quant_quarter(4, 2)

@@ -30,7 +30,8 @@ STORED = (0, 1, 3, 4)
 FIRST = 3
 ON_VECTOR = (0, 1, 2, 3, 4)
 WARM = 256
-G_HOLD = 208
+G_HOLD_0 = 272
+G_HOLD_4 = 208
 
 
 def tile_tpvformersoftplusoccupancydecoder_d1p_kernel(
@@ -233,8 +234,8 @@ def tile_tpvformersoftplusoccupancydecoder_d1p_kernel(
         def sigmoid_unit(j):
             nc.scalar.activation(out=soft[j][:], in_=stored[j][:], func=AF.Sigmoid)
 
-        def hold_sigmoid(j, eng, c0, c1, low=FLOOR):
-            e = soft[j][:, :, c0:c1]
+        def hold_sigmoid(j, eng, c0, c1, low=FLOOR, t0=0, t1=4):
+            e = soft[j][:, t0:t1, c0:c1]
             eng.tensor_scalar(out=e, in0=e, scalar1=1.0, scalar2=low, op0=ALU.min, op1=ALU.max)
 
         def hold_log(j, hf):
@@ -509,7 +510,8 @@ def tile_tpvformersoftplusoccupancydecoder_d1p_kernel(
         add_c(0, 3)
         for t in range(4):
             sigmoid(0, t)
-        hold_sigmoid(0, nc.gpsimd, 0, G_HOLD)
+        hold_sigmoid(0, nc.gpsimd, 0, NV, t1=1)
+        hold_sigmoid(0, nc.gpsimd, 0, G_HOLD_0, t0=1)
         for t in range(4):
             add_c(1, t)
             sigmoid(1, t)
@@ -523,11 +525,12 @@ def tile_tpvformersoftplusoccupancydecoder_d1p_kernel(
         turn_a(3, 2)
         turn_a(5, 2)
         turn_a(7, 1)
-        hold_sigmoid(0, nc.vector, G_HOLD, NV)
+        hold_sigmoid(0, nc.vector, G_HOLD_0, NV, t0=1)
         scaled(gk[:], gt[:], 1.0 / KNEE)
         scaled(ng_run[:], gt[:].unsqueeze(2).to_broadcast([P, 4, RUN]), -1.0)
         repeat_c_scales(5, 3)
         repeat_c_codes(5, 3)
+        factor(1, 0)
         copy_a(3, 2, nc.vector.tensor_copy)
         factor(0, 0)
         quant_a(3, 2)
@@ -554,7 +557,7 @@ def tile_tpvformersoftplusoccupancydecoder_d1p_kernel(
         project(5, 0)
         guard(2, 1)
         project(5, 1)
-        for t in range(4):
+        for t in range(1, 4):
             factor(1, t)
         quant_v(0, 0)
         product_stored(0, 1, nc.gpsimd)
@@ -585,18 +588,18 @@ def tile_tpvformersoftplusoccupancydecoder_d1p_kernel(
         product_kept(2, 0)
         finish(0, 1)
         product_kept(2, 1)
-        hold_log(1, 1)
+        hold_sigmoid(3, nc.vector, 0, NV)
         quant_v(2, 0)
         quant_v(2, 1)
         decode(2, 0)
-        product_stored(1, 1, nc.vector)
+        for t in range(3):
+            factor(3, t)
         quant_v(1, 0)
-        quant_v(1, 1)
         nc.vector.memset(floor_col[:], FLOOR)
-        hold_sigmoid(3, nc.gpsimd, 0, 3 * P, floor_col[:])
         sigmoid(6, 0, True)
         sigmoid(6, 1, True)
         sigmoid_unit(4)
+        hold_sigmoid(4, nc.gpsimd, 0, G_HOLD_4, floor_col[:])
         project(7, 2)
         decode(2, 1)
         sigmoid(6, 2, True)
@@ -604,20 +607,22 @@ def tile_tpvformersoftplusoccupancydecoder_d1p_kernel(
         decode(1, 0)
         project(7, 3)
         finish(2, 1)
-        decode(1, 1)
         finish(1, 0)
-        project(6, 0)
         sigmoid(6, 3)
         for t in range(4):
             sigmoid(7, t)
+        hold_log(1, 1)
+        hold_sigmoid(4, nc.vector, G_HOLD_4, NV)
+        product_stored(1, 1, nc.vector)
+        factor(4, 0)
+        quant_v(1, 1)
+        decode(1, 1)
+        project(6, 0)
+        for t in range(1, 4):
+            factor(4, t)
+        factor(3, 3)
         finish(1, 1)
         project(6, 1)
-        hold_sigmoid(3, nc.vector, 3 * P, NV)
-        hold_sigmoid(4, nc.vector, 0, NV)
-        for t in range(4):
-            factor(4, t)
-        for t in range(4):
-            factor(3, t)
         log_half(3, 0)
         product_stored(3, 0, nc.gpsimd)
         for t in range(4):
@@ -635,6 +640,7 @@ def tile_tpvformersoftplusoccupancydecoder_d1p_kernel(
         guard(7, 1)
         project(5, 0)
         guard(7, 2)
+        project(5, 1)
         guard(7, 3)
         guard(6, 3)
         product_kept(7, 0)
@@ -643,7 +649,6 @@ def tile_tpvformersoftplusoccupancydecoder_d1p_kernel(
         product_stored(3, 1, nc.gpsimd)
         decode(3, 0)
         decode(7, 0)
-        project(5, 1)
         guard(6, 0)
         project(5, 2)
         finish(3, 0)

from contextlib import ExitStack

import concourse.mybir as mybir
from concourse.masks import make_identity

H, W, Z, D, F, E = 32, 32, 4, 512, 512, 256
FLOPS = 2 * (H * W + Z * H + W * Z) * D * F + 2 * H * W * Z * F * E

F32 = mybir.dt.float32
BF16 = mybir.dt.bfloat16
I32 = mybir.dt.int32
U32 = mybir.dt.uint32
U8 = mybir.dt.uint8
FP8 = mybir.dt.float8_e4m3fn
FP8X4 = mybir.dt.float8_e4m3fn_x4
AF = mybir.ActivationFunctionType
ALU = mybir.AluOpType

P = 128
NU = 8
NV = 512
HV = 256
NQ = W // NU
NC = Z * NQ
FLOOR = 2.0 ** -23
KNEE = 23 * 0.6931471805599453
EPS = 2.0 ** -60
RUN = 4
STORED = (0, 1, 3, 4)
FIRST = 3
ON_VECTOR = (0, 1, 2, 3, 4)
WARM = 256
G_HOLD_0 = 272
G_HOLD_4 = 208


def tile_tpvformersoftplusoccupancydecoder_d1p_kernel(
    tc, thw_bytes, thw_scale, tzh, twz, w1_words, w1_scales, b1, g, w2_words, w2_scales, b2, out
):
    nc = tc.nc
    with ExitStack() as ctx:
        keep = ctx.enter_context(tc.tile_pool(name="keep", bufs=1))
        grp = ctx.enter_context(tc.tile_pool(name="grp", bufs=3))
        vpool = ctx.enter_context(tc.tile_pool(name="vpool", bufs=7))
        one = ctx.enter_context(tc.tile_pool(name="one", bufs=1))
        opool = ctx.enter_context(tc.tile_pool(name="opool", bufs=10))
        psum = ctx.enter_context(tc.psum_pool(name="psum", bufs=1))
        ctx.enter_context(tc.manual_schedule())

        ident = keep.tile([P, P], F32, name="ident")
        bytes_first = keep.tile([P, FIRST, D], U8, name="bytes_first")
        bytes_rest = keep.tile([P, NU - FIRST, D], U8, name="bytes_rest")
        sc = keep.tile([P, NU, 4], F32, name="sc")
        nsc = keep.tile([P, NU, 4], F32, name="nsc")
        xa = [keep.tile([P, D], BF16, name="xa%d" % j, align_bytes=64) for j in range(NU)]
        xb = keep.tile([P, D], BF16, name="xb", align_bytes=64)
        xc = keep.tile([P, D], BF16, name="xc", align_bytes=64)
        nxb = keep.tile([P, D], BF16, name="nxb", align_bytes=64)
        nxc = keep.tile([P, D], BF16, name="nxc", align_bytes=64)
        w1raw = keep.tile([P, F], I32, name="w1raw", align_bytes=64)
        s1raw = keep.tile([P, F], U8, name="s1raw", align_bytes=64)
        w1p = keep.tile([P, 4, P], I32, name="w1p", align_bytes=64)
        s1p = keep.tile([P, 4, P], U8, name="s1p", align_bytes=64)
        w2w = keep.tile([P, E], I32, name="w2w", align_bytes=64)
        s2w = keep.tile([P, E], U8, name="s2w", align_bytes=64)
        b1t = keep.tile([P, 4], BF16, name="b1t")
        gt = keep.tile([P, 4], BF16, name="gt")
        nb1 = keep.tile([P, 4], F32, name="nb1")
        gk = keep.tile([P, 4], F32, name="gk")
        ng = keep.tile([P, 4], F32, name="ng")
        ng_run = keep.tile([P, 4, RUN], F32, name="ng_run")
        b2t = keep.tile([P, E], BF16, name="b2t")
        b2c = [keep.tile([P, 1], BF16, name="b2c%d" % i) for i in range(2)]
        c_codes = keep.tile([P, P], I32, name="c_codes", align_bytes=64)
        c_scales = keep.tile([P, P], U8, name="c_scales", align_bytes=64)
        b_codes = keep.tile([P, NV], I32, name="b_codes", align_bytes=64)
        b_scales = keep.tile([P, NV], U8, name="b_scales", align_bytes=64)
        c_codes_rep = keep.tile([P, NU * NV], I32, name="c_codes_rep", align_bytes=64)
        c_scales_rep = keep.tile([P, NU * NV], U8, name="c_scales_rep", align_bytes=64)
        a_codes = keep.tile([P, NU * P], U32, name="a_codes", align_bytes=64)
        a_scales = keep.tile([P, NU * P], U8, name="a_scales", align_bytes=64)
        c_bias = keep.tile([P, 4, NU, NC], F32, name="c_bias")
        diag = keep.tile([P, 4, P], F32, name="diag")
        zero = keep.tile([P, WARM], F32, name="zero")
        floor_col = keep.tile([P, 1], F32, name="floor_col")
        dummy = keep.tile([P, 1], F32, name="dummy")
        b_grouped = keep.tile([P, NV, 4], BF16, name="b_grouped", align_bytes=64)
        soft = [keep.tile([P, 4, NV], F32, name="soft%d" % j) for j in range(NU)]
        stored = {}
        grouped, woven, quarters, flats, codes, turned = {}, {}, {}, {}, {}, {}

        bytes_v = thw_bytes.rearrange("h (q j) k -> (h q) j k", j=NU)
        scale_v = thw_scale.rearrange("h (q j) s -> (h q) j s", j=NU)
        out_v = out.rearrange("h (q j) z e -> (h q) j z e", j=NU)

        free = list(range(8))
        held = {}

        def take(key):
            k = free.pop(0)
            held[key] = (psum.tile([P, NV], F32, name="bank%d" % k), k)
            return held[key][0]

        def release(key):
            free.append(held.pop(key)[1])

        def load_rows(tile, scales, quad, eng):
            eng.dma_start(
                out=tile[32 * quad : 32 * quad + 4, :].bitcast(I32),
                in_=scales[0, 4 * quad : 4 * quad + 4, :].bitcast(I32),
            )

        def scaled(dst, src, factor):
            nc.vector.tensor_scalar(out=dst, in0=src, scalar1=factor, scalar2=0.0, op0=ALU.mult, op1=ALU.add)

        def sorted_words(tile):
            return tile[:].rearrange("p (u m e) -> p m u e", u=2, e=2)

        def negate(dst, src):
            scaled(sorted_words(dst), src[:].rearrange("p (m u e) -> p m u e", u=2, e=2), -1.0)

        def widen(j):
            for s in range(4):
                cols = slice(P * s, P * (s + 1))
                src = (bytes_first[:, j, cols] if j < FIRST else bytes_rest[:, j - FIRST, cols]).bitcast(FP8)
                if j in ON_VECTOR:
                    nc.vector.tensor_scalar(
                        out=sorted_words(xa[j])[:, 32 * s : 32 * (s + 1)],
                        in0=src.rearrange("p (m u e) -> p m u e", u=2, e=2),
                        scalar1=nsc[:, j, s : s + 1], scalar2=None, op0=ALU.mult,
                    )
                else:
                    nc.scalar.activation(out=xa[j][:, cols], in_=src, func=AF.Copy, scale=nsc[:, j, s : s + 1])

        def turn(key, srcs, ordered):
            bank = take(key)
            for s, (src, is_sorted) in enumerate(zip(srcs, ordered)):
                words = src[:].bitcast(F32)
                for u in range(2):
                    part = words[:, P * u : P * (u + 1)] if is_sorted else words[:, u : 2 * P : 2]
                    nc.tensor.transpose(bank[:, HV * s + P * u : HV * s + P * (u + 1)], part, ident[:])
            return bank

        def turn_a(first, count):
            tiles = range(first, first + count)
            turn(("a", first), [xa[j] for j in tiles], [j in ON_VECTOR for j in tiles])

        def warm_up(count, width):
            bank = take("warm")
            for i in range(count):
                nc.tensor.matmul(
                    out=bank[:, HV * i : HV * i + width], lhsT=zero[:, 0:P], rhs=zero[:, 0:width], start=True, stop=True
                )
            release("warm")

        def words_of(tile):
            return tile.rearrange("p r e -> p (r e)").bitcast(F32)

        def copy_a(first, count, copy):
            grouped[first] = grp.tile([P, 2 * P, 4], BF16, name="ga", align_bytes=64)
            copy(
                out=words_of(grouped[first][:, 0 : count * P]).rearrange("p (s r u) -> p s r u", s=count, u=2),
                in_=held["a", first][0][:, 0 : count * HV].rearrange("p (s u r) -> p s r u", s=count, u=2),
            )
            release(("a", first))

        def quant(words, scales, src):
            nc.vector.quantize_mx(out=words.bitcast(FP8X4), scales=scales, in_=src.rearrange("p r e -> p (r e)"))

        def quant_a(first, count):
            cols = slice(first * P, (first + count) * P)
            quant(a_codes[:, cols], a_scales[:, cols], grouped[first][:, 0 : count * P])

        def repeat_c_scales(first, count):
            nc.vector.tensor_copy(
                out=c_scales_rep[:, NV * first : NV * (first + count)].bitcast(I32).rearrange("p (r h) -> p r h", h=H),
                in_=c_scales[:].bitcast(I32)[:, Z * first : Z * (first + count)].unsqueeze(2).to_broadcast([P, Z * count, H]),
            )

        def repeat_c_codes(first, count):
            nc.vector.tensor_copy(
                out=c_codes_rep[:, NV * first : NV * (first + count)].rearrange("p (r h q) -> p r h q", h=H, q=NQ),
                in_=c_codes[:, NC * first : NC * (first + count)]
                .rearrange("p (r q) -> p r q", q=NQ).unsqueeze(2).to_broadcast([P, Z * count, H, NQ]),
            )

        def project(j, t):
            bank = take((j, t))
            lhs, lhs_s = w1p[:, t, :].bitcast(FP8X4), s1p[:, t, :]
            ucols = slice(NV * j, NV * (j + 1))
            acols = slice(P * j, P * (j + 1))
            nc.tensor.matmul_mx(
                out=bank[:], lhsT=lhs, lhsT_scale=lhs_s, rhs=b_codes[:].bitcast(FP8X4), rhs_scale=b_scales[:],
                start=True, stop=False,
            )
            for z in range(Z):
                nc.tensor.matmul_mx(
                    out=bank[:, P * z : P * (z + 1)], lhsT=lhs, lhsT_scale=lhs_s,
                    rhs=a_codes[:, acols].bitcast(FP8X4), rhs_scale=a_scales[:, acols],
                    start=False, stop=z == Z - 1 and j in STORED,
                )
            if j not in STORED:
                nc.tensor.matmul_mx(
                    out=bank[:], lhsT=lhs, lhsT_scale=lhs_s,
                    rhs=c_codes_rep[:, ucols].bitcast(FP8X4), rhs_scale=c_scales_rep[:, ucols], start=False, stop=True,
                )

        def bias_c(j0, j1):
            nc.vector.tensor_tensor(
                out=c_bias[:, :, j0:j1, :],
                in0=held["c proj"][0][:].rearrange("p (t j r) -> p t j r", t=4, r=NC)[:, :, j0:j1, :],
                in1=nb1[:].unsqueeze(2).unsqueeze(3).to_broadcast([P, 4, j1 - j0, NC]), op=ALU.add,
            )

        def add_c(j, t):
            if j not in stored:
                stored[j] = keep.tile([P, 4, NV], F32, name="stored%d" % j)
            nc.vector.tensor_tensor(
                out=stored[j][:, t, :].rearrange("p (z h q) -> p z h q", z=Z, q=NQ),
                in0=held[j, t][0][:].rearrange("p (z h q) -> p z h q", z=Z, q=NQ),
                in1=c_bias[:, t, j, :].rearrange("p (z q) -> p z q", q=NQ).unsqueeze(2).to_broadcast([P, Z, H, NQ]),
                op=ALU.add,
            )
            release((j, t))

        def sigmoid(j, t, give_back=False):
            if j in STORED:
                nc.scalar.activation(out=soft[j][:, t, :], in_=stored[j][:, t, :], func=AF.Sigmoid)
            else:
                nc.scalar.activation(out=soft[j][:, t, :], in_=held[j, t][0][:], func=AF.Sigmoid, bias=nb1[:, t : t + 1])
            if give_back:
                release((j, t))

        def sigmoid_unit(j):
            nc.scalar.activation(out=soft[j][:], in_=stored[j][:], func=AF.Sigmoid)

        def hold_sigmoid(j, eng, c0, c1, low=FLOOR, t0=0, t1=4):
            e = soft[j][:, t0:t1, c0:c1]
            eng.tensor_scalar(out=e, in0=e, scalar1=1.0, scalar2=low, op0=ALU.min, op1=ALU.max)

        def hold_log(j, hf):
            e = soft[j][:, :, HV * hf : HV * (hf + 1)]
            nc.vector.tensor_scalar(out=e, in0=e, scalar1=-KNEE, scalar2=None, op0=ALU.max)

        def factor(j, t):
            e = stored[j][:, t, :]
            nc.vector.tensor_scalar(out=e, in0=e, scalar1=-KNEE, scalar2=gk[:, t : t + 1], op0=ALU.min, op1=ALU.mult)

        def log_slots(j, t0, t1):
            e = soft[j][:, t0:t1, :]
            nc.scalar.activation(out=e, in_=e, func=AF.Ln, bias=EPS)

        def log_half(j, hf):
            e = soft[j][:, :, HV * hf : HV * (hf + 1)]
            nc.scalar.activation(out=e, in_=e, func=AF.Ln, bias=EPS)

        def guard(j, t):
            e = soft[j][:, t, :]
            nc.vector.scalar_tensor_tensor(
                out=e, in0=held[j, t][0][:], scalar=nb1[:, t : t + 1], in1=e, op0=ALU.add, op1=ALU.min
            )
            release((j, t))

        def walk(ap):
            return ap.rearrange("p t (c i) -> p c t i", i=RUN)

        def weave_out(tile, c0, c1):
            return tile[:, c0:c1].rearrange("p (c i) t -> p c t i", i=RUN)

        def new_half(eng):
            if eng is nc.gpsimd:
                return one.tile([P, HV, 4], BF16, name="vg", align_bytes=64)
            return vpool.tile([P, HV, 4], BF16, name="vv", align_bytes=64)

        def product_kept(j, hf, c0=0, c1=HV):
            if (j, hf) not in woven:
                woven[j, hf] = new_half(nc.vector)
            gain = held["g"][0][:, 0 : 4 * RUN].rearrange("p (t i) -> p t i", i=RUN)
            nc.vector.tensor_tensor(
                out=weave_out(woven[j, hf], c0, c1), in0=walk(soft[j][:, :, HV * hf + c0 : HV * hf + c1]),
                in1=gain.unsqueeze(1).to_broadcast([P, (c1 - c0) // RUN, 4, RUN]), op=ALU.mult,
            )

        def product_stored(j, hf, eng):
            woven[j, hf] = new_half(eng)
            cols = slice(HV * hf, HV * (hf + 1))
            eng.tensor_tensor(
                out=weave_out(woven[j, hf], 0, HV), in0=walk(soft[j][:, :, cols]), in1=walk(stored[j][:, :, cols]), op=ALU.mult
            )

        def product_quarter(j, z, eng):
            quarters[j, z] = new_half(eng)
            cols = slice(P * z, P * (z + 1))
            eng.tensor_tensor(
                out=weave_out(quarters[j, z], 0, P), in0=walk(soft[j][:, :, cols]), in1=walk(stored[j][:, :, cols]), op=ALU.mult
            )

        def gain_diag(j, z):
            bank = take((j, "gain", z))
            for t in range(4):
                nc.tensor.matmul(
                    out=bank[:, P * t : P * (t + 1)], lhsT=diag[:, t, :], rhs=soft[j][:, t, P * z : P * (z + 1)],
                    start=True, stop=True,
                )

        def weave_diag(j, z):
            hf, c0 = z // 2, P * (z % 2)
            if (j, hf) not in woven:
                woven[j, hf] = new_half(nc.scalar)
            nc.scalar.copy(
                out=woven[j, hf][:, c0 : c0 + P], in_=held[j, "gain", z][0][:].rearrange("p (t n) -> p n t", t=4)
            )
            release((j, "gain", z))

        def gain_scalar(j, hf):
            woven[j, hf] = new_half(nc.scalar)
            flats[j, hf] = keep.tile([P, 4, HV], BF16, name="flat%d_%d" % (j, hf))
            for t in range(4):
                nc.scalar.activation(
                    out=flats[j, hf][:, t, :], in_=soft[j][:, t, HV * hf : HV * (hf + 1)], func=AF.Copy, scale=ng[:, t : t + 1]
                )

        def weave_scalar(j, hf):
            nc.scalar.copy(out=woven[j, hf][:], in_=flats[j, hf][:].rearrange("p t n -> p n t"))

        def new_codes(j, hf):
            vc = vpool.tile([P, HV], U32, name="vc", align_bytes=64)
            vs = vpool.tile([P, HV], U8, name="vs", align_bytes=64)
            codes[j, hf] = (vc, vs)

        def quant_v(j, hf):
            new_codes(j, hf)
            quant(codes[j, hf][0][:], codes[j, hf][1][:], woven[j, hf][:])

        def quant_quarter(j, z):
            if (j, z // 2) not in codes:
                new_codes(j, z // 2)
            vc, vs = codes[j, z // 2]
            cols = slice(P * (z % 2), P * (z % 2 + 1))
            quant(vc[:, cols], vs[:, cols], quarters[j, z][:, 0:P])

        def decode(j, hf):
            vc, vs = codes[j, hf]
            bank = take((j, "out", hf))
            for zz in range(2):
                cols = slice(P * zz, P * (zz + 1))
                nc.tensor.matmul_mx(
                    out=bank[:, E * zz : E * (zz + 1)], lhsT=vc[:, cols].bitcast(FP8X4), lhsT_scale=vs[:, cols],
                    rhs=w2w[:].bitcast(FP8X4), rhs_scale=s2w[:], start=True, stop=True,
                )

        def finish(j, hf):
            ot = opool.tile([P, 2, E], F32, name="ot")
            nc.vector.tensor_tensor(
                out=ot[:], in0=held[j, "out", hf][0][:].rearrange("p (z e) -> p z e", z=2),
                in1=b2t[:].unsqueeze(1).to_broadcast([P, 2, E]), op=ALU.add,
            )
            release((j, "out", hf))
            nc.sync.dma_start(out=out_v[:, j, 2 * hf : 2 * hf + 2], in_=ot[:])

        def finish_last(j, hf):
            ot = opool.tile([P, 2, E], F32, name="ot")
            for zz, eng in enumerate((nc.scalar, nc.sync)):
                nc.vector.tensor_tensor(
                    out=ot[:, zz, :], in0=held[j, "out", hf][0][:, E * zz : E * (zz + 1)], in1=b2t[:], op=ALU.add
                )
                eng.dma_start(out=out_v[:, j, 2 * hf + zz], in_=ot[:, zz, :])
            release((j, "out", hf))

        def decode_turned(j, hf):
            vc, vs = codes[j, hf]
            bank = take((j, "turned", hf))
            for i in range(2):
                cols = slice(P * i, P * (i + 1))
                nc.tensor.matmul_mx(
                    out=bank[:, HV * i : HV * (i + 1)], lhsT=w2w[:, cols].bitcast(FP8X4), lhsT_scale=s2w[:, cols],
                    rhs=vc[:].bitcast(FP8X4), rhs_scale=vs[:], start=True, stop=True,
                )

        def bias_turned(j, hf):
            bank = held[j, "turned", hf][0]
            turned[j, hf] = grp.tile([P, 2, HV], F32, name="turned")
            for i in range(2):
                nc.scalar.activation(
                    out=turned[j, hf][:, i, :], in_=bank[:, HV * i : HV * (i + 1)], func=AF.Identity, bias=b2c[i][:]
                )
            release((j, "turned", hf))

        def turn_back(j, hf):
            bank = take((j, "out", hf))
            for zz in range(2):
                for i in range(2):
                    nc.tensor.transpose(
                        bank[:, E * zz + P * i : E * zz + P * (i + 1)], turned[j, hf][:, i, P * zz : P * (zz + 1)], ident[:]
                    )

        def finish_scalar(j, hf):
            ot = opool.tile([P, 2, E], F32, name="ot")
            nc.scalar.copy(out=ot[:].rearrange("p z e -> p (z e)"), in_=held[j, "out", hf][0][:])
            release((j, "out", hf))
            nc.sync.dma_start(out=out_v[:, j, 2 * hf : 2 * hf + 2], in_=ot[:])

        def copy_b(bank, hf):
            rows = slice(P // 2 * hf, P // 2 * (hf + 1))
            nc.scalar.copy(
                out=words_of(b_grouped[:, HV * hf : HV * (hf + 1)]).rearrange("p (r q u) -> p r q u", q=NQ, u=2),
                in_=bank[:, 0:HV].rearrange("p (u r) -> p r u", u=2)[:, rows].unsqueeze(2).to_broadcast([P, P // 2, NQ, 2]),
            )

        def quant_b(hf):
            cols = slice(HV * hf, HV * (hf + 1))
            quant(b_codes[:, cols], b_scales[:, cols], b_grouped[:, cols])

        def copy_c(bank):
            tile = grp.tile([P, P, 4], BF16, name="gc", align_bytes=64)
            nc.scalar.copy(
                out=words_of(tile[:]).rearrange("p (j z q u) -> p j z q u", z=Z, q=NQ, u=2),
                in_=bank[:, 0:HV].rearrange("p (u q j z) -> p j z q u", u=2, q=NQ, z=Z),
            )
            release("c")
            return tile

        def project_c():
            bank = take("c proj")
            for t in range(4):
                nc.tensor.matmul_mx(
                    out=bank[:, P * t : P * (t + 1)], lhsT=w1p[:, t, :].bitcast(FP8X4), lhsT_scale=s1p[:, t, :],
                    rhs=c_codes[:].bitcast(FP8X4), rhs_scale=c_scales[:], start=True, stop=True,
                )

        def make_diag():
            nc.gpsimd.tensor_tensor(
                out=diag[:], in0=ident[:].unsqueeze(1).to_broadcast([P, 4, P]),
                in1=ng[:].unsqueeze(2).to_broadcast([P, 4, P]), op=ALU.mult,
            )

        def place_gain():
            nc.tensor.matmul(
                out=take("g")[:, 0 : 4 * RUN], lhsT=ident[:], rhs=ng_run[:].rearrange("p t i -> p (t i)"), start=True, stop=True
            )

        nc.vector.memset(s1raw[:].bitcast(I32), 0)
        nc.vector.memset(zero[:], 0.0)
        nc.vector.memset(dummy[:], 0.0)
        nc.vector.memset(c_scales[:].bitcast(I32), 0)
        nc.vector.memset(s2w[:].bitcast(I32), 0)
        nc.sync.dma_start(out=xb[:], in_=tzh.rearrange("z h d -> (z h) d"))
        nc.scalar.dma_start(out=sc[:], in_=scale_v)
        nc.sync.dma_start(out=bytes_first[:], in_=bytes_v[:, 0:FIRST, :])
        nc.scalar.dma_start(out=xc[:], in_=twz.rearrange("w z d -> (w z) d"))
        nc.sync.dma_start(out=w1raw[:], in_=w1_words[0].rearrange("p n t -> p (n t)").bitcast(I32))
        for quad in range(4):
            load_rows(s1raw, w1_scales, quad, nc.sync)
        nc.scalar.activation(out=dummy[:], in_=dummy[:], func=AF.Sigmoid)
        nc.sync.dma_start(out=b1t[:], in_=b1.rearrange("(p t) -> p t", t=4))
        nc.sync.dma_start(out=bytes_rest[:], in_=bytes_v[:, FIRST:NU, :])
        nc.sync.dma_start(out=gt[:], in_=g.rearrange("(p t) -> p t", t=4))
        make_identity(nc, ident[:])
        nc.sync.dma_start(out=w2w[:], in_=w2_words[0].rearrange("p n t -> p (n t)").bitcast(I32))
        for quad in range(4):
            load_rows(s2w, w2_scales, quad, nc.sync)
        nc.sync.dma_start(out=b2t[:], in_=b2.partition_broadcast(P))
        for i in range(2):
            nc.sync.dma_start(out=b2c[i][:], in_=b2[P * i : P * (i + 1)].rearrange("(p o) -> p o", o=1))

        warm_up(2, WARM)
        scaled(nsc[:], sc[:], -1.0)
        negate(nxb, xb)
        b_bank = turn("b", [nxb], [True])
        widen(0)
        turn_a(0, 1)
        negate(nxc, xc)
        c_bank = turn("c", [nxc], [True])
        warm_up(1, WARM)
        copy_b(b_bank, 0)
        copy_b(b_bank, 1)
        release("b")
        widen(1)
        nc.vector.tensor_copy(out=w1p[:], in_=w1raw[:].rearrange("p (m t) -> p t m", t=4))
        widen(2)
        turn_a(1, 2)
        warm_up(1, WARM)
        copy_a(0, 1, nc.scalar.copy)
        c_grouped = copy_c(c_bank)
        copy_a(1, 2, nc.scalar.copy)
        quant_b(0)
        nc.vector.tensor_copy(out=s1p[:], in_=s1raw[:].rearrange("p (m t) -> p t m", t=4))
        quant_b(1)
        quant_a(0, 1)
        quant(c_codes[:], c_scales[:], c_grouped[:])
        project(0, 0)
        project_c()
        scaled(nb1[:], b1t[:], -1.0)
        repeat_c_scales(2, 1)
        repeat_c_codes(2, 1)
        quant_a(1, 2)
        scaled(ng[:], gt[:], -1.0)
        make_diag()
        bias_c(0, 2)
        for j in range(5, NU):
            widen(j)
        project(0, 1)
        project(0, 2)
        project(0, 3)
        add_c(0, 0)
        add_c(0, 1)
        add_c(0, 2)
        for t in range(4):
            project(1, t)
        add_c(0, 3)
        for t in range(4):
            sigmoid(0, t)
        hold_sigmoid(0, nc.gpsimd, 0, NV, t1=1)
        hold_sigmoid(0, nc.gpsimd, 0, G_HOLD_0, t0=1)
        for t in range(4):
            add_c(1, t)
            sigmoid(1, t)
            project(2, t)
        bias_c(3, 5)
        release("c proj")
        for t in range(4):
            sigmoid(2, t)
        widen(3)
        widen(4)
        turn_a(3, 2)
        turn_a(5, 2)
        turn_a(7, 1)
        hold_sigmoid(0, nc.vector, G_HOLD_0, NV, t0=1)
        scaled(gk[:], gt[:], 1.0 / KNEE)
        scaled(ng_run[:], gt[:].unsqueeze(2).to_broadcast([P, 4, RUN]), -1.0)
        repeat_c_scales(5, 3)
        repeat_c_codes(5, 3)
        factor(1, 0)
        copy_a(3, 2, nc.vector.tensor_copy)
        factor(0, 0)
        quant_a(3, 2)
        copy_a(5, 2, nc.vector.tensor_copy)
        factor(0, 1)
        copy_a(7, 1, nc.vector.tensor_copy)
        quant_a(5, 2)
        for t in range(4):
            project(3, t)
        quant_a(7, 1)
        factor(0, 2)
        factor(0, 3)
        log_half(0, 0)
        log_slots(2, 0, 2)
        log_slots(2, 2, 4)
        log_half(0, 1)
        log_half(1, 0)
        log_half(1, 1)
        product_stored(0, 0, nc.gpsimd)
        for t in range(4):
            add_c(3, t)
            project(4, t)
        guard(2, 0)
        project(5, 0)
        guard(2, 1)
        project(5, 1)
        for t in range(1, 4):
            factor(1, t)
        quant_v(0, 0)
        product_stored(0, 1, nc.gpsimd)
        guard(2, 2)
        project(5, 2)
        guard(2, 3)
        project(5, 3)
        add_c(4, 0)
        place_gain()
        add_c(4, 1)
        decode(0, 0)
        add_c(4, 2)
        project(6, 0)
        add_c(4, 3)
        project(6, 1)
        hold_log(1, 0)
        quant_v(0, 1)
        product_stored(1, 0, nc.gpsimd)
        sigmoid_unit(3)
        for t in range(4):
            sigmoid(5, t, True)
        finish(0, 0)
        decode(0, 1)
        project(6, 2)
        project(6, 3)
        project(7, 0)
        project(7, 1)
        product_kept(2, 0)
        finish(0, 1)
        product_kept(2, 1)
        hold_sigmoid(3, nc.vector, 0, NV)
        quant_v(2, 0)
        quant_v(2, 1)
        decode(2, 0)
        for t in range(3):
            factor(3, t)
        quant_v(1, 0)
        nc.vector.memset(floor_col[:], FLOOR)
        sigmoid(6, 0, True)
        sigmoid(6, 1, True)
        sigmoid_unit(4)
        hold_sigmoid(4, nc.gpsimd, 0, G_HOLD_4, floor_col[:])
        project(7, 2)
        decode(2, 1)
        sigmoid(6, 2, True)
        finish(2, 0)
        decode(1, 0)
        project(7, 3)
        finish(2, 1)
        finish(1, 0)
        sigmoid(6, 3)
        for t in range(4):
            sigmoid(7, t)
        hold_log(1, 1)
        hold_sigmoid(4, nc.vector, G_HOLD_4, NV)
        product_stored(1, 1, nc.vector)
        factor(4, 0)
        quant_v(1, 1)
        decode(1, 1)
        project(6, 0)
        for t in range(1, 4):
            factor(4, t)
        factor(3, 3)
        finish(1, 1)
        project(6, 1)
        log_half(3, 0)
        product_stored(3, 0, nc.gpsimd)
        for t in range(4):
            log_slots(7, t, t + 1)
        log_slots(6, 3, 4)
        log_half(3, 1)
        log_slots(6, 0, 2)
        log_slots(6, 2, 3)
        log_half(4, 0)
        log_slots(5, 0, 2)
        log_slots(5, 2, 4)
        log_half(4, 1)
        guard(7, 0)
        project(6, 2)
        guard(7, 1)
        project(5, 0)
        guard(7, 2)
        project(5, 1)
        guard(7, 3)
        guard(6, 3)
        product_kept(7, 0)
        quant_v(3, 0)
        quant_v(7, 0)
        product_stored(3, 1, nc.gpsimd)
        decode(3, 0)
        decode(7, 0)
        guard(6, 0)
        project(5, 2)
        finish(3, 0)
        project(5, 3)
        guard(6, 1)
        guard(6, 2)
        gain_diag(6, 0)
        gain_diag(6, 1)
        finish(7, 0)
        product_kept(7, 1, 0, P)
        quant_v(3, 1)
        product_stored(4, 0, nc.gpsimd)
        decode(3, 1)
        product_kept(7, 1, P, HV)
        for t in range(4):
            guard(5, t)
        weave_diag(6, 0)
        gain_scalar(6, 1)
        weave_diag(6, 1)
        weave_scalar(6, 1)
        gain_diag(5, 0)
        gain_diag(5, 1)
        finish(3, 1)
        quant_v(7, 1)
        product_quarter(4, 2, nc.vector)
        quant_v(6, 0)
        quant_v(4, 0)
        quant_v(6, 1)
        product_quarter(4, 3, nc.gpsimd)
        decode(7, 1)
        decode_turned(6, 0)
        decode(4, 0)
        decode_turned(6, 1)
        weave_diag(5, 0)
        weave_diag(5, 1)
        bias_turned(6, 0)
        turn_back(6, 0)
        bias_turned(6, 1)
        turn_back(6, 1)
        finish(7, 1)
        finish(4, 0)
        finish_scalar(6, 0)
        finish_scalar(6, 1)
        product_kept(5, 1)
        quant_v(5, 0)
        decode(5, 0)
        quant_quarter(4, 2)
        quant_quarter(4, 3)
        decode(4, 1)
        quant_v(5, 1)
        decode(5, 1)
        finish(5, 0)
        finish(4, 1)
        finish_last(5, 1)
